import numpy as np, ml_dtypes
CORES = [5,29,101,125,133,157,229,253]
N = 8
import mx_ref
BF = ml_dtypes.bfloat16
def entries(a):
    return np.ascontiguousarray(a.T).reshape(-1)
def table(e):
    return np.ascontiguousarray(np.reshape(e, (-1, 16)).T).astype(np.int32)
def cols(t, e):
    v = np.concatenate([t.reshape(128, -1, 4), np.zeros((128, 1, 4), BF)], axis=1)
    return np.ascontiguousarray(v[:, e]).reshape(128, -1)
def cut(t, i, w=512):
    return t[:, w * i:w * i + w]
def pick(q, e):
    c = np.concatenate([q[0].reshape(128, -1, 4), np.zeros((128, 1, 4), np.uint8)], axis=1); s = np.concatenate([q[1], np.ones((16, 1), np.uint8)], axis=1)
    return (np.ascontiguousarray(c[:, e].reshape(128, -1)), np.ascontiguousarray(s[:, e]))
def join(*qs):
    return (np.concatenate([q[0] for q in qs], axis=1), np.concatenate([q[1] for q in qs], axis=1))
def put(q, e, v):
    c, s = q[0].reshape(128, -1, 4).copy(), q[1].copy(); c[:, e] = v[0].reshape(128, -1, 4); s[:, e] = v[1]
    return (c.reshape(128, -1), s)
def pk(c, s):
    return (np.ascontiguousarray(c), mx_ref.live(s))
def emit(q):
    return q[0], q[1]
def decode(q):
    o = []
    for b in range(4):
        e = np.zeros((128, 128, 4), np.float32); e[np.arange(128), np.arange(128), b] = 1
        o.append(mx_ref.matmul(mx_ref.quantize(e.reshape(128, 512).astype(BF)), q))
    return np.stack(o, axis=2).reshape(128, -1)
def f(rng, *shape):
    return mx_ref.flush((rng.standard_normal(shape, dtype=np.float32) * np.exp2(rng.integers(-2, 3, shape[:-1] + (1,)))).astype(BF))
def wide(rng, *shape, cols=0):
    v = rng.standard_normal(shape, dtype=np.float32) * np.exp2(rng.integers(-12, 13, shape)).astype(np.float32)
    if cols: v *= np.repeat(np.exp2(rng.integers(-cols, cols + 1, shape[:-2] + (1, shape[-1] // 4))) * (rng.random(shape[:-2] + (1, shape[-1] // 4)) > 0.0625), 4, axis=-1).astype(np.float32)
    return mx_ref.flush(v.astype(BF))
P, A, C, E, KP = 128, 16, 16, 8, 4
LC, M = 48, 5
def clean(v):
    v = np.array(v, np.float32)
    v[np.abs(v) < np.float32(2.0 ** -16)] = 0
    return v.astype(BF)
def lists(rng, full=False, own=False):
    out = []
    for r in range(N):
        pool = np.stack([P * q + rng.permutation(P)[:LC] for q in range(N)])
        must = np.zeros(0, int)
        if full: must = rng.permutation(pool[(r + 1 + rng.permutation(N - 1)[:M]) % N].reshape(-1))
        if own: must = P * r + rng.permutation(P)[:A * (C - 4)]
        rows = []
        for i in range(A):
            a = must[i::A]
            b = rng.permutation(np.setdiff1d(pool, a))[:C - a.size]
            rows.append(rng.permutation(np.concatenate([a, b])))
        out.append(table(np.concatenate(rows)))
    return {"cd": np.stack(out)}
def clusters(rng, n, low, high, noise):
    m = f(rng, 128, 4 * n).astype(np.float32).reshape(128, n, 4)
    h = rng.integers(0, n, (N, P))
    tb = np.stack([m[:, h[q]].reshape(128, -1) for q in range(N)]) + noise * f(rng, N, 128, 4 * P).astype(np.float32)
    a = low + (high - low) * rng.random((N, A, n))
    x = np.einsum("png,rin->rpig", m, a).reshape(N, 128, 4 * A) + noise * f(rng, N, 128, 4 * A).astype(np.float32)
    return {"tb": clean(tb), "x": clean(x), "w": f(rng, N, 128, 512)}
def setup_inputs(rng):
    return {**clusters(rng, 8, 0.2, 1.0, 0.5), **lists(rng)}
def setup_inputs_alike(rng):
    return {**clusters(rng, 3, 0.3, 0.7, 0.25), **lists(rng, full=True)}
def setup_inputs_one(rng):
    o, m, n = 0, min(A, LC // KP), P // KP
    kind = rng.permutation(P) % KP
    part = np.arange(128) // (128 // KP)
    tb = f(rng, N, 128, 4 * P).astype(np.float32).reshape(N, 128, P, 4) * np.float32(0.0625)
    tb[o] = (4 + 4 * rng.random((128, P, 4))) * (part[:, None] == kind[None, :])[:, :, None]
    order = np.stack([rng.permutation(np.flatnonzero(kind == k)) for k in range(KP)])
    out = []
    for r in range(N):
        size, at = (A, 0) if r == o else (m, A + m * (r - int(r > o)))
        big = P * o + order[:, (at + np.arange(A) % size) % n]
        pool = rng.permutation(np.concatenate([P * q + rng.permutation(P)[:LC] for q in range(N) if q != o]))
        rest = pool[:A * (C - KP)].reshape(A, C - KP)
        out.append(table(np.concatenate([rng.permutation(v) for v in np.concatenate([big.T, rest], axis=1)])))
    return {"tb": clean(tb.reshape(N, 128, 4 * P)), "x": clean(1 + rng.random((N, 128, 4 * A))), "w": f(rng, N, 128, 512), "cd": np.stack(out)}
def setup_inputs_ties(rng):
    m = clean(f(rng, 128, 12)).astype(np.float32).reshape(128, 3, 4)
    h = rng.integers(0, 3, (N, P))
    i = np.arange(A)
    k = np.where(i // 3 % 2 == 0, 1.0, 2.0)[None, :, None]
    tb = clean(np.stack([m[:, h[q]].reshape(128, -1) for q in range(N)])).reshape(N, 128, P, 4)
    x = clean(np.stack([(m[:, (i + r) % 3] * k).reshape(128, -1) for r in range(N)])).reshape(N, 128, A, 4)
    cd = lists(rng, own=True)["cd"]
    top = np.arange(128) < 64
    x[:, :, A - 2] = np.where(top, 4.0, 1.0).astype(BF)[None, :, None]
    x[:, :, A - 1] = np.where(top, -1.0, -4.0).astype(BF)[None, :, None]
    for r in range(N):
        g = rng.permutation(P)[:C + 1]
        g[:3] = np.sort(g[:3])
        tb[r][:, g[0]] = BF(-0.0)
        tb[r][:, g[1]] = BF(0.0)
        tb[r][:, g[2]] = np.array([1.0, -1.0, 1.0, -1.0]).astype(BF)[None, :]
        tb[r][:, g[3:]] = clean((1 + rng.random((128, C - 2, 4))) * np.where(top, -1.0, 1.0)[:, None, None])
        e = np.array(entries(cd[r])).reshape(A, C)
        e[A - 2] = P * r + rng.permutation(np.delete(g, 1))
        e[A - 1] = P * r + rng.permutation(np.delete(g, 0))
        cd[r] = table(e)
    return {"tb": tb.reshape(N, 128, 4 * P), "x": x.reshape(N, 128, 4 * A), "w": f(rng, N, 128, 512), "cd": cd}
def setup_inputs_shared(rng):
    place = np.stack([rng.permutation(P) for q in range(N)])
    tb = f(rng, N, 128, 4 * P).astype(np.float32).reshape(N, 128, P, 4) * np.float32(0.0625)
    part = np.arange(128) // (128 // KP)
    big = np.zeros((N, KP), int)
    for g in range(N):
        for k in range(KP):
            o = (g + k) % N
            tb[o, :, place[o, k]] = (4 + 4 * rng.random((128, 4))) * (part == k)[:, None]
            big[g, k] = P * o + place[o, k]
    out = []
    for r in range(N):
        pool = np.concatenate([P * q + rng.permutation(place[q, KP:])[:LC - KP] for q in range(N)])
        at = rng.integers(0, r + 1, A)
        at[0], at[A - 1] = 0, r
        out.append(table(np.concatenate([rng.permutation(np.concatenate([big[g], rng.permutation(pool)[:C - KP]])) for g in at])))
    return {"tb": clean(tb.reshape(N, 128, 4 * P)), "x": clean(1 + rng.random((N, 128, 4 * A))), "w": f(rng, N, 128, 512), "cd": np.stack(out)}
def setup_inputs_spread(rng):
    return {"tb": clean(wide(rng, N, 128, 4 * P, cols=6)), "x": clean(wide(rng, N, 128, 4 * A, cols=6)), "w": f(rng, N, 128, 512), **lists(rng)}
def check_inputs(d):
    b = []
    for k, low in (("tb", -16), ("x", -16), ("w", -30)):
        v = np.abs(d[k].astype(np.float32))
        if not (np.isfinite(v).all() and ((v == 0) | (v >= 2.0 ** low) & (v <= 2.0 ** 30)).all()): b.append("a value of " + k)
    for r in range(N):
        e = entries(d["cd"][r])
        if e.min() < 0 or e.max() >= N * P:
            b.append("cd: a number out of range")
            continue
        if any(len(set(v.tolist())) < C for v in e.reshape(A, C)): b.append("cd: a candidate twice at one point")
        n = np.bincount(np.unique(e) // P, minlength=N)
        n[r] = 0
        if n.max() > LC: b.append("cd: too many columns of one other rank")
    return b
def chosen(every, x, cd):
    kept = np.full((N, A, KP), -1)
    for r in range(N):
        e = entries(cd[r])
        t = cols(every, e)
        v = mx_ref.quantize(t)
        points = mx_ref.quantize(cols(x[r], np.concatenate([np.arange(A), np.full(128 - A, -1)])))
        s = mx_ref.matmul(points, v) + np.float32(0)
        g = np.concatenate([mx_ref.matmul(mx_ref.quantize(np.ascontiguousarray(cut(t, j))), v) for j in range(C * A // 128)]) + np.float32(0)
        for i in range(A):
            at = np.arange(C * i, C * i + C)
            best = at[np.lexsort((e[at], -s[i, at]))[:E]]
            mine = []
            for c in best:
                if len(mine) < KP and all(s[i, c] > g[c, k] for k in mine): mine.append(c)
            kept[r, i, :len(mine)] = e[mine]
    return kept
def reference(tb, x, w, cd):
    every = np.concatenate([tb[q] for q in range(N)], axis=1)
    kept = chosen(every, x, cd)
    y = np.zeros((N, 128, KP * A), np.float32)
    oc, osc = np.zeros((N, 128, 4 * P), np.uint8), np.zeros((N, 16, P), np.uint8)
    for r in range(N):
        y[r] = mx_ref.matmul(mx_ref.quantize(w[r]), mx_ref.quantize(cols(every, kept[r].reshape(-1))))
    dx = [decode(mx_ref.quantize(x[r])).reshape(128, A, 4) for r in range(N)]
    half = np.float32(0.5)
    for q in range(N):
        v = mx_ref.quantize(tb[q])
        m = decode(v).reshape(128, P, 4)
        named = np.zeros(P, bool)
        for r in range(N):
            for i in range(A):
                for c in kept[r, i]:
                    j = c - P * q
                    if 0 <= j < P and not named[j]:
                        m[:, j] = m[:, j] * half + dx[r][:, i] * half
                        named[j] = True
        at = np.flatnonzero(named)
        new = mx_ref.quantize(np.ascontiguousarray(m.reshape(128, -1).astype(BF)))
        oc[q], osc[q] = emit(put(v, at, pick(new, at)))
    return {"y": y, "kp": np.ascontiguousarray(kept.transpose(0, 2, 1)).astype(np.float32), "oc": oc, "osc": osc}

@@ -1,0 +1,543 @@
+from concourse.bass import DstId, RemoteDMATransfer
+from concourse.mybir import dt, AluOpType, ActivationFunctionType
+
+N, P, A, LC = 8, 128, 16, 48
+F32, BF, I32, U16, U8, X4 = "float32", "bfloat16", "int32", "uint16", "uint8", "float8_e4m3fn_x4"
+WCOLS = P + 7 * LC
+SCRATCH = {}
+
+
+def _sb(name, n, d):
+    SCRATCH[name] = ("sbuf", [128, n], d)
+
+
+for _n, _w, _d in [
+    ("cdi", 16, I32), ("cpi", 2, I32), ("tbt", 512, BF), ("xt", 512, BF), ("xu", 512, BF), ("wt", 512, BF),
+    ("cdu", 32, U16), ("fla", 1024, BF), ("flb", 1024, BF), ("mrg", 1024, BF), ("nam", 1024, BF), ("one", 128, BF),
+    ("inc", 1024, BF), ("le", 1792, BF), ("cs", 1792, BF), ("rs", 512, BF),
+    ("sgo", 512, BF), ("sga", 16, F32), ("rq", 12, U16), ("rqx", 10, U16), ("rqr", 6, U16), ("rql", 22, U16),
+    ("tbc", 128, X4), ("tbs", 128, U8), ("wc", 480, X4), ("ws", 480, U8), ("fwc", 256, X4), ("fws", 256, U8),
+    ("xc", 128, X4), ("xs", 128, U8), ("wqc", 128, X4), ("wqs", 128, U8), ("pwc", 128, X4), ("pws", 128, U8),
+    ("xrc", 256, X4), ("xrs", 256, U8),
+    ("dcc", 192, X4), ("dcs", 192, U8), ("dsc", 144, X4), ("dss", 144, U8), ("rlc", 96, X4), ("rls", 96, U8),
+    ("rpc", 16, X4), ("rps", 16, U8), ("kc", 288, X4), ("ks", 288, U8), ("ppc", 128, X4), ("pps", 128, U8),
+    ("foc", 128, X4), ("fos", 128, U8), ("ebt", 2048, BF), ("ec", 512, X4), ("es", 512, U8),
+    ("ii", 8, I32), ("fc", 40, F32), ("cj", 96, F32), ("idx", 1040, F32), ("c16", 256, F32), ("wm", 256, F32), ("wmb", 128, BF),
+    ("r16", 256, F32), ("r16b", 128, BF), ("lm", 64, F32), ("r17", 34, F32), ("r8", 32, F32), ("c4", 32, F32),
+    ("zt", 512, F32), ("nrz", 32, F32), ("hid", 128, BF), ("val", 512, BF), ("lgs", 6, U16), ("lrep", 2, U16), ("xl", 16, U16),
+    ("loc", 1040, F32), ("cdk", 16, U16), ("posm", 256, F32), ("posc", 256, F32), ("kpl", 16, U16),
+    ("cpu", 2, U16), ("nr", 32, F32), ("lw", 32, F32),
+    ("pb", 288, F32), ("pbx", 256, F32), ("gs", 32, F32), ("qa", 128, F32), ("rku", 2, U16), ("ge2", 32, F32),
+    ("bsw", 40, F32), ("pk", 34, F32), ("pku", 2, U16), ("own", 32, F32), ("msw", 40, I32), ("ms", 8, I32), ("nsw", 40, F32),
+    ("ui", 56, I32), ("fv", 8, F32), ("pn", 48, F32), ("qb", 96, F32), ("klu", 4, U16),
+    ("kr", 4, F32), ("kru", 4, U16), ("rwm", 64, F32), ("eqd", 256, BF), ("scf", 256, F32),
+    ("lu", 4, U16), ("lr", 4, U16), ("ll", 28, U16), ("kpf", 64, F32), ("locr", 192, F32), ("yl", 8, U16), ("zb", 480, F32), ("yb", 64, F32),
+    ("wns", 1552, BF), ("wnc", 1552, BF), ("wno", 1552, BF), ("wsm", 512, BF), ("wl", 8, F32), ("wu", 8, U16), ("fl", 8, U16), ("nt", 512, BF),
+]:
+    _sb(_n, _w, _d)
+for _n in ("pg0", "pg1", "pz", "pd0", "pd1", "pd2", "pd3"):
+    SCRATCH[_n] = ("psum", [128, 512], F32)
+SEMAPHORES = ["cv", "ca", "ct", "cg", "dcd", "dcp", "dtb", "dx", "dxu", "dw", "dkx", "drep", "dy", "dkp", "doc", "ls",
+              "a_rqc", "a_rqs", "a_dt", "a_pt", "a_klc", "a_kls", "r_pt", "r_rq", "r_dt", "r_kl"]
+PART = ("lerq", "lerqx", "csrq", "csrqx", "lgf", "lrep", "loc", "cdk", "yb", "ebz", "ebt", "rs1", "idxs",
+        "rq", "rqx", "sgarq", "sgarqx")
+
+
+def _bits(es):
+    m = 0
+    for e in es:
+        m |= 1 << e
+    return m
+
+
+def _peers(topo, cores, r):
+    cross = [q for q in range(N) if q != r and not topo.may_write(cores[r], cores[q])]
+    same = [q for q in range(N) if q != r and topo.may_write(cores[r], cores[q])]
+    return cross, same
+
+
+def _relays(topo, cores, r):
+    cross, _ = _peers(topo, cores, r)
+    ok = [c for c in topo.cores_of(cores[r]) if c != cores[r] and topo.may_write(c, cores[cross[0]])]
+    d0 = [c for c in ok if topo.die(c) == topo.die(cores[r])]
+    d1 = [c for c in ok if topo.die(c) != topo.die(cores[r])]
+    return cross, [d0[0], d1[0], d0[1], d1[1]]
+
+
+def _dst(topo, d, s):
+    rid, pid = topo.addr(d, s)
+    return DstId(rid=rid, pnc=pid)
+
+
+def _same_engines(es):
+    return [es[0:4], es[4:6], es[6:8]], [es[0:2], es[2:4], es[4:8]]
+
+
+def _relay_program(g, core, T, topo, cores, r, x):
+    cross, _ = _peers(topo, cores, r)
+    h = x % 2
+    pair = cross[2 * h:2 * h + 2]
+    ids = [_dst(topo, cores[q], core) for q in pair]
+    es = topo.engines(core, cores[pair[0]])
+    half = [es[0:4], es[4:8]]
+    at = [_peers(topo, cores, q)[0].index(r) for q in pair]
+    n = [0]
+
+    def fwd(ts):
+        out = []
+        for src, dsts, to, e, sem in ts:
+            out.append(RemoteDMATransfer(dst_ids=to, dma_engine_mask=_bits(e), remote_sem=T.sem[sem], srcs=[src], dsts=dsts))
+            n[0] += len(e)
+        g.remote_dma_fused(out, local_sem=T.sem.ls)
+
+    non = len(topo.engines(cores[r], core))
+    a = 16 * r
+    w = [P + LC * at[0], P + LC * at[1]]
+    g.wait_ge(T.sem.r_pt, non // 2)
+    if x < 2:
+        fwd([(T.rpc[:].bitcast(dt.uint8), [T.pwc[:, a:a + 16].bitcast(dt.uint8)] * 2, ids, es, "a_pt")])
+        g.wait_ge(T.sem.r_rq, non // 2)
+        fwd([(T.rqr[:, 3 * k:3 * k + 3], [T.rql[:, 3 * at[k]:3 * at[k] + 3]], [ids[k]], half[k], "a_rqc") for k in range(2)])
+        g.wait_ge(T.sem.r_dt, non // 2)
+        fwd([(T.rlc[:, LC * k:LC * k + LC].bitcast(dt.uint8), [T.wc[:, w[k]:w[k] + LC].bitcast(dt.uint8)], [ids[k]], half[k], "a_dt") for k in range(2)])
+        g.wait_ge(T.sem.r_kl, non)
+        fwd([(T.lr[:], [T.ll[:, 4 * at[k]:4 * at[k] + 4]], [ids[k]], half[k], "a_klc") for k in range(2)])
+    else:
+        fwd([(T.rps[:], [T.pws[:, a:a + 16]] * 2, ids, es, "a_pt")])
+        g.wait_ge(T.sem.r_dt, non // 2)
+        fwd([(T.rls[:, LC * k:LC * k + LC], [T.ws[:, w[k]:w[k] + LC]], [ids[k]], half[k], "a_dt") for k in range(2)])
+    g.wait_ge(T.sem.ls, n[0])
+
+
+def rank_program(g, core, T, topo):
+    cores = T.cores
+    r = T.rank_of(core)
+    if r is None:
+        for k in range(N):
+            if cores[k] in topo.cores_of(core):
+                _, rel = _relays(topo, cores, k)
+                if core in rel:
+                    _relay_program(g, core, T, topo, cores, k, rel.index(core))
+        return
+
+    op_ = AluOpType
+    AF = ActivationFunctionType
+    Copy, Sign, Ident, Abs, Relu = AF.Copy, AF.Sign, AF.Identity, AF.Abs, AF.Relu
+    cross, rel = _relays(topo, cores, r)
+    _, same = _peers(topo, cores, r)
+    peers = cross + same
+
+    eng = {"v": g.vector, "a": g.scalar, "t": g.tensor, "g": g, "s": g.sync}
+    csem = {"v": "cv", "a": "ca", "t": "ct", "g": "cg"}
+    tot, seen, wr_, rd_ = {}, {e: {} for e in eng}, {}, {}
+
+    def need(e, toks):
+        want = {}
+        for s, c in toks:
+            c = tot[s] if c is None else c
+            want[s] = max(want.get(s, 0), c)
+        for s in want:
+            if seen[e].get(s, 0) < want[s]:
+                eng[e].wait_ge(T.sem[s], want[s])
+                seen[e][s] = want[s]
+
+    def do(e, fn, rd, wr):
+        mine = csem[e]
+        toks = []
+        for k in rd:
+            toks += wr_.get(k, [])
+        for k in wr:
+            toks += [t for t in wr_.get(k, []) + rd_.get(k, []) if k not in PART or t[0] != mine]
+        need(e, toks)
+        fn(eng[e]).then_inc(T.sem[mine], 1)
+        tot[mine] = tot.get(mine, 0) + 1
+        tok = (mine, tot[mine])
+        for k in wr:
+            wr_[k] = [t for t in wr_.get(k, []) if t[0] != mine] + [tok] if k in PART else [tok]
+            rd_[k] = []
+        for k in rd:
+            rd_[k] = [t for t in rd_.get(k, []) if t[0] != mine] + [tok]
+
+    def V(name, wr, rd, *args):
+        def fn(q):
+            f = {"copy": q.tensor_copy, "tt": q.tensor_tensor, "ts": q.tensor_scalar, "set": q.memset,
+                 "scan": q.tensor_tensor_scan, "qz": q.quantize_mx}[name]
+            return f(*args)
+        do("v", fn, rd.split(), wr.split())
+
+    def S(f, wr, rd, out, in_, **k):
+        do("a", lambda q: q.activation(out, in_, f, **k), rd.split(), wr.split())
+
+    def iota(out, wr, pattern, base=0, cm=0):
+        do("g", lambda q: q.iota(out, pattern, base, cm, allow_small_or_imprecise_dtypes=True), [], [wr])
+
+    def dma(e, sem, out, in_, rd, wr):
+        toks = []
+        for k in rd.split():
+            toks += wr_.get(k, [])
+        for k in wr.split():
+            toks += [t for t in wr_.get(k, []) + rd_.get(k, []) if t[0] != sem]
+        need(e, toks)
+        eng[e].dma_start(out, in_).then_inc(T.sem[sem], 16)
+        tot[sem] = tot.get(sem, 0) + 16
+        for k in wr.split():
+            wr_[k] = [(sem, None)]
+        for k in rd.split():
+            rd_[k] = rd_.get(k, []) + [(sem, None)]
+
+    def mm(out, l, ls, m, ms, start, stop, rd, wr):
+        do("t", lambda q: q.matmul_mx(out, l, ls, m, ms, start, stop), rd.split(), wr.split())
+
+    def u8(v):
+        return v.bitcast(dt.uint8)
+
+    def u32(v):
+        return v.bitcast(dt.uint32)
+
+    def send(transfers, rd):
+        need("g", wr_.get(rd, []))
+        ts = []
+        for src, dsts, ids, es, sem in transfers:
+            ts.append(RemoteDMATransfer(dst_ids=ids, dma_engine_mask=_bits(es), remote_sem=T.sem[sem], srcs=[src], dsts=dsts))
+            tot["ls"] = tot.get("ls", 0) + len(es)
+        g.remote_dma_fused(ts, local_sem=T.sem.ls)
+
+    ids_r = [_dst(topo, c, core) for c in rel]
+    ids_s = [_dst(topo, cores[q], core) for q in same]
+    eon = topo.engines(core, rel[0])
+    eoff = topo.engines(core, cores[same[0]])
+    noff = len(eoff)
+    e_h = [eon[0:len(eon) // 2], eon[len(eon) // 2:]]
+    e_s, e_s2 = _same_engines(eoff)
+    at_s = []
+    from_s = []
+    for q in same:
+        cq, sq = _peers(topo, cores, q)
+        at_s.append(4 + sq.index(r))
+        from_s.append(sq.index(r))
+
+    pin, ti, o7 = [T.ii[:, 2 * k:2 * k + 2] for k in range(3)]
+    tf = T.fc[:, 0:1]
+    sk = [T.fc[:, k:k + 1] for k in range(8)]
+    trs = [T.fc[:, 16 + k:17 + k] for k in range(4)]
+    cpf, half2, pf2, n8, n8b = T.fc[:, 20:22], T.fc[:, 22:23], T.fc[:, 30:31], T.fc[:, 32:33], T.fc[:, 33:34]
+    lo, hi, half1 = T.fc[:, 36:37], T.fc[:, 37:38], T.fc[:, 38:39]
+    c8, c17, xlf = T.cj[:, 0:32], T.cj[:, 32:66], T.cj[:, 72:88]
+    eqt, gt, el = [T.qa[:, 32 * k:32 * k + 32] for k in range(3)]
+    eq, v4, sc8 = [T.qb[:, 32 * k:32 * k + 32] for k in range(3)]
+    psn, nf, kn, ns = [T.pn[:, 8 * k:8 * k + 8] for k in range(4)]
+
+    dma("a", "dx", T.xt[:, 0:64], T.x[:], "", "xt")
+    for k in range(8):
+        dma("s" if k % 2 == 0 else "a", "dcd", T.cdi[16 * k:16 * k + 16, :], T.cd[:], "", "cdi")
+    dma("s", "dtb", T.tbt[:], T.tb[:], "", "tbt")
+    dma("s", "dxu", T.xu[:, 448:512], T.x[:], "", "xu")
+    dma("s", "dw", T.wt[:], T.w[:], "", "wt")
+    for k in range(8):
+        dma("s", "dcp", T.cpi[16 * k:16 * k + 16, :], T.cd[:, 2 * k:2 * k + 2], "", "cpi")
+
+    do("g", lambda q: q.iota(pin, [[0, 2]], 0, 1), [], ["pin"])
+    iota(T.fc[:, 8:16], "k16", [[16, 8]])
+    iota(T.c16[:], "c16", [[0, 16], [1, 16]])
+    iota(T.fc[:, 24:26], "lgf", [[128, 2]], 16, 1)
+    iota(T.fc[:, 28:30], "lgf", [[128, 2]], 0, 1)
+    iota(pf2, "pf2", [[0, 1]], 0, 1)
+
+    V("set", "xtz", "", T.xt[:, 64:512], 0.0)
+    V("set", "one", "", T.one[:], 1.0)
+    V("set", "fla", "", T.fla[:], -200.0)
+
+    for a in range(0, 1024, 448):
+        w = min(448, 1024 - a)
+        S(Copy, "flb%d" % (a // 448), "xtz", T.flb[:, a:a + w], T.xt[:, 64:64 + w])
+    for k in range(4):
+        S(Copy, "rs1", "one", T.rs[:, P * k:P * k + P], T.one[:])
+    S(Copy, "rs", "rs1 xtz", T.rs[:, 0:512:128], T.xt[:, 64:68])
+
+    V("qz", "xc xs", "xt xtz", T.xc[:], T.xs[:], T.xt[:])
+    send([(u8(T.xc[:, 0:16]), [u8(T.rpc[:])] * 2, ids_r[0:2], e_h[0], "r_pt")], "xc")
+    send([(T.xs[:, 0:16], [T.rps[:]] * 2, ids_r[2:4], e_h[1], "r_pt")], "xs")
+    iota(T.idx[:, 0:256], "idx", [[1, 256]])
+    iota(xlf, "xlf", [[1, 2], [2, 8]])
+
+    V("copy", "cdu", "cdi", T.cdu[:, 0:32:2], T.cdi[:])
+    for i in range(A):
+        f = "flb" if i % 2 else "fla"
+        V("copy", f, "cdu one flb0 flb1 flb2" if i % 2 else "cdu one", T[f][:].indirect(T.cdu[:, 2 * i:2 * i + 1]), T.one[:, 0:16])
+        if i == 0:
+            V("ts", "ti", "pin", ti, pin, 15, None, op_.bitwise_and)
+        elif i == 3:
+            V("copy", "tf", "ti", T.fc[:, 34:36], ti)
+        elif i == 6:
+            V("ts", "sk", "k16 tf", T.fc[:, 0:8], T.fc[:, 8:16], T.fc[:, 34:35], None, op_.add)
+    S(Ident, "half2", "sk", half2, sk[2], bias=0.5)
+    S(Ident, "half1", "sk", half1, sk[1], bias=0.5)
+    S(Copy, "n8", "sk", n8, tf, scale=-0.125)
+    S(Copy, "lhc", "sk", T.fc[:, 39:40], tf, scale=-1.0)
+    S(Abs, "wm", "c16 sk", T.wm[:], T.c16[:], bias=tf, scale=-1.0)
+    S(Ident, "n8b", "n8", n8b, n8, bias=273.0)
+    S(Ident, "lo", "lhc", lo, T.fc[:, 39:40], bias=7.5)
+    S(Ident, "lgf", "pf2 n8", T.fc[:, 26:27], pf2, bias=n8, scale=0.125)
+    S(Relu, "wm", "wm", T.wm[:], T.wm[:], bias=1.0, scale=-1.0)
+
+    def lists(qs, base, name, out, more):
+        n = len(qs)
+        h0 = base // P
+        nk = [n, n - more]
+        todo = [(x, half2, h0 + x) for x in range(n)] + [(x, half1, h0 + 4 + x) for x in range(n - more, n)]
+        for q in qs:
+            V("scan", "mrg%d" % q, "fla flb", T.mrg[:, P * q:P * q + P], T.fla[:, P * q:P * q + P], T.flb[:, P * q:P * q + P], 0.0, op_.add, op_.max)
+        for q in qs:
+            V("ts", "nam%d" % q, "mrg%d" % q, T.nam[:, P * q:P * q + P], T.mrg[:, P * q:P * q + P], 0.5, None, op_.is_ge)
+        for q in qs:
+            V("scan", "inc%d" % q, "nam%d one" % q, T.inc[:, P * q:P * q + P], T.one[:], T.nam[:, P * q:P * q + P], 0.0, op_.mult, op_.add)
+        for y, (x, half, col) in enumerate(todo):
+            b = P * (y % 4)
+            S(Sign, "sgo%d sga%s" % (y % 4, name), "inc%d half1 half2" % qs[x], T.sgo[:, b:b + P - 1], T.inc[:, P * qs[x]:P * qs[x] + P - 1],
+              bias=half, scale=-1.0, accum_out=T.sga[:, col:col + 1])
+        for k in range(2):
+            for x in range(nk[k]):
+                a = base + P * (n * k + x)
+                V("ts", "le" + name, "inc%d sk" % qs[x], T.le[:, a:a + P], T.inc[:, P * qs[x]:P * qs[x] + P], sk[k], None, op_.is_le)
+        for k in range(2):
+            a, e = base + P * n * k, base + P * (n * k + nk[k])
+            V("scan", "cs" + name, "rs le" + name, T.cs[:, a:e], T.rs[:, 0:P * nk[k]], T.le[:, a:e], 0.0, op_.mult, op_.add)
+        V("ts", name, "sga" + name, out[:, 2:3 * n:3], T.sga[:, h0:h0 + n], 0.5, 0.5 * (P - 1), op_.mult, op_.add)
+        V("ts", name, "sga" + name, out[:, 3 * (n - more) + 1:3 * n:3], T.sga[:, h0 + 4 + n - more:h0 + 4 + n], 0.5, 0.5 * (P - 1), op_.mult, op_.add)
+        for k in range(2):
+            V("copy", name, "cs" + name, out[:, k:3 * nk[k]:3], T.cs[:, base + P * n * k + P - 2:base + P * (n * k + nk[k]):P])
+
+    lists(cross, 0, "rq", T.rq, 2)
+    send([(T.rq[:, 6 * h:6 * h + 6], [T.rqr[:]], [ids_r[h]], e_h[h], "r_rq") for h in range(2)], "rq")
+    lists(same, 1024, "rqx", T.rqx, 1)
+    send([(T.rqx[:, 3 * y:3 * y + 3], [T.rql[:, 3 * at_s[y]:3 * at_s[y] + 3]], [ids_s[y]], e_s[y], "a_rqs") for y in range(3)], "rqx")
+
+    V("qz", "tbc tbs", "tbt", T.tbc[:], T.tbs[:], T.tbt[:])
+    for x, q in enumerate(peers):
+        S(Ident, "loc", "inc%d" % q, T.loc[:, 1 + P * q:1 + P * q + P], T.inc[:, P * q:P * q + P], bias=float(P + LC * x - 1))
+    S(Ident, "loc", "idx", T.loc[:, 1 + P * r:1 + P * r + P], T.idx[:, 0:P], bias=0.0)
+    S(Sign, "r16", "c16", T.r16[:], T.c16[:])
+    S(Ident, "lgf", "pf2 n8b", T.fc[:, 27:28], pf2, bias=n8b, scale=0.125)
+    V("set", "locz", "", T.loc[:, 0:1], float(WCOLS))
+    V("set", "locy", "", T.loc[:, 1025:1040], float(WCOLS))
+    V("ts", "o7", "pin", o7, pin, 7, None, op_.bitwise_and)
+    V("ts", "cdk", "cdi", T.cdk[:, 0:8], T.cdi[:, 0:16:2], 1.0, None, op_.add)
+    V("ts", "cdk", "cdi", T.cdk[:, 8:16], T.cdi[:, 1:16:2], 1.0, None, op_.add)
+    V("copy", "cpf", "cpi", cpf, T.cpi[:])
+    V("copy", "cpu", "cpi", T.cpu[:], T.cpi[:])
+    V("copy", "xl", "xlf", T.xl[:], xlf)
+    V("ts", "lrep", "o7", T.lrep[:], o7, 0.0, None, op_.add)
+
+    tot["a_rqc"] = 4 * noff // 2
+    tot["a_rqs"] = sum(len(e_s[f]) for f in from_s)
+    wr_["rqlc"] = [("a_rqc", tot["a_rqc"])]
+    wr_["rqls"] = [("a_rqs", tot["a_rqs"])]
+    S(Copy, "dcs", "tbs rqlc", T.dcs[:], T.tbs[:].indirect(T.rql[:, 0:12]))
+    V("copy", "dcc", "tbc rqlc", u32(T.dcc[:]), u32(T.tbc[:]).indirect(T.rql[:, 0:12]))
+    S(Copy, "dss", "tbs rqls", T.dss[:], T.tbs[:].indirect(T.rql[:, 12:21]))
+    V("copy", "dsc", "tbc rqls", u32(T.dsc[:]), u32(T.tbc[:]).indirect(T.rql[:, 12:21]))
+    send([(u8(T.dcc[:, 96 * h:96 * h + 96]), [u8(T.rlc[:])], [ids_r[h]], e_h[h], "r_dt") for h in range(2)], "dcc")
+    send([(T.dcs[:, 96 * h:96 * h + 96], [T.rls[:]], [ids_r[2 + h]], e_h[h], "r_dt") for h in range(2)], "dcs")
+    ws_ = [P + LC * at_s[y] for y in range(3)]
+    send([(u8(T.dsc[:, LC * y:LC * y + LC]), [u8(T.wc[:, ws_[y]:ws_[y] + LC])], [ids_s[y]], e_s[y], "a_dt") for y in range(3)], "dsc")
+    send([(T.dss[:, LC * y:LC * y + LC], [T.ws[:, ws_[y]:ws_[y] + LC]], [ids_s[y]], e_s2[y], "a_dt") for y in range(3)], "dss")
+    iota(c17, "c17", [[0, 2], [1, 17]])
+    iota(c8, "c8", [[0, 4], [1, 8]])
+    iota(T.c4[:], "c4", [[1, 4], [0, 8]], 1)
+    send([(u8(T.xc[:, 0:16]), [u8(T.pwc[:, 16 * r:16 * r + 16])] * 3, ids_s, eoff, "a_pt")], "xc")
+    send([(T.xs[:, 0:16], [T.pws[:, 16 * r:16 * r + 16]] * 3, ids_s, eoff, "a_pt")], "xs")
+    do("g", lambda q: q.affine_select(T.hid[:], T.one[:], [[-1, 128]], op_.is_equal, 0.0, 0, 1), ["one"], ["hid"])
+    iota(T.val[:], "val", [[16, 8], [0, 4], [1, 16]])
+
+    S(Copy, "xuz", "xtz", T.xu[:, 0:448], T.xt[:, 64:512])
+    S(Copy, "xrs", "xs xl", T.xrs[:], T.xs[:].indirect(T.xl[:]))
+    for k in range(1, 4):
+        S(Ident, "idxs", "idx", T.idx[:, 256 * k:256 * k + 256], T.idx[:, 0:256], bias=float(256 * k))
+    S(Ident, "idxs", "idx", T.idx[:, 1024:1040], T.idx[:, 0:16], bias=1024.0)
+    V("qz", "wco wso", "tbt", T.wc[:, 0:P], T.ws[:, 0:P], T.tbt[:])
+    V("qz", "kcx ksx", "xt xtz", T.kc[:, 0:P], T.ks[:, 0:P], T.xt[:])
+    V("tt", "posm", "loc locz locy cdk wm", T.posm[:], T.loc[:].indirect(T.cdk[:]), T.wm[:], op_.mult)
+    V("qz", "kcx ksx", "xu xuz", T.kc[:, 160:288], T.ks[:, 160:288], T.xu[:])
+    V("scan", "posc", "posm r16", T.posc[:], T.r16[:], T.posm[:], 0.0, op_.mult, op_.add)
+    V("copy", "lgs", "lgf", T.lgs[:], T.fc[:, 24:30])
+    V("copy", "kpl", "posc", T.kpl[:], T.posc[:, 15:256:16])
+    V("copy", "xrc", "xc xl", u32(T.xrc[:]), u32(T.xc[:]).indirect(T.xl[:]))
+    V("copy", "nr", "idx idxs cpu", T.nr[:], T.idx[:].indirect(T.cpu[:]))
+    V("qz", "wqc wqs", "wt", T.wqc[:], T.wqs[:], T.wt[:])
+    for j in range(2):
+        V("ts", "lw%d" % j, "nr cpf", T.lw[:, 16 * j:16 * j + 16], T.nr[:, 16 * j:16 * j + 16], T.fc[:, 20 + j:21 + j], None, op_.is_lt)
+    V("qz", "fwo fso", "tbt", T.fwc[:, 0:P], T.fws[:, 0:P], T.tbt[:])
+
+    tot["a_dt"] = 4 * noff + sum(len(e_s[f]) + len(e_s2[f]) for f in from_s)
+    wr_["wca"] = [("a_dt", tot["a_dt"])]
+    for j in range(2):
+        a = 16 + P * j
+        S(Copy, "ks%d" % j, "wso wca kpl ksx", T.ks[:, a:a + P], T.ws[:, 0:WCOLS].indirect(T.kpl[:, 8 * j:8 * j + 8]))
+        V("copy", "kc%d" % j, "wco wca kpl kcx", u32(T.kc[:, a:a + P]), u32(T.wc[:, 0:WCOLS]).indirect(T.kpl[:, 8 * j:8 * j + 8]))
+    for j in range(2):
+        a, c = 16 + P * j, 144 * j
+        mm(T["pg%d" % j][:, 0:144], T.kc[:, a:a + P], T.ks[:, a:a + P], T.kc[:, c:c + 144], T.ks[:, c:c + 144], True, True,
+           "kc%d ks%d kcx ksx" % (j, j), "pg%d" % j)
+        mm(T["pd%d" % j][:, 0:P], T.xrc[:, P * j:P * j + P], T.xrs[:, P * j:P * j + P], T.kc[:, a:a + P], T.ks[:, a:a + P], True, True,
+           "kc%d ks%d xrc xrs" % (j, j), "pd%d" % j)
+    mm(T.pz[:, 0:WCOLS], T.wqc[:], T.wqs[:], T.wc[:, 0:WCOLS], T.ws[:, 0:WCOLS], True, True, "wqc wqs wco wso wca", "pz")
+    S(Ident, "hi", "sk", hi, tf, bias=-7.5)
+    S(Copy, "bsw", "c16", T.bsw[:, 0:34:17], T.c16[:, 0:2])
+    S(Copy, "fv0", "c16", T.fv[:, 0:1], T.c16[:, 0:1])
+    S(Sign, "lh", "lo hi", T.fc[:, 36:38], T.fc[:, 36:38])
+    S(Sign, "r17", "c17", T.r17[:], c17)
+    S(Sign, "r8", "c8", T.r8[:], c8)
+    S(Relu, "lh", "lh", T.fc[:, 36:38], T.fc[:, 36:38])
+    S(Copy, "r17", "r17", T.r17[:], T.r17[:], scale=2.0)
+    V("copy", "pb0", "pg0", T.pb[:, 0:144], T.pg0[:, 0:144])
+    S(Copy, "pb1", "pg1", T.pb[:, 144:288], T.pg1[:, 0:144])
+    V("copy", "pbx0", "pd0", T.pbx[:, 0:P], T.pd0[:, 0:P])
+    S(Copy, "pbx1", "pd1", T.pbx[:, P:2 * P], T.pd1[:, 0:P])
+    for j in range(2):
+        S(Ident, "nrz%d" % j, "nr lh", T.nrz[:, 16 * j:16 * j + 16], T.nr[:, 16 * j:16 * j + 16], bias=[lo, hi][j], scale=[lo, hi][j])
+    S(Ident, "zt1", "idx lh", T.zt[:, 0:256], T.idx[:, 0:256], scale=lo)
+    S(Ident, "zt2", "idx lh", T.zt[:, 256:512], T.idx[:, 0:256], scale=hi)
+    S(Copy, "zb", "pz", T.zb[:, 0:WCOLS], T.pz[:, 0:WCOLS])
+    S(Sign, "lm", "c16 sk", T.lm[:], T.c16[:, 0:64], bias=tf, scale=-1.0)
+    S(Ident, "trs", "sk", T.fc[:, 16:20], T.fc[:, 0:4], bias=1032.0, scale=8.0)
+    V("copy", "gs", "pb0 pb1 lgs", T.gs[:], T.pb[:].indirect(T.lgs[:, 2:4]))
+    V("tt", "eqt", "pbx0 pbx1 lgs gs", eqt, T.pbx[:].indirect(T.lgs[:, 4:6]), T.gs[:], op_.is_equal)
+    V("tt", "gt", "pbx0 pbx1 lgs gs", gt, T.pbx[:].indirect(T.lgs[:, 4:6]), T.gs[:], op_.is_gt)
+    V("tt", "ge2", "pb0 pb1 lgs gs", T.ge2[:], T.pb[:].indirect(T.lgs[:, 0:2]), T.gs[:], op_.is_ge)
+    V("tt", "el", "eqt lw0 lw1", el, eqt, T.lw[:], op_.mult)
+    for j in range(2):
+        a = 16 * j
+        V("scan", "sc%d" % j, "gt el", T.qa[:, 96 + a:112 + a], T.qa[:, 32 + a:48 + a], T.qa[:, 64 + a:80 + a], float(1 + 17 * j), op_.add, op_.add)
+    V("copy", "rku", "sc0 sc1", T.rku[:], T.qa[:, 111:128:16])
+    V("copy", "bsw", "ge2 rku", T.bsw[:].indirect(T.rku[:]), T.ge2[:])
+    V("copy", "nsw", "nrz0 nrz1 rku", T.nsw[:].indirect(T.rku[:]), T.nrz[:])
+    V("scan", "pk", "bsw r17", T.pk[:], T.r17[:], T.bsw[:, 0:34], 0.0, op_.mult, op_.add)
+    V("tt", "ns", "nsw", ns, T.nsw[:, 1:9], T.nsw[:, 18:26], op_.add)
+    V("copy", "pku", "pk", T.pku[:], T.pk[:, 8:26:17])
+    V("copy", "own", "zt1 zt2 pku", T.own[:], T.zt[:].indirect(T.pku[:]))
+    V("copy", "msw", "own rku", T.msw[:].indirect(T.rku[:]), T.own[:])
+    V("tt", "ms", "msw", T.ms[:], T.msw[:, 1:9], T.msw[:, 18:26], op_.add)
+
+    def plane(m):
+        V("ts", "ui%d" % m, "ms", T.ui[:, 8 * m:8 * m + 8], T.ms[:], 7 - m, 1, op_.logical_shift_right, op_.bitwise_and)
+
+    def pair(m, j):
+        V("ts", "fv%d" % j, "ui%d fv%d fv%d" % (m, m, j), T.fv[:, j:j + 1], T.ui[:, 8 * m + j:8 * m + j + 1], T.fv[:, m:m + 1],
+          T.fv[:, j:j + 1], op_.subtract, op_.max)
+
+    def far(m):
+        a = m + 3
+        V("ts", "tmp%d" % m, "ui%d fv%d" % (m, m), T.pn[:, 24 + 8 * m + a:32 + 8 * m], T.ui[:, 8 * m + a:8 * m + 8], T.fv[:, m:m + 1], None, op_.subtract)
+
+    def far2(m):
+        a = m + 3
+        k = " ".join("fv%d" % j for j in range(a, 8))
+        V("tt", k, "tmp%d " % m + k, T.fv[:, a:8], T.fv[:, a:8], T.pn[:, 24 + 8 * m + a:32 + 8 * m], op_.max)
+
+    V("ts", "fv1 fv2 fv3 fv4 fv5 fv6 fv7", "ms", T.fv[:, 1:8], T.ms[:, 1:8], 128.0, None, op_.is_ge)
+    plane(1)
+    plane(2)
+    pair(1, 2)
+    pair(1, 3)
+    far(1)
+    plane(3)
+    pair(2, 3)
+    far2(1)
+    plane(4)
+    pair(2, 4)
+    far(2)
+    plane(5)
+    pair(3, 4)
+    far2(2)
+    plane(6)
+    for m in range(3, 7):
+        for j in range(m + 1, 8):
+            if (m, j) != (3, 4):
+                pair(m, j)
+    fvs = "fv0 fv1 fv2 fv3 fv4 fv5 fv6 fv7"
+    V("ts", "nf", fvs, nf, T.fv[:], 0.0, None, op_.is_equal)
+    V("scan", "psn", fvs + " one", psn, T.one[:, 0:8], T.fv[:], 0.0, op_.add, op_.subtract)
+    V("tt", "kn", "ns nf", kn, ns, nf, op_.mult)
+    V("tt", "eq", "psn c4 lrep", eq, psn.indirect(T.lrep[:]), T.c4[:], op_.is_equal)
+    V("tt", "v4", "eq kn lrep", v4, kn.indirect(T.lrep[:]), eq, op_.mult)
+    V("scan", "sc8", "v4 r8", sc8, T.r8[:], v4, 0.0, op_.mult, op_.add)
+    V("copy", "klu", "sc8", T.klu[:], T.qb[:, 71:96:8])
+    for a in range(0, 2048, 448):
+        w = min(448, 2048 - a)
+        S(Copy, "ebz", "xtz", T.ebt[:, a:a + w], T.xt[:, 64:64 + w])
+    for b in range(4):
+        S(Copy, "ebt", "hid ebz", T.ebt[:, 512 * b + b:512 * b + 512:4], T.hid[:], scale=0.5)
+    S(Relu, "lm", "lm", T.lm[:], T.lm[:])
+    for k in range(8):
+        dma("s" if k % 2 == 0 else "a", "drep", T.kru[16 * k:16 * k + 16, :], T.klu[0:128:8, :], "klu", "kru")
+    dma("s", "dkx", u8(T.pwc[:, 16 * r:16 * r + 16]), u8(T.xc[:, 0:16]), "xc", "pwo")
+    dma("s", "dkx", T.pws[:, 16 * r:16 * r + 16], T.xs[:, 0:16], "xs", "pwo")
+    V("qz", "ec es", "ebt ebz", T.ec[:], T.es[:], T.ebt[:])
+    for b in range(4):
+        mm(T["pd%d" % b][:, 0:P], T.ec[:, P * b:P * b + P], T.es[:, P * b:P * b + P], T.tbc[:], T.tbs[:], True, False, "ec es tbc tbs", "pd%d" % b)
+    S(Copy, "zbz", "xtz", T.zb[:, WCOLS:480], T.xt[:, 64:80])
+    for k in ("wno", "wns", "wnc"):
+        S(Copy, k, "one", T[k][:, P * r + 1:P * r + 1 + P], T.one[:], scale=float(P))
+    S(Copy, "wmb", "wm", T.wmb[:], T.wm[:, 0:P])
+    S(Sign, "r16b", "c16", T.r16b[:], T.c16[:, 0:P])
+
+    V("copy", "kr", "kru", T.kr[:], T.kru[:])
+    V("tt", "rwm", "idx idxs kru lm", T.rwm[:], T.idx[:].indirect(T.kru[:]), T.lm[:], op_.mult)
+    for k in range(4):
+        V("ts", "eqd%d" % k, "rwm kr trs", T.eqd[:, 64 * k:64 * k + 64], T.rwm[:], T.kr[:, k:k + 1], trs[k], op_.is_equal, op_.mult)
+    for k in range(4):
+        V("scan", "scf%d" % k, "eqd%d kr one" % k, T.scf[:, 64 * k:64 * k + 64], T.one[:, 0:64], T.eqd[:, 64 * k:64 * k + 64], T.kr[:, k:k + 1], op_.mult, op_.max)
+    V("copy", "lu", "scf0 scf1 scf2 scf3", T.lu[:], T.scf[:, 63:256:64])
+    send([(T.lu[:], [T.lr[:]] * 2, ids_r[0:2], eon, "r_kl")], "lu")
+    send([(T.lu[:], [T.ll[:, 4 * at_s[y]:4 * at_s[y] + 4]], [ids_s[y]], e_s[y], "a_kls") for y in range(3)], "lu")
+
+    S(Copy, "locr", "loc locz locy kru", T.locr[:, 0:64], T.loc[:].indirect(T.kru[:]))
+    S(Ident, "kpf", "idx idxs kru", T.kpf[:], T.idx[:].indirect(T.kru[:]), bias=-1.0)
+    dma("s", "dkp", T.kp[:], T.kpf[0:1, :], "kpf", "kp")
+    s = P * r + 1
+    V("copy", "wno", "val lu", T.wno[:].indirect(T.lu[:]), T.val[:, 64 * r:64 * r + 64])
+    V("tt", "loc2", "locr wm", T.locr[:, 64:128], T.locr[:, 0:64], T.wm[:, 0:64], op_.mult)
+    V("tt", "wsmo", "wno wmb", T.wsm[:, 3 * P:4 * P], T.wno[:, s:s + P], T.wmb[:], op_.mult)
+    V("scan", "loc3", "loc2 r16", T.locr[:, 128:192], T.r16[:, 0:64], T.locr[:, 64:128], 0.0, op_.mult, op_.add)
+    V("copy", "yl", "loc3", T.yl[:, 0:8:2], T.locr[:, 143:192:16])
+    for k in range(4):
+        S(Copy, "yb", "zb zbz yl", T.yb[:, k:64:4], T.zb[:].indirect(T.yl[:, 2 * k:2 * k + 1]))
+    dma("s", "dy", T.y[:], T.yb[:], "yb", "y")
+
+    tot["a_kls"] = sum(len(e_s[f]) for f in from_s)
+    tot["a_klc"] = 4 * noff // 2
+    wr_["lls"] = [("a_kls", tot["a_kls"])]
+    wr_["llc"] = [("a_klc", tot["a_klc"])]
+    for q in sorted(same, reverse=True):
+        c = 4 * peers.index(q)
+        V("copy", "wns", "val lls", T.wns[:].indirect(T.ll[:, c:c + 4]), T.val[:, 64 * q:64 * q + 64])
+    V("tt", "wsm0", "wns wsmo", T.wsm[:, 0:P], T.wns[:, s:s + P], T.wsm[:, 3 * P:4 * P], op_.min)
+    for q in sorted(cross, reverse=True):
+        c = 4 * peers.index(q)
+        V("copy", "wnc", "val llc", T.wnc[:].indirect(T.ll[:, c:c + 4]), T.val[:, 64 * q:64 * q + 64])
+    V("tt", "wsm1", "wsm0 wnc", T.wsm[:, P:2 * P], T.wsm[:, 0:P], T.wnc[:, s:s + P], op_.min)
+    V("scan", "wsm2", "wsm1 r16b", T.wsm[:, 2 * P:3 * P], T.r16b[:], T.wsm[:, P:2 * P], 0.0, op_.mult, op_.add)
+    won = T.wsm[:, 2 * P + 15:3 * P:16]
+    V("ts", "wu", "wsm2", T.wu[:], won, float(P - 1), None, op_.min)
+    tot["a_pt"] = 7 * 2 * noff
+    wr_["pwa"] = [("a_pt", tot["a_pt"])]
+    S(Copy, "pps", "pwa pwo wu", T.pps[:], T.pws[:].indirect(T.wu[:]))
+    V("copy", "ppc", "pwa pwo wu", u32(T.ppc[:]), u32(T.pwc[:]).indirect(T.wu[:]))
+    for b in range(4):
+        mm(T["pd%d" % b][:, 0:P], T.ec[:, P * b:P * b + P], T.es[:, P * b:P * b + P], T.ppc[:], T.pps[:], False, True, "ec es ppc pps", "pd%d" % b)
+    V("ts", "wl", "wsm2", T.wl[:], won, float(P), float(P), op_.is_lt, op_.mult)
+    V("tt", "wl", "wl sk", T.wl[:], T.wl[:], T.fc[:, 0:8], op_.add)
+    V("copy", "fl", "wl", T.fl[:], T.wl[:])
+    for b in range(4):
+        o, i = T.nt[:, b:512:4], T["pd%d" % b][:, 0:P]
+        if b % 2 == 0:
+            V("copy", "nt%d" % b, "pd%d" % b, o, i)
+        else:
+            S(Copy, "nt%d" % b, "pd%d" % b, o, i)
+    V("qz", "fwn fsn", "nt0 nt1 nt2 nt3", T.fwc[:, P:2 * P], T.fws[:, P:2 * P], T.nt[:])
+    S(Copy, "fos", "fso fsn fl", T.fos[:], T.fws[:].indirect(T.fl[:]))
+    V("copy", "foc", "fwo fwn fl", u32(T.foc[:]), u32(T.fwc[:]).indirect(T.fl[:]))
+    dma("s", "doc", T.oc[:], u8(T.foc[:]), "foc", "oc")
+    for k in range(4):
+        dma("a" if k < 3 else "s", "doc", T.osc[4 * k:4 * k + 4, :], T.fos[32 * k:32 * k + 4, :], "fos", "osc")
+    need("g", [(x, tot[x]) for x in tot])

@@ -1,9 +1,10 @@
 from concourse.bass import DstId, RemoteDMATransfer
-from concourse.mybir import dt, AluOpType, ActivationFunctionType
+from concourse.mybir import dt, AluOpType, ActivationFunctionType, AxisListType
 
 N, P, A, LC = 8, 128, 16, 48
 F32, BF, I32, U16, U8, X4 = "float32", "bfloat16", "int32", "uint16", "uint8", "float8_e4m3fn_x4"
-WCOLS = P + 7 * LC
+RUN = 2 * LC
+WCOLS = 2 * P + 4 * RUN
 SCRATCH = {}
 
 
@@ -12,35 +13,34 @@ def _sb(name, n, d):
 
 
 for _n, _w, _d in [
-    ("cdi", 16, I32), ("cpi", 2, I32), ("tbt", 512, BF), ("xt", 512, BF), ("xu", 512, BF), ("wt", 512, BF),
-    ("cdu", 32, U16), ("fla", 1024, BF), ("flb", 1024, BF), ("mrg", 1024, BF), ("nam", 1024, BF), ("one", 128, BF),
-    ("inc", 1024, BF), ("le", 1792, BF), ("cs", 1792, BF), ("rs", 512, BF),
-    ("sgo", 512, BF), ("sga", 16, F32), ("rq", 12, U16), ("rqx", 10, U16), ("rqr", 6, U16), ("rql", 22, U16),
-    ("tbc", 128, X4), ("tbs", 128, U8), ("wc", 480, X4), ("ws", 480, U8), ("fwc", 256, X4), ("fws", 256, U8),
+    ("cdi", 16, I32), ("cpi", 2, I32), ("tbx", 1024, BF), ("wt", 512, BF),
+    ("cdu", 32, U16), ("fla", 1792, BF), ("flb", 1792, BF), ("mrg", 256, BF), ("nam", 256, BF), ("one", 128, BF),
+    ("inc", 256, BF), ("le", 384, BF), ("cs", 384, BF), ("rs", 384, BF), ("sgo", 384, BF), ("sga", 4, F32),
+    ("rq", 6, U16), ("rql", 18, U16),
+    ("tw", 2 * P, X4), ("tws", 2 * P, U8), ("idl", 10, U16), ("wc", WCOLS, X4), ("ws", WCOLS, U8),
     ("xc", 128, X4), ("xs", 128, U8), ("wqc", 128, X4), ("wqs", 128, U8), ("pwc", 128, X4), ("pws", 128, U8),
-    ("xrc", 256, X4), ("xrs", 256, U8),
-    ("dcc", 192, X4), ("dcs", 192, U8), ("dsc", 144, X4), ("dss", 144, U8), ("rlc", 96, X4), ("rls", 96, U8),
-    ("rpc", 16, X4), ("rps", 16, U8), ("kc", 288, X4), ("ks", 288, U8), ("ppc", 128, X4), ("pps", 128, U8),
-    ("foc", 128, X4), ("fos", 128, U8), ("ebt", 2048, BF), ("ec", 512, X4), ("es", 512, U8),
-    ("ii", 8, I32), ("fc", 40, F32), ("cj", 96, F32), ("idx", 1040, F32), ("c16", 256, F32), ("wm", 256, F32), ("wmb", 128, BF),
-    ("r16", 256, F32), ("r16b", 128, BF), ("lm", 64, F32), ("r17", 34, F32), ("r8", 32, F32), ("c4", 32, F32),
-    ("zt", 512, F32), ("nrz", 32, F32), ("hid", 128, BF), ("val", 512, BF), ("lgs", 6, U16), ("lrep", 2, U16), ("xl", 16, U16),
-    ("loc", 1040, F32), ("cdk", 16, U16), ("posm", 256, F32), ("posc", 256, F32), ("kpl", 16, U16),
+    ("xrc", 256, X4), ("xrs", 256, U8), ("dc", 3 * RUN, X4), ("ds", 3 * RUN, U8), ("rlc", LC, X4), ("rls", P, U8),
+    ("rpc", 16, X4), ("rps", 64, U8), ("kc", 288, X4), ("ks", 288, U8),
+    ("foc", 128, X4), ("fos", 128, U8), ("ez", 516, BF), ("ec", 512, X4), ("es", 512, U8),
+    ("ii", 8, I32), ("fc", 64, F32), ("cj", 64, F32), ("idx", 1024, F32), ("c16", 256, F32), ("wm", 256, F32),
+    ("r16", 256, F32), ("r16b", 128, BF), ("r17", 34, F32), ("c8", 128, F32), ("r8", 128, F32), ("m16", 1040, BF),
+    ("zt", 512, F32), ("nrz", 32, F32), ("lgs", 6, U16), ("xl", 16, U16), ("ci", 32, F32), ("dfl", 8, BF),
+    ("loc", 264, F32), ("cdk", 16, U16), ("posm", 256, F32), ("posc", 256, F32), ("psa", 32, F32), ("kpl", 16, U16),
     ("cpu", 2, U16), ("nr", 32, F32), ("lw", 32, F32),
     ("pb", 288, F32), ("pbx", 256, F32), ("gs", 32, F32), ("qa", 128, F32), ("rku", 2, U16), ("ge2", 32, F32),
     ("bsw", 40, F32), ("pk", 34, F32), ("pku", 2, U16), ("own", 32, F32), ("msw", 40, I32), ("ms", 8, I32), ("nsw", 40, F32),
-    ("ui", 56, I32), ("fv", 8, F32), ("pn", 48, F32), ("qb", 96, F32), ("klu", 4, U16),
-    ("kr", 4, F32), ("kru", 4, U16), ("rwm", 64, F32), ("eqd", 256, BF), ("scf", 256, F32),
-    ("lu", 4, U16), ("lr", 4, U16), ("ll", 28, U16), ("kpf", 64, F32), ("locr", 192, F32), ("yl", 8, U16), ("zb", 480, F32), ("yb", 64, F32),
-    ("wns", 1552, BF), ("wnc", 1552, BF), ("wno", 1552, BF), ("wsm", 512, BF), ("wl", 8, F32), ("wu", 8, U16), ("fl", 8, U16), ("nt", 512, BF),
+    ("ui", 56, I32), ("fv", 8, F32), ("pn", 80, F32),
+    ("off", 4, U16), ("val", 32, BF), ("mp", 1040, BF), ("msc", 1024, BF), ("mo", 64, BF), ("rm", 8, BF), ("ml", 64, BF),
+    ("mx", 64, BF), ("mt", 128, BF), ("wu", 8, U16),
+    ("qb", 72, F32), ("t0", 32, F32), ("t1", 128, F32), ("t2", 128, F32), ("t3", 32, F32), ("t4", 32, F32), ("kpf", 32, F32),
+    ("yl", 8, U16), ("zb", 272, F32), ("yb", 64, F32),
+    ("h0", 384, F32), ("h1", 384, F32), ("h2", 384, F32), ("h3", 384, F32), ("nt", 512, BF),
 ]:
     _sb(_n, _w, _d)
-for _n in ("pg0", "pg1", "pz", "pd0", "pd1", "pd2", "pd3"):
+for _n in ("pg0", "pg1", "pd0", "pd1", "pz", "ph0", "ph1", "ph2"):
     SCRATCH[_n] = ("psum", [128, 512], F32)
-SEMAPHORES = ["cv", "ca", "ct", "cg", "dcd", "dcp", "dtb", "dx", "dxu", "dw", "dkx", "drep", "dy", "dkp", "doc", "ls",
-              "a_rqc", "a_rqs", "a_dt", "a_pt", "a_klc", "a_kls", "r_pt", "r_rq", "r_dt", "r_kl"]
-PART = ("lerq", "lerqx", "csrq", "csrqx", "lgf", "lrep", "loc", "cdk", "yb", "ebz", "ebt", "rs1", "idxs",
-        "rq", "rqx", "sgarq", "sgarqx")
+SEMAPHORES = ["cv", "ca", "ct", "cg", "dcd", "dcp", "dtb", "dx", "dw", "dy", "dkp", "doc", "ls",
+              "a_tb", "a_rq", "a_dt", "a_pt", "a_mc", "a_ms", "r_pt", "r_tb", "r_mp"]
 
 
 def _bits(es):
@@ -53,6 +53,7 @@ def _bits(es):
 def _peers(topo, cores, r):
     cross = [q for q in range(N) if q != r and not topo.may_write(cores[r], cores[q])]
     same = [q for q in range(N) if q != r and topo.may_write(cores[r], cores[q])]
+    assert sorted(q // 2 for q in same + [r]) == list(range(N // 2))
     return cross, same
 
 
@@ -61,7 +62,7 @@ def _relays(topo, cores, r):
     ok = [c for c in topo.cores_of(cores[r]) if c != cores[r] and topo.may_write(c, cores[cross[0]])]
     d0 = [c for c in ok if topo.die(c) == topo.die(cores[r])]
     d1 = [c for c in ok if topo.die(c) != topo.die(cores[r])]
-    return cross, [d0[0], d1[0], d0[1], d1[1]]
+    return [d0[0], d1[0], d0[1], d1[1]]
 
 
 def _dst(topo, d, s):
@@ -74,38 +75,33 @@ def _same_engines(es):
 
 
 def _relay_program(g, core, T, topo, cores, r, x):
-    cross, _ = _peers(topo, cores, r)
-    h = x % 2
-    pair = cross[2 * h:2 * h + 2]
-    ids = [_dst(topo, cores[q], core) for q in pair]
-    es = topo.engines(core, cores[pair[0]])
-    half = [es[0:4], es[4:8]]
-    at = [_peers(topo, cores, q)[0].index(r) for q in pair]
+    cross, same = _peers(topo, cores, r)
+    to = cross + same
+    es = topo.engines(core, cores[cross[x]])
     n = [0]
 
-    def fwd(ts):
-        out = []
-        for src, dsts, to, e, sem in ts:
-            out.append(RemoteDMATransfer(dst_ids=to, dma_engine_mask=_bits(e), remote_sem=T.sem[sem], srcs=[src], dsts=dsts))
-            n[0] += len(e)
-        g.remote_dma_fused(out, local_sem=T.sem.ls)
+    def fwd(src, dst, qs, sem):
+        g.remote_dma_fused([RemoteDMATransfer(dst_ids=[_dst(topo, cores[q], core) for q in qs], dma_engine_mask=_bits(es),
+                                              remote_sem=T.sem[sem], srcs=[src], dsts=[dst] * len(qs))], local_sem=T.sem.ls)
+        n[0] += len(es)
 
     non = len(topo.engines(cores[r], core))
-    a = 16 * r
-    w = [P + LC * at[0], P + LC * at[1]]
-    g.wait_ge(T.sem.r_pt, non // 2)
+    a, o = A * r, P * (r % 2)
+    pts = [(T.rpc[:].bitcast(dt.uint8), T.pwc[:, a:a + A].bitcast(dt.uint8)), (T.rps[:, 0:A], T.pws[:, a:a + A])]
     if x < 2:
-        fwd([(T.rpc[:].bitcast(dt.uint8), [T.pwc[:, a:a + 16].bitcast(dt.uint8)] * 2, ids, es, "a_pt")])
-        g.wait_ge(T.sem.r_rq, non // 2)
-        fwd([(T.rqr[:, 3 * k:3 * k + 3], [T.rql[:, 3 * at[k]:3 * at[k] + 3]], [ids[k]], half[k], "a_rqc") for k in range(2)])
-        g.wait_ge(T.sem.r_dt, non // 2)
-        fwd([(T.rlc[:, LC * k:LC * k + LC].bitcast(dt.uint8), [T.wc[:, w[k]:w[k] + LC].bitcast(dt.uint8)], [ids[k]], half[k], "a_dt") for k in range(2)])
-        g.wait_ge(T.sem.r_kl, non)
-        fwd([(T.lr[:], [T.ll[:, 4 * at[k]:4 * at[k] + 4]], [ids[k]], half[k], "a_klc") for k in range(2)])
+        g.wait_ge(T.sem.r_pt, non // 2)
+        fwd(pts[x][0], pts[x][1], to[0:1], "a_pt")
+    g.wait_ge(T.sem.r_tb, non // 2)
+    if x < 3:
+        w = min(LC, P - LC * x)
+        fwd(T.rlc[:, 0:w].bitcast(dt.uint8), T.tw[:, o + LC * x:o + LC * x + w].bitcast(dt.uint8), [r ^ 1], "a_tb")
     else:
-        fwd([(T.rps[:], [T.pws[:, a:a + 16]] * 2, ids, es, "a_pt")])
-        g.wait_ge(T.sem.r_dt, non // 2)
-        fwd([(T.rls[:, LC * k:LC * k + LC], [T.ws[:, w[k]:w[k] + LC]], [ids[k]], half[k], "a_dt") for k in range(2)])
+        fwd(T.rls[:, 0:P], T.tws[:, o:o + P], [r ^ 1], "a_tb")
+    if x < 2:
+        fwd(pts[x][0], pts[x][1], to[1:], "a_pt")
+    at = _peers(topo, cores, cross[x])[0].index(r)
+    g.wait_ge(T.sem.r_mp, non // 4)
+    fwd(T.rm[:], T.ml[:, 8 * at:8 * at + 8], [cross[x]], "a_mc")
     g.wait_ge(T.sem.ls, n[0])
 
 
@@ -115,7 +111,7 @@ def rank_program(g, core, T, topo):
     if r is None:
         for k in range(N):
             if cores[k] in topo.cores_of(core):
-                _, rel = _relays(topo, cores, k)
+                rel = _relays(topo, cores, k)
                 if core in rel:
                     _relay_program(g, core, T, topo, cores, k, rel.index(core))
         return
@@ -123,9 +119,10 @@ def rank_program(g, core, T, topo):
     op_ = AluOpType
     AF = ActivationFunctionType
     Copy, Sign, Ident, Abs, Relu = AF.Copy, AF.Sign, AF.Identity, AF.Abs, AF.Relu
-    cross, rel = _relays(topo, cores, r)
-    _, same = _peers(topo, cores, r)
-    peers = cross + same
+    rel = _relays(topo, cores, r)
+    cross, same = _peers(topo, cores, r)
+    B = r // 2
+    blk = [slice(32 * b, 32 * b + 32) for b in range(4)]
 
     eng = {"v": g.vector, "a": g.scalar, "t": g.tensor, "g": g, "s": g.sync}
     csem = {"v": "cv", "a": "ca", "t": "ct", "g": "cg"}
@@ -145,25 +142,29 @@ def rank_program(g, core, T, topo):
         mine = csem[e]
         toks = []
         for k in rd:
-            toks += wr_.get(k, [])
+            toks += wr_[k]
         for k in wr:
-            toks += [t for t in wr_.get(k, []) + rd_.get(k, []) if k not in PART or t[0] != mine]
+            toks += wr_.get(k, []) + rd_.get(k, [])
         need(e, toks)
         fn(eng[e]).then_inc(T.sem[mine], 1)
         tot[mine] = tot.get(mine, 0) + 1
         tok = (mine, tot[mine])
         for k in wr:
-            wr_[k] = [t for t in wr_.get(k, []) if t[0] != mine] + [tok] if k in PART else [tok]
+            wr_[k] = [tok]
             rd_[k] = []
         for k in rd:
             rd_[k] = [t for t in rd_.get(k, []) if t[0] != mine] + [tok]
 
     def V(name, wr, rd, *args):
         def fn(q):
-            f = {"copy": q.tensor_copy, "tt": q.tensor_tensor, "ts": q.tensor_scalar, "set": q.memset,
-                 "scan": q.tensor_tensor_scan, "qz": q.quantize_mx}[name]
+            f = {"copy": q.tensor_copy, "tt": q.tensor_tensor, "ts": q.tensor_scalar, "set": q.memset, "tr": q.transpose,
+                 "scan": q.tensor_tensor_scan, "qz": q.quantize_mx, "red": q.tensor_reduce}[name]
             return f(*args)
         do("v", fn, rd.split(), wr.split())
+
+    def VX(wr, rd, *args):
+        V("tt", wr, rd, *args)
+        need("v", wr_[wr])
 
     def S(f, wr, rd, out, in_, **k):
         do("a", lambda q: q.activation(out, in_, f, **k), rd.split(), wr.split())
@@ -174,7 +175,7 @@ def rank_program(g, core, T, topo):
     def dma(e, sem, out, in_, rd, wr):
         toks = []
         for k in rd.split():
-            toks += wr_.get(k, [])
+            toks += wr_[k]
         for k in wr.split():
             toks += [t for t in wr_.get(k, []) + rd_.get(k, []) if t[0] != sem]
         need(e, toks)
@@ -185,8 +186,8 @@ def rank_program(g, core, T, topo):
         for k in rd.split():
             rd_[k] = rd_.get(k, []) + [(sem, None)]
 
-    def mm(out, l, ls, m, ms, start, stop, rd, wr):
-        do("t", lambda q: q.matmul_mx(out, l, ls, m, ms, start, stop), rd.split(), wr.split())
+    def mm(out, l, ls, m, ms, rd, wr):
+        do("t", lambda q: q.matmul_mx(out, l, ls, m, ms, True, True), rd.split(), wr.split())
 
     def u8(v):
         return v.bitcast(dt.uint8)
@@ -195,12 +196,20 @@ def rank_program(g, core, T, topo):
         return v.bitcast(dt.uint32)
 
     def send(transfers, rd):
-        need("g", wr_.get(rd, []))
+        for k in rd.split():
+            need("g", wr_[k])
         ts = []
         for src, dsts, ids, es, sem in transfers:
             ts.append(RemoteDMATransfer(dst_ids=ids, dma_engine_mask=_bits(es), remote_sem=T.sem[sem], srcs=[src], dsts=dsts))
             tot["ls"] = tot.get("ls", 0) + len(es)
         g.remote_dma_fused(ts, local_sem=T.sem.ls)
+
+    def lands(key, sem, n):
+        tot[sem] = n
+        wr_[key] = [(sem, n)]
+
+    def keys(k, n, a=0):
+        return " ".join(k + str(i) for i in range(a, n))
 
     ids_r = [_dst(topo, c, core) for c in rel]
     ids_s = [_dst(topo, cores[q], core) for q in same]
@@ -208,198 +217,208 @@ def rank_program(g, core, T, topo):
     eoff = topo.engines(core, cores[same[0]])
     noff = len(eoff)
     e_h = [eon[0:len(eon) // 2], eon[len(eon) // 2:]]
+    e_q = [eon[len(eon) // 4 * k:len(eon) // 4 * (k + 1)] for k in range(4)]
     e_s, e_s2 = _same_engines(eoff)
-    at_s = []
-    from_s = []
-    for q in same:
-        cq, sq = _peers(topo, cores, q)
-        at_s.append(4 + sq.index(r))
-        from_s.append(sq.index(r))
+    at_s = [_peers(topo, cores, q)[1].index(r) for q in same]
+    o, op = P * (r % 2), P * (1 - r % 2)
 
     pin, ti, o7 = [T.ii[:, 2 * k:2 * k + 2] for k in range(3)]
-    tf = T.fc[:, 0:1]
-    sk = [T.fc[:, k:k + 1] for k in range(8)]
-    trs = [T.fc[:, 16 + k:17 + k] for k in range(4)]
-    cpf, half2, pf2, n8, n8b = T.fc[:, 20:22], T.fc[:, 22:23], T.fc[:, 30:31], T.fc[:, 32:33], T.fc[:, 33:34]
-    lo, hi, half1 = T.fc[:, 36:37], T.fc[:, 37:38], T.fc[:, 38:39]
-    c8, c17, xlf = T.cj[:, 0:32], T.cj[:, 32:66], T.cj[:, 72:88]
+    fc = T.fc
+    tf = fc[:, 0:1]
+    sk = [fc[:, k:k + 1] for k in range(8)]
+    pf2, n8, n8b = fc[:, 30:31], fc[:, 32:33], fc[:, 33:34]
+    lo, hi = fc[:, 36:37], fc[:, 37:38]
+    k7, kq, gb = fc[:, 48:49], fc[:, 50:51], fc[:, 51:52]
+    c17, xlf = T.cj[:, 0:34], T.cj[:, 40:56]
     eqt, gt, el = [T.qa[:, 32 * k:32 * k + 32] for k in range(3)]
-    eq, v4, sc8 = [T.qb[:, 32 * k:32 * k + 32] for k in range(3)]
-    psn, nf, kn, ns = [T.pn[:, 8 * k:8 * k + 8] for k in range(4)]
+    psn, geq, vsc, dn = [T.pn[:, 8 * k:8 * k + 8] for k in range(4)]
+    vv = T.pn[:, 23:24]
+    H = [T["h%d" % b] for b in range(4)]
 
-    dma("a", "dx", T.xt[:, 0:64], T.x[:], "", "xt")
-    for k in range(8):
-        dma("s" if k % 2 == 0 else "a", "dcd", T.cdi[16 * k:16 * k + 16, :], T.cd[:], "", "cdi")
-    dma("s", "dtb", T.tbt[:], T.tb[:], "", "tbt")
-    dma("s", "dxu", T.xu[:, 448:512], T.x[:], "", "xu")
+    dma("s", "dcd", T.cdi[0:16, :], T.cd[:], "", "cdi")
+    dma("a", "dx", T.tbx[:, 512:576], T.x[:], "", "xt")
+    dma("s", "dcd", T.cdi[16:32, :], T.cd[:], "", "cdi")
+    dma("s", "dtb", T.tbx[:, 0:512], T.tb[:], "", "tbt")
     dma("s", "dw", T.wt[:], T.w[:], "", "wt")
     for k in range(8):
         dma("s", "dcp", T.cpi[16 * k:16 * k + 16, :], T.cd[:, 2 * k:2 * k + 2], "", "cpi")
 
     do("g", lambda q: q.iota(pin, [[0, 2]], 0, 1), [], ["pin"])
-    iota(T.fc[:, 8:16], "k16", [[16, 8]])
+    iota(fc[:, 8:16], "k16", [[16, 8]])
     iota(T.c16[:], "c16", [[0, 16], [1, 16]])
-    iota(T.fc[:, 24:26], "lgf", [[128, 2]], 16, 1)
-    iota(T.fc[:, 28:30], "lgf", [[128, 2]], 0, 1)
     iota(pf2, "pf2", [[0, 1]], 0, 1)
+    iota(c17, "c17", [[0, 2], [1, 17]])
 
-    V("set", "xtz", "", T.xt[:, 64:512], 0.0)
+    V("set", "xtz", "", T.tbx[:, 576:1024], 0.0)
     V("set", "one", "", T.one[:], 1.0)
-    V("set", "fla", "", T.fla[:], -200.0)
-
-    for a in range(0, 1024, 448):
-        w = min(448, 1024 - a)
-        S(Copy, "flb%d" % (a // 448), "xtz", T.flb[:, a:a + w], T.xt[:, 64:64 + w])
-    for k in range(4):
-        S(Copy, "rs1", "one", T.rs[:, P * k:P * k + P], T.one[:])
-    S(Copy, "rs", "rs1 xtz", T.rs[:, 0:512:128], T.xt[:, 64:68])
-
-    V("qz", "xc xs", "xt xtz", T.xc[:], T.xs[:], T.xt[:])
-    send([(u8(T.xc[:, 0:16]), [u8(T.rpc[:])] * 2, ids_r[0:2], e_h[0], "r_pt")], "xc")
-    send([(T.xs[:, 0:16], [T.rps[:]] * 2, ids_r[2:4], e_h[1], "r_pt")], "xs")
-    iota(T.idx[:, 0:256], "idx", [[1, 256]])
-    iota(xlf, "xlf", [[1, 2], [2, 8]])
-
-    V("copy", "cdu", "cdi", T.cdu[:, 0:32:2], T.cdi[:])
-    for i in range(A):
-        f = "flb" if i % 2 else "fla"
-        V("copy", f, "cdu one flb0 flb1 flb2" if i % 2 else "cdu one", T[f][:].indirect(T.cdu[:, 2 * i:2 * i + 1]), T.one[:, 0:16])
-        if i == 0:
-            V("ts", "ti", "pin", ti, pin, 15, None, op_.bitwise_and)
-        elif i == 3:
-            V("copy", "tf", "ti", T.fc[:, 34:36], ti)
-        elif i == 6:
-            V("ts", "sk", "k16 tf", T.fc[:, 0:8], T.fc[:, 8:16], T.fc[:, 34:35], None, op_.add)
-    S(Ident, "half2", "sk", half2, sk[2], bias=0.5)
-    S(Ident, "half1", "sk", half1, sk[1], bias=0.5)
+    V("ts", "ti", "pin", ti, pin, 15, None, op_.bitwise_and)
+    V("set", "fla", "", T.fla[:, 768:1024], -200.0)
+    V("copy", "tf", "ti", fc[:, 34:36], ti)
+    V("set", "flb", "", T.flb[:, 768:1024], 0.0)
+    V("ts", "sk", "k16 tf", fc[:, 0:8], fc[:, 8:16], fc[:, 34:35], None, op_.add)
+    V("ts", "bi", "pin", T.ii[:, 6:8], pin, 5, None, op_.logical_shift_right)
+    V("set", "ez", "", T.ez[:], 0.5)
+    V("copy", "bf", "bi", fc[:, 60:62], T.ii[:, 6:8])
+    for k in range(3):
+        S(Copy, "rs%d" % k, "one", T.rs[:, P * k:P * k + P], T.one[:])
+    S(Copy, "rs", "rs0 rs1 rs2 xtz", T.rs[:, 0:384:128], T.tbx[:, 576:579])
+    S(Ident, "half", "sk", fc[:, 44:47], fc[:, 0:3], bias=0.5)
     S(Copy, "n8", "sk", n8, tf, scale=-0.125)
-    S(Copy, "lhc", "sk", T.fc[:, 39:40], tf, scale=-1.0)
+    S(Copy, "lhc", "sk", fc[:, 39:40], tf, scale=-1.0)
     S(Abs, "wm", "c16 sk", T.wm[:], T.c16[:], bias=tf, scale=-1.0)
     S(Ident, "n8b", "n8", n8b, n8, bias=273.0)
-    S(Ident, "lo", "lhc", lo, T.fc[:, 39:40], bias=7.5)
-    S(Ident, "lgf", "pf2 n8", T.fc[:, 26:27], pf2, bias=n8, scale=0.125)
+    S(Ident, "lo", "lhc", lo, fc[:, 39:40], bias=7.5)
+    S(Ident, "lg2", "pf2 n8", fc[:, 26:27], pf2, bias=n8, scale=0.125)
     S(Relu, "wm", "wm", T.wm[:], T.wm[:], bias=1.0, scale=-1.0)
-
-    def lists(qs, base, name, out, more):
-        n = len(qs)
-        h0 = base // P
-        nk = [n, n - more]
-        todo = [(x, half2, h0 + x) for x in range(n)] + [(x, half1, h0 + 4 + x) for x in range(n - more, n)]
-        for q in qs:
-            V("scan", "mrg%d" % q, "fla flb", T.mrg[:, P * q:P * q + P], T.fla[:, P * q:P * q + P], T.flb[:, P * q:P * q + P], 0.0, op_.add, op_.max)
-        for q in qs:
-            V("ts", "nam%d" % q, "mrg%d" % q, T.nam[:, P * q:P * q + P], T.mrg[:, P * q:P * q + P], 0.5, None, op_.is_ge)
-        for q in qs:
-            V("scan", "inc%d" % q, "nam%d one" % q, T.inc[:, P * q:P * q + P], T.one[:], T.nam[:, P * q:P * q + P], 0.0, op_.mult, op_.add)
-        for y, (x, half, col) in enumerate(todo):
-            b = P * (y % 4)
-            S(Sign, "sgo%d sga%s" % (y % 4, name), "inc%d half1 half2" % qs[x], T.sgo[:, b:b + P - 1], T.inc[:, P * qs[x]:P * qs[x] + P - 1],
-              bias=half, scale=-1.0, accum_out=T.sga[:, col:col + 1])
-        for k in range(2):
-            for x in range(nk[k]):
-                a = base + P * (n * k + x)
-                V("ts", "le" + name, "inc%d sk" % qs[x], T.le[:, a:a + P], T.inc[:, P * qs[x]:P * qs[x] + P], sk[k], None, op_.is_le)
-        for k in range(2):
-            a, e = base + P * n * k, base + P * (n * k + nk[k])
-            V("scan", "cs" + name, "rs le" + name, T.cs[:, a:e], T.rs[:, 0:P * nk[k]], T.le[:, a:e], 0.0, op_.mult, op_.add)
-        V("ts", name, "sga" + name, out[:, 2:3 * n:3], T.sga[:, h0:h0 + n], 0.5, 0.5 * (P - 1), op_.mult, op_.add)
-        V("ts", name, "sga" + name, out[:, 3 * (n - more) + 1:3 * n:3], T.sga[:, h0 + 4 + n - more:h0 + 4 + n], 0.5, 0.5 * (P - 1), op_.mult, op_.add)
-        for k in range(2):
-            V("copy", name, "cs" + name, out[:, k:3 * nk[k]:3], T.cs[:, base + P * n * k + P - 2:base + P * (n * k + nk[k]):P])
-
-    lists(cross, 0, "rq", T.rq, 2)
-    send([(T.rq[:, 6 * h:6 * h + 6], [T.rqr[:]], [ids_r[h]], e_h[h], "r_rq") for h in range(2)], "rq")
-    lists(same, 1024, "rqx", T.rqx, 1)
-    send([(T.rqx[:, 3 * y:3 * y + 3], [T.rql[:, 3 * at_s[y]:3 * at_s[y] + 3]], [ids_s[y]], e_s[y], "a_rqs") for y in range(3)], "rqx")
-
-    V("qz", "tbc tbs", "tbt", T.tbc[:], T.tbs[:], T.tbt[:])
-    for x, q in enumerate(peers):
-        S(Ident, "loc", "inc%d" % q, T.loc[:, 1 + P * q:1 + P * q + P], T.inc[:, P * q:P * q + P], bias=float(P + LC * x - 1))
-    S(Ident, "loc", "idx", T.loc[:, 1 + P * r:1 + P * r + P], T.idx[:, 0:P], bias=0.0)
-    S(Sign, "r16", "c16", T.r16[:], T.c16[:])
-    S(Ident, "lgf", "pf2 n8b", T.fc[:, 27:28], pf2, bias=n8b, scale=0.125)
-    V("set", "locz", "", T.loc[:, 0:1], float(WCOLS))
-    V("set", "locy", "", T.loc[:, 1025:1040], float(WCOLS))
-    V("ts", "o7", "pin", o7, pin, 7, None, op_.bitwise_and)
-    V("ts", "cdk", "cdi", T.cdk[:, 0:8], T.cdi[:, 0:16:2], 1.0, None, op_.add)
-    V("ts", "cdk", "cdi", T.cdk[:, 8:16], T.cdi[:, 1:16:2], 1.0, None, op_.add)
-    V("copy", "cpf", "cpi", cpf, T.cpi[:])
-    V("copy", "cpu", "cpi", T.cpu[:], T.cpi[:])
-    V("copy", "xl", "xlf", T.xl[:], xlf)
-    V("ts", "lrep", "o7", T.lrep[:], o7, 0.0, None, op_.add)
-
-    tot["a_rqc"] = 4 * noff // 2
-    tot["a_rqs"] = sum(len(e_s[f]) for f in from_s)
-    wr_["rqlc"] = [("a_rqc", tot["a_rqc"])]
-    wr_["rqls"] = [("a_rqs", tot["a_rqs"])]
-    S(Copy, "dcs", "tbs rqlc", T.dcs[:], T.tbs[:].indirect(T.rql[:, 0:12]))
-    V("copy", "dcc", "tbc rqlc", u32(T.dcc[:]), u32(T.tbc[:]).indirect(T.rql[:, 0:12]))
-    S(Copy, "dss", "tbs rqls", T.dss[:], T.tbs[:].indirect(T.rql[:, 12:21]))
-    V("copy", "dsc", "tbc rqls", u32(T.dsc[:]), u32(T.tbc[:]).indirect(T.rql[:, 12:21]))
-    send([(u8(T.dcc[:, 96 * h:96 * h + 96]), [u8(T.rlc[:])], [ids_r[h]], e_h[h], "r_dt") for h in range(2)], "dcc")
-    send([(T.dcs[:, 96 * h:96 * h + 96], [T.rls[:]], [ids_r[2 + h]], e_h[h], "r_dt") for h in range(2)], "dcs")
-    ws_ = [P + LC * at_s[y] for y in range(3)]
-    send([(u8(T.dsc[:, LC * y:LC * y + LC]), [u8(T.wc[:, ws_[y]:ws_[y] + LC])], [ids_s[y]], e_s[y], "a_dt") for y in range(3)], "dsc")
-    send([(T.dss[:, LC * y:LC * y + LC], [T.ws[:, ws_[y]:ws_[y] + LC]], [ids_s[y]], e_s2[y], "a_dt") for y in range(3)], "dss")
-    iota(c17, "c17", [[0, 2], [1, 17]])
-    iota(c8, "c8", [[0, 4], [1, 8]])
-    iota(T.c4[:], "c4", [[1, 4], [0, 8]], 1)
-    send([(u8(T.xc[:, 0:16]), [u8(T.pwc[:, 16 * r:16 * r + 16])] * 3, ids_s, eoff, "a_pt")], "xc")
-    send([(T.xs[:, 0:16], [T.pws[:, 16 * r:16 * r + 16]] * 3, ids_s, eoff, "a_pt")], "xs")
-    do("g", lambda q: q.affine_select(T.hid[:], T.one[:], [[-1, 128]], op_.is_equal, 0.0, 0, 1), ["one"], ["hid"])
-    iota(T.val[:], "val", [[16, 8], [0, 4], [1, 16]])
-
-    S(Copy, "xuz", "xtz", T.xu[:, 0:448], T.xt[:, 64:512])
-    S(Copy, "xrs", "xs xl", T.xrs[:], T.xs[:].indirect(T.xl[:]))
-    for k in range(1, 4):
-        S(Ident, "idxs", "idx", T.idx[:, 256 * k:256 * k + 256], T.idx[:, 0:256], bias=float(256 * k))
-    S(Ident, "idxs", "idx", T.idx[:, 1024:1040], T.idx[:, 0:16], bias=1024.0)
-    V("qz", "wco wso", "tbt", T.wc[:, 0:P], T.ws[:, 0:P], T.tbt[:])
-    V("qz", "kcx ksx", "xt xtz", T.kc[:, 0:P], T.ks[:, 0:P], T.xt[:])
-    V("tt", "posm", "loc locz locy cdk wm", T.posm[:], T.loc[:].indirect(T.cdk[:]), T.wm[:], op_.mult)
-    V("qz", "kcx ksx", "xu xuz", T.kc[:, 160:288], T.ks[:, 160:288], T.xu[:])
-    V("scan", "posc", "posm r16", T.posc[:], T.r16[:], T.posm[:], 0.0, op_.mult, op_.add)
-    V("copy", "lgs", "lgf", T.lgs[:], T.fc[:, 24:30])
-    V("copy", "kpl", "posc", T.kpl[:], T.posc[:, 15:256:16])
-    V("copy", "xrc", "xc xl", u32(T.xrc[:]), u32(T.xc[:]).indirect(T.xl[:]))
-    V("copy", "nr", "idx idxs cpu", T.nr[:], T.idx[:].indirect(T.cpu[:]))
-    V("qz", "wqc wqs", "wt", T.wqc[:], T.wqs[:], T.wt[:])
-    for j in range(2):
-        V("ts", "lw%d" % j, "nr cpf", T.lw[:, 16 * j:16 * j + 16], T.nr[:, 16 * j:16 * j + 16], T.fc[:, 20 + j:21 + j], None, op_.is_lt)
-    V("qz", "fwo fso", "tbt", T.fwc[:, 0:P], T.fws[:, 0:P], T.tbt[:])
-
-    tot["a_dt"] = 4 * noff + sum(len(e_s[f]) + len(e_s2[f]) for f in from_s)
-    wr_["wca"] = [("a_dt", tot["a_dt"])]
-    for j in range(2):
-        a = 16 + P * j
-        S(Copy, "ks%d" % j, "wso wca kpl ksx", T.ks[:, a:a + P], T.ws[:, 0:WCOLS].indirect(T.kpl[:, 8 * j:8 * j + 8]))
-        V("copy", "kc%d" % j, "wco wca kpl kcx", u32(T.kc[:, a:a + P]), u32(T.wc[:, 0:WCOLS]).indirect(T.kpl[:, 8 * j:8 * j + 8]))
-    for j in range(2):
-        a, c = 16 + P * j, 144 * j
-        mm(T["pg%d" % j][:, 0:144], T.kc[:, a:a + P], T.ks[:, a:a + P], T.kc[:, c:c + 144], T.ks[:, c:c + 144], True, True,
-           "kc%d ks%d kcx ksx" % (j, j), "pg%d" % j)
-        mm(T["pd%d" % j][:, 0:P], T.xrc[:, P * j:P * j + P], T.xrs[:, P * j:P * j + P], T.kc[:, a:a + P], T.ks[:, a:a + P], True, True,
-           "kc%d ks%d xrc xrs" % (j, j), "pd%d" % j)
-    mm(T.pz[:, 0:WCOLS], T.wqc[:], T.wqs[:], T.wc[:, 0:WCOLS], T.ws[:, 0:WCOLS], True, True, "wqc wqs wco wso wca", "pz")
     S(Ident, "hi", "sk", hi, tf, bias=-7.5)
     S(Copy, "bsw", "c16", T.bsw[:, 0:34:17], T.c16[:, 0:2])
     S(Copy, "fv0", "c16", T.fv[:, 0:1], T.c16[:, 0:1])
-    S(Sign, "lh", "lo hi", T.fc[:, 36:38], T.fc[:, 36:38])
+    S(Sign, "lh", "lo hi", fc[:, 36:38], fc[:, 36:38])
     S(Sign, "r17", "c17", T.r17[:], c17)
-    S(Sign, "r8", "c8", T.r8[:], c8)
-    S(Relu, "lh", "lh", T.fc[:, 36:38], T.fc[:, 36:38])
+    S(Relu, "lh", "lh", fc[:, 36:38], fc[:, 36:38])
     S(Copy, "r17", "r17", T.r17[:], T.r17[:], scale=2.0)
+    S(Copy, "lh16", "lh", fc[:, 56:58], fc[:, 36:38], scale=16.0)
+    S(Ident, "lg3", "pf2 n8b", fc[:, 27:28], pf2, bias=n8b, scale=0.125)
+    for h in range(2):
+        S(Ident, "lb%d" % h, "bf", fc[:, 42 + h:43 + h], fc[:, 60:61], bias=float(2 * P + LC * h - 1), scale=float(RUN))
+    S(Sign, "r16", "c16", T.r16[:], T.c16[:])
+
+    V("qz", "xc xs", "xt xtz", T.xc[:], T.xs[:], T.tbx[:, 512:1024])
+    send([(u8(T.xc[:, 0:16]), [u8(T.rpc[:])], ids_r[0:1], e_h[0], "r_pt"),
+          (T.xs[:, 0:64], [T.rps[:]], ids_r[1:2], e_h[1], "r_pt")], "xc")
+
+    for b in range(4):
+        V("ts", "cdu%d" % b, "cdi", T.cdu[blk[b], 0:32:2], T.cdi[0:32, :], float(768 - 256 * b), None, op_.add)
+    for i in range(A):
+        f = "flb" if i % 2 else "fla"
+        V("copy", f, keys("cdu", 4) + " one", T[f][:].indirect(T.cdu[:, 2 * i:2 * i + 1]), T.one[:, 0:16])
+        if i == 3:
+            V("qz", "two", "tbt", T.tw[:, o:o + P], T.tws[:, o:o + P], T.tbx[:, 0:512])
+    send([(u8(T.tw[:, o + 2 * LC:o + P]), [u8(T.rlc[:, 0:P - 2 * LC])], [ids_r[2]], e_h[0], "r_tb"),
+          (T.tws[:, o:o + P], [T.rls[:]], [ids_r[3]], e_h[1], "r_tb")], "two")
+    send([(u8(T.tw[:, o + LC * x:o + LC * x + LC]), [u8(T.rlc[:])], [ids_r[x]], e_h[x], "r_tb") for x in range(2)], "two")
+    iota(T.idx[:, 0:256], "idx", [[1, 256]])
+    V("scan", "mrg", "fla flb", T.mrg[:], T.fla[:, 768:1024], T.flb[:, 768:1024], 0.0, op_.add, op_.max)
+    V("ts", "nam", "mrg", T.nam[:], T.mrg[:], 0.5, None, op_.is_ge)
+    V("scan", "inc", "nam rs", T.inc[:], T.rs[:, 0:256], T.nam[:], 0.0, op_.mult, op_.add)
+    for k in range(3):
+        S(Sign, "sg%d" % k, "inc half", T.sgo[:, P * k:P * k + P - 1], T.inc[:, P:2 * P - 1],
+          bias=fc[:, 44 + k:45 + k], scale=-1.0, accum_out=T.sga[:, k:k + 1])
+    for k in range(3):
+        V("ts", "le%d" % k, "inc sk", T.le[:, P * k:P * k + P], T.inc[:, 0:P], sk[k], None, op_.is_le)
+    V("scan", "cs", "rs le0 le1 le2", T.cs[:], T.rs[:], T.le[:], 0.0, op_.mult, op_.add)
+    V("ts", "rq1", "sg0 sg1 sg2", T.rq[:, 3:6], T.sga[:, 0:3], 0.5, 0.5 * (P - 1) + P, op_.mult, op_.add)
+    V("copy", "rq0", "cs", T.rq[:, 0:3], T.cs[:, P - 2:384:P])
+    send([(T.rq[:], [T.rql[:, 6 * a:6 * a + 6] for a in at_s], ids_s, eoff, "a_rq")], "rq0 rq1")
+    iota(xlf, "xlf", [[1, 2], [2, 8]])
+    iota(fc[:, 24:26], "lg0", [[128, 2]], 16, 1)
+    iota(fc[:, 28:30], "lg4", [[128, 2]], 0, 1)
+    do("g", lambda q: q.affine_select(T.ez[:], T.ez[:], [[-1, 516]], op_.is_equal, 0.0, 3, 4), ["ez"], ["ez"])
+
+    for k in range(2):
+        V("ts", "cdk%d" % k, keys("cdu", 4), T.cdk[:, 8 * k:8 * k + 8], T.cdu[:, 2 * k:32:4], -767.0, 257.0, op_.add, op_.min)
+    V("set", "locz", "", T.loc[:, 0:258:257], 0.0)
+    V("qz", "wco", "tbt", T.wc[:, o:o + P], T.ws[:, o:o + P], T.tbx[:, 0:512])
+    V("ts", "idl", "sk", T.idl[:, 0:8], fc[:, 0:8], float(op), None, op_.add)
+    V("copy", "idx8", "sk", T.idl[:, 8:10], fc[:, 0:2])
+    V("qz", "kcx", "xt xtz", T.kc[:, 0:P], T.ks[:, 0:P], T.tbx[:, 512:1024])
+    V("qz", "kcy", "xt tbt", T.kc[:, 160:288], T.ks[:, 160:288], T.tbx[:, 64:576])
+    V("ts", "o7", "pin", o7, pin, 7, None, op_.bitwise_and)
+    V("copy", "cpf", "cpi", fc[:, 20:22], T.cpi[:])
+    V("copy", "cpu", "cpi", T.cpu[:], T.cpi[:])
+    V("copy", "k7", "o7", fc[:, 48:50], o7)
+    for h in range(2):
+        S(Ident, "loc%d" % h, "inc lb%d" % h, T.loc[:, 1 + P * h:1 + P * h + P], T.inc[:, P * h:P * h + P], bias=fc[:, 42 + h:43 + h])
+    S(Copy, "loc", "loc0 loc1 idx", T.loc[blk[B], 1:257], T.idx[blk[B], 0:256])
+
+    lands("twp", "a_tb", 4 * noff)
+    lands("rqa", "a_rq", 3 * noff)
+    for b in range(4):
+        if b != B:
+            V("copy", "rql%d" % b, "rqa", T.rql[blk[b], :], T.rql[blk[B], :])
+    wr_["rql%d" % B] = wr_["rqa"]
+    S(Copy, "ds", "two twp " + keys("rql", 4), T.ds[:], T.tws[:].indirect(T.rql[:]))
+    V("copy", "dc", "two twp " + keys("rql", 4), u32(T.dc[:]), u32(T.tw[:]).indirect(T.rql[:]))
+    w0 = 2 * P + RUN * B
+    send([(u8(T.dc[:, RUN * y:RUN * y + RUN]), [u8(T.wc[:, w0:w0 + RUN])], [ids_s[y]], e_s[y], "a_dt") for y in range(3)], "dc")
+    send([(T.ds[:, RUN * y:RUN * y + RUN], [T.ws[:, w0:w0 + RUN]], [ids_s[y]], e_s2[y], "a_dt") for y in range(3)], "ds")
+    iota(T.c8[:], "c8", [[0, 16], [1, 8]])
+    iota(T.m16[:], "m16", [[0, 65], [1, 16]])
+
+    S(Copy, "wsp", "two twp idl", T.ws[:, op:op + P], T.tws[:].indirect(T.idl[:, 0:8]))
+    for k in range(1, 4):
+        S(Ident, "idx%d" % k, "idx", T.idx[:, 256 * k:256 * k + 256], T.idx[:, 0:256], bias=float(256 * k))
+    V("tt", "posm", "loc locz cdk0 cdk1 wm", T.posm[:], T.loc[:, 0:258].indirect(T.cdk[:]), T.wm[:], op_.mult)
+    V("copy", "xl", "xlf", T.xl[:], xlf)
+    V("scan", "posc", "posm r16", T.posc[:], T.r16[:], T.posm[:], 0.0, op_.mult, op_.add)
+    V("copy", "lgs", "lg0 lg2 lg3 lg4", T.lgs[:], fc[:, 24:30])
+    VX("psa", "posc", T.psa[0:64, 0:16], T.posc[0:64, 15:256:16], T.posc[64:128, 15:256:16], op_.add)
+    VX("psb", "psa", T.psa[0:32, 16:32], T.psa[0:32, 0:16], T.psa[32:64, 0:16], op_.add)
+    for b in range(4):
+        V("qz", "ec%d" % b, "ez", T.ec[:, P * b:P * b + P], T.es[:, P * b:P * b + P], T.ez[:, 3 - b:515 - b])
+    for b in range(4):
+        V("copy", "kpl%d" % b, "psb", T.kpl[blk[b], :], T.psa[0:32, 16:32])
+    pb_ = ["pg0", "pg1", "pd0", "pd1"]
+    for b in range(4):
+        mm(T[pb_[b]][:, 0:P], T.ec[:, P * b:P * b + P], T.es[:, P * b:P * b + P], T.wc[:, o:o + P], T.ws[:, o:o + P], "ec%d wco" % b, pb_[b])
+    for b in range(4):
+        V("tt", "ho%d" % b, "tbt " + pb_[b], H[b][:, 256:384], T.tbx[:, b:512:4], T[pb_[b]][:, 0:P], op_.subtract)
+    V("copy", "wcp", "two twp idl", u32(T.wc[:, op:op + P]), u32(T.tw[:]).indirect(T.idl[:, 0:8]))
+    V("copy", "nr", "idx idx1 idx2 idx3 cpu", T.nr[:], T.idx[:].indirect(T.cpu[:]))
+    S(Copy, "xrs", "xs xl", T.xrs[:], T.xs[:].indirect(T.xl[:]))
+    V("copy", "xrc", "xc xl", u32(T.xrc[:]), u32(T.xc[:]).indirect(T.xl[:]))
+    for b in range(4):
+        S(Copy, "hv%d" % b, "ho%d " % b + pb_[b], H[b][:, 0:P], T[pb_[b]][:, 0:P])
+    for j in range(2):
+        V("ts", "lw%d" % j, "nr cpf", T.lw[:, 16 * j:16 * j + 16], T.nr[:, 16 * j:16 * j + 16], fc[:, 20 + j:21 + j], None, op_.is_lt)
+    V("qz", "wqc wqs", "wt", T.wqc[:], T.wqs[:], T.wt[:])
+    V("copy", "pwo", "xc idx8", u32(T.pwc[:, A * r:A * r + A]), u32(T.xc[:]).indirect(T.idl[:, 8:9]))
+    V("ts", "kq0", "k7", kq, k7, 3.5, 100.0, op_.is_ge, op_.mult)
+    V("ts", "mk4", "k7 c16", fc[:, 52:56], T.c16[:, 0:4], k7, None, op_.is_equal)
+    V("ts", "kq", "kq0 k7", kq, kq, k7, 1.0, op_.add, op_.add)
+    V("set", "nsz", "", T.pn[:, 40:41], 0.0)
+    S(Ident, "zt1", "idx lh", T.zt[:, 0:256], T.idx[:, 0:256], scale=lo)
+    S(Ident, "zt2", "idx lh", T.zt[:, 256:512], T.idx[:, 0:256], scale=hi)
+    S(Copy, "pso", "xs idx8", T.pws[:, A * r:A * r + A], T.xs[:].indirect(T.idl[:, 8:9]))
+    V("set", "mp", "", T.mp[:], 0.0)
+
+    lands("wca", "a_dt", sum(len(e_s[f]) + len(e_s2[f]) for f in at_s))
+    for j in range(2):
+        a = 16 + P * j
+        rd = "wco wcp wsp wca kcx kcy " + keys("kpl", 4)
+        S(Copy, "ks%d" % j, rd, T.ks[:, a:a + P], T.ws[:].indirect(T.kpl[:, 8 * j:8 * j + 8]))
+        V("copy", "kc%d" % j, rd, u32(T.kc[:, a:a + P]), u32(T.wc[:]).indirect(T.kpl[:, 8 * j:8 * j + 8]))
+    for j in range(2):
+        a, c = 16 + P * j, 144 * j
+        mm(T["pg%d" % j][:, 0:144], T.kc[:, a:a + P], T.ks[:, a:a + P], T.kc[:, c:c + 144], T.ks[:, c:c + 144], "kc%d ks%d" % (j, j), "pg%d" % j)
+        mm(T["pd%d" % j][:, 0:P], T.xrc[:, P * j:P * j + P], T.xrs[:, P * j:P * j + P], T.kc[:, a:a + P], T.ks[:, a:a + P],
+           "kc%d ks%d xrc xrs" % (j, j), "pd%d" % j)
+    mm(T.pz[:, 0:256], T.wqc[:], T.wqs[:], T.kc[:, 16:272], T.ks[:, 16:272], "wqc wqs kc0 ks0 kc1 ks1", "pz")
+    lands("pwa", "a_pt", 7 * 2 * noff)
+    ph_ = ["ph0", "ph1", "ph2", "pd0"]
+    for b in range(3):
+        mm(T[ph_[b]][:, 0:P], T.ec[:, P * b:P * b + P], T.es[:, P * b:P * b + P], T.pwc[:], T.pws[:], "ec%d pwa pwo pso" % b, ph_[b])
+    V("set", "mx0", "", T.mx[0:32, 32:64], 0.0)
+    V("set", "t0z", "", T.t0[:], 0.0)
     V("copy", "pb0", "pg0", T.pb[:, 0:144], T.pg0[:, 0:144])
     S(Copy, "pb1", "pg1", T.pb[:, 144:288], T.pg1[:, 0:144])
     V("copy", "pbx0", "pd0", T.pbx[:, 0:P], T.pd0[:, 0:P])
     S(Copy, "pbx1", "pd1", T.pbx[:, P:2 * P], T.pd1[:, 0:P])
+    mm(T.pd0[:, 0:P], T.ec[:, 3 * P:4 * P], T.es[:, 3 * P:4 * P], T.pwc[:], T.pws[:], "ec3 pwa pwo pso", "pd0")
     for j in range(2):
-        S(Ident, "nrz%d" % j, "nr lh", T.nrz[:, 16 * j:16 * j + 16], T.nr[:, 16 * j:16 * j + 16], bias=[lo, hi][j], scale=[lo, hi][j])
-    S(Ident, "zt1", "idx lh", T.zt[:, 0:256], T.idx[:, 0:256], scale=lo)
-    S(Ident, "zt2", "idx lh", T.zt[:, 256:512], T.idx[:, 0:256], scale=hi)
-    S(Copy, "zb", "pz", T.zb[:, 0:WCOLS], T.pz[:, 0:WCOLS])
-    S(Sign, "lm", "c16 sk", T.lm[:], T.c16[:, 0:64], bias=tf, scale=-1.0)
-    S(Ident, "trs", "sk", T.fc[:, 16:20], T.fc[:, 0:4], bias=1032.0, scale=8.0)
+        S(Ident, "nrz%d" % j, "nr lh lh16", T.nrz[:, 16 * j:16 * j + 16], T.nr[:, 16 * j:16 * j + 16], bias=fc[:, 56 + j:57 + j], scale=[lo, hi][j])
+    S(Ident, "cd0", "lg2", fc[:, 58:59], fc[:, 26:27], bias=float(255 - A * r), scale=-1.0)
+    S(Ident, "cd1", "lg2", fc[:, 59:60], fc[:, 26:27], bias=float(254 - A * r), scale=-1.0)
+    S(Sign, "r16b", "c16", T.r16b[:], T.c16[:, 0:P])
+    S(Copy, "zb", "pz", T.zb[:, 16:272], T.pz[:, 0:256])
+    S(Copy, "zbz", "xtz", T.zb[:, 0:16], T.tbx[:, 576:592])
+    S(Ident, "dfl", "sk", T.dfl[:], fc[:, 0:8], bias=float(P - 1), scale=-1.0)
+    S(Ident, "gb", "lg2", gb, fc[:, 26:27], bias=16.0, scale=8.0)
+    S(Sign, "r8", "c8", T.r8[:], T.c8[:])
+    S(Ident, "ci0", "gb c16", T.ci[:, 0:16], T.c16[:, 0:16], bias=gb)
+    S(Ident, "ci1", "ci0", T.ci[:, 16:32], T.ci[:, 0:16], bias=float(P))
+    for b in range(4):
+        S(Copy, "hp%d" % b, ph_[b], H[b][:, P:2 * P], T[ph_[b]][:, 0:P])
     V("copy", "gs", "pb0 pb1 lgs", T.gs[:], T.pb[:].indirect(T.lgs[:, 2:4]))
     V("tt", "eqt", "pbx0 pbx1 lgs gs", eqt, T.pbx[:].indirect(T.lgs[:, 4:6]), T.gs[:], op_.is_equal)
     V("tt", "gt", "pbx0 pbx1 lgs gs", gt, T.pbx[:].indirect(T.lgs[:, 4:6]), T.gs[:], op_.is_gt)
@@ -412,8 +431,9 @@ def rank_program(g, core, T, topo):
     V("copy", "bsw", "ge2 rku", T.bsw[:].indirect(T.rku[:]), T.ge2[:])
     V("copy", "nsw", "nrz0 nrz1 rku", T.nsw[:].indirect(T.rku[:]), T.nrz[:])
     V("scan", "pk", "bsw r17", T.pk[:], T.r17[:], T.bsw[:, 0:34], 0.0, op_.mult, op_.add)
-    V("tt", "ns", "nsw", ns, T.nsw[:, 1:9], T.nsw[:, 18:26], op_.add)
+    V("tt", "ns", "nsw", T.pn[:, 32:40], T.nsw[:, 1:9], T.nsw[:, 18:26], op_.add)
     V("copy", "pku", "pk", T.pku[:], T.pk[:, 8:26:17])
+    V("tt", "dn", "ns nsz", dn, T.pn[:, 32:40], T.pn[:, 33:41], op_.subtract)
     V("copy", "own", "zt1 zt2 pku", T.own[:], T.zt[:].indirect(T.pku[:]))
     V("copy", "msw", "own rku", T.msw[:].indirect(T.rku[:]), T.own[:])
     V("tt", "ms", "msw", T.ms[:], T.msw[:, 1:9], T.msw[:, 18:26], op_.add)
@@ -425,119 +445,98 @@ def rank_program(g, core, T, topo):
         V("ts", "fv%d" % j, "ui%d fv%d fv%d" % (m, m, j), T.fv[:, j:j + 1], T.ui[:, 8 * m + j:8 * m + j + 1], T.fv[:, m:m + 1],
           T.fv[:, j:j + 1], op_.subtract, op_.max)
 
-    def far(m):
-        a = m + 3
-        V("ts", "tmp%d" % m, "ui%d fv%d" % (m, m), T.pn[:, 24 + 8 * m + a:32 + 8 * m], T.ui[:, 8 * m + a:8 * m + 8], T.fv[:, m:m + 1], None, op_.subtract)
+    def far(m, a):
+        V("ts", "tmp%d" % m, "ui%d fv%d" % (m, m), T.pn[:, 40 + 8 * m + a:48 + 8 * m], T.ui[:, 8 * m + a:8 * m + 8], T.fv[:, m:m + 1], None, op_.subtract)
 
-    def far2(m):
-        a = m + 3
-        k = " ".join("fv%d" % j for j in range(a, 8))
-        V("tt", k, "tmp%d " % m + k, T.fv[:, a:8], T.fv[:, a:8], T.pn[:, 24 + 8 * m + a:32 + 8 * m], op_.max)
+    def far2(m, a):
+        k = keys("fv", 8, a)
+        V("tt", k, "tmp%d " % m + k, T.fv[:, a:8], T.fv[:, a:8], T.pn[:, 40 + 8 * m + a:48 + 8 * m], op_.max)
 
-    V("ts", "fv1 fv2 fv3 fv4 fv5 fv6 fv7", "ms", T.fv[:, 1:8], T.ms[:, 1:8], 128.0, None, op_.is_ge)
+    V("ts", keys("fv", 8, 1), "ms", T.fv[:, 1:8], T.ms[:, 1:8], 128.0, None, op_.is_ge)
     plane(1)
     plane(2)
     pair(1, 2)
-    pair(1, 3)
-    far(1)
+    far(1, 3)
     plane(3)
-    pair(2, 3)
-    far2(1)
+    far(2, 4)
+    far2(1, 3)
     plane(4)
-    pair(2, 4)
-    far(2)
-    plane(5)
+    pair(2, 3)
+    far2(2, 4)
+    far(3, 5)
     pair(3, 4)
-    far2(2)
+    far2(3, 5)
+    plane(5)
+    pair(4, 5)
+    pair(4, 6)
     plane(6)
-    for m in range(3, 7):
-        for j in range(m + 1, 8):
-            if (m, j) != (3, 4):
-                pair(m, j)
-    fvs = "fv0 fv1 fv2 fv3 fv4 fv5 fv6 fv7"
-    V("ts", "nf", fvs, nf, T.fv[:], 0.0, None, op_.is_equal)
-    V("scan", "psn", fvs + " one", psn, T.one[:, 0:8], T.fv[:], 0.0, op_.add, op_.subtract)
-    V("tt", "kn", "ns nf", kn, ns, nf, op_.mult)
-    V("tt", "eq", "psn c4 lrep", eq, psn.indirect(T.lrep[:]), T.c4[:], op_.is_equal)
-    V("tt", "v4", "eq kn lrep", v4, kn.indirect(T.lrep[:]), eq, op_.mult)
-    V("scan", "sc8", "v4 r8", sc8, T.r8[:], v4, 0.0, op_.mult, op_.add)
-    V("copy", "klu", "sc8", T.klu[:], T.qb[:, 71:96:8])
-    for a in range(0, 2048, 448):
-        w = min(448, 2048 - a)
-        S(Copy, "ebz", "xtz", T.ebt[:, a:a + w], T.xt[:, 64:64 + w])
-    for b in range(4):
-        S(Copy, "ebt", "hid ebz", T.ebt[:, 512 * b + b:512 * b + 512:4], T.hid[:], scale=0.5)
-    S(Relu, "lm", "lm", T.lm[:], T.lm[:])
-    for k in range(8):
-        dma("s" if k % 2 == 0 else "a", "drep", T.kru[16 * k:16 * k + 16, :], T.klu[0:128:8, :], "klu", "kru")
-    dma("s", "dkx", u8(T.pwc[:, 16 * r:16 * r + 16]), u8(T.xc[:, 0:16]), "xc", "pwo")
-    dma("s", "dkx", T.pws[:, 16 * r:16 * r + 16], T.xs[:, 0:16], "xs", "pwo")
-    V("qz", "ec es", "ebt ebz", T.ec[:], T.es[:], T.ebt[:])
-    for b in range(4):
-        mm(T["pd%d" % b][:, 0:P], T.ec[:, P * b:P * b + P], T.es[:, P * b:P * b + P], T.tbc[:], T.tbs[:], True, False, "ec es tbc tbs", "pd%d" % b)
-    S(Copy, "zbz", "xtz", T.zb[:, WCOLS:480], T.xt[:, 64:80])
-    for k in ("wno", "wns", "wnc"):
-        S(Copy, k, "one", T[k][:, P * r + 1:P * r + 1 + P], T.one[:], scale=float(P))
-    S(Copy, "wmb", "wm", T.wmb[:], T.wm[:, 0:P])
-    S(Sign, "r16b", "c16", T.r16b[:], T.c16[:, 0:P])
+    pair(4, 7)
+    pair(5, 6)
+    pair(5, 7)
+    pair(6, 7)
+    V("scan", "psn", keys("fv", 8) + " one", psn, T.one[:, 0:8], T.fv[:], 0.0, op_.add, op_.subtract)
+    V("ts", "geq", "psn kq", geq, psn, kq, None, op_.is_ge)
+    V("scan", "vv", "dn geq", vsc, dn, geq, 0.0, op_.add, op_.mult)
 
-    V("copy", "kr", "kru", T.kr[:], T.kru[:])
-    V("tt", "rwm", "idx idxs kru lm", T.rwm[:], T.idx[:].indirect(T.kru[:]), T.lm[:], op_.mult)
-    for k in range(4):
-        V("ts", "eqd%d" % k, "rwm kr trs", T.eqd[:, 64 * k:64 * k + 64], T.rwm[:], T.kr[:, k:k + 1], trs[k], op_.is_equal, op_.mult)
-    for k in range(4):
-        V("scan", "scf%d" % k, "eqd%d kr one" % k, T.scf[:, 64 * k:64 * k + 64], T.one[:, 0:64], T.eqd[:, 64 * k:64 * k + 64], T.kr[:, k:k + 1], op_.mult, op_.max)
-    V("copy", "lu", "scf0 scf1 scf2 scf3", T.lu[:], T.scf[:, 63:256:64])
-    send([(T.lu[:], [T.lr[:]] * 2, ids_r[0:2], eon, "r_kl")], "lu")
-    send([(T.lu[:], [T.ll[:, 4 * at_s[y]:4 * at_s[y] + 4]], [ids_s[y]], e_s[y], "a_kls") for y in range(3)], "lu")
+    V("ts", "off", "vv lh sk", T.off[:, 0:4:2], fc[:, 36:38], vv, tf, op_.mult, op_.max)
+    for j in (1, 0):
+        V("ts", "val%d" % j, "off m16 sk cd%d" % j, T.val[:, 16 * j:16 * j + 16], T.m16[:].indirect(T.off[:, 2 * j:2 * j + 1]), tf,
+          fc[:, 58 + j:59 + j], op_.is_equal, op_.mult)
+    for j in (1, 0):
+        V("copy", "mp", "off val%d" % j, T.mp[:].indirect(T.off[:, 2 * j:2 * j + 1]), T.val[:, 16 * j:16 * j + 16])
+    order = cross + same + [r]
 
-    S(Copy, "locr", "loc locz locy kru", T.locr[:, 0:64], T.loc[:].indirect(T.kru[:]))
-    S(Ident, "kpf", "idx idxs kru", T.kpf[:], T.idx[:].indirect(T.kru[:]), bias=-1.0)
-    dma("s", "dkp", T.kp[:], T.kpf[0:1, :], "kpf", "kp")
-    s = P * r + 1
-    V("copy", "wno", "val lu", T.wno[:].indirect(T.lu[:]), T.val[:, 64 * r:64 * r + 64])
-    V("tt", "loc2", "locr wm", T.locr[:, 64:128], T.locr[:, 0:64], T.wm[:, 0:64], op_.mult)
-    V("tt", "wsmo", "wno wmb", T.wsm[:, 3 * P:4 * P], T.wno[:, s:s + P], T.wmb[:], op_.mult)
-    V("scan", "loc3", "loc2 r16", T.locr[:, 128:192], T.r16[:, 0:64], T.locr[:, 64:128], 0.0, op_.mult, op_.add)
-    V("copy", "yl", "loc3", T.yl[:, 0:8:2], T.locr[:, 143:192:16])
-    for k in range(4):
-        S(Copy, "yb", "zb zbz yl", T.yb[:, k:64:4], T.zb[:].indirect(T.yl[:, 2 * k:2 * k + 1]))
-    dma("s", "dy", T.y[:], T.yb[:], "yb", "y")
+    def maps(h):
+        for x in range(4 * h, 4 * h + 4):
+            a = 16 + P * order[x]
+            V("scan", "msc%d" % x, "mp r16b", T.msc[:, P * x:P * x + P], T.r16b[:], T.mp[:, a:a + P], 0.0, op_.mult, op_.max)
+        V("copy", "mo%d" % h, keys("msc", 4 * h + 4, 4 * h), T.mo[:, 32 * h:32 * h + 32], T.msc[:, 512 * h + 15:512 * h + 512:16])
 
-    tot["a_kls"] = sum(len(e_s[f]) for f in from_s)
-    tot["a_klc"] = 4 * noff // 2
-    wr_["lls"] = [("a_kls", tot["a_kls"])]
-    wr_["llc"] = [("a_klc", tot["a_klc"])]
-    for q in sorted(same, reverse=True):
-        c = 4 * peers.index(q)
-        V("copy", "wns", "val lls", T.wns[:].indirect(T.ll[:, c:c + 4]), T.val[:, 64 * q:64 * q + 64])
-    V("tt", "wsm0", "wns wsmo", T.wsm[:, 0:P], T.wns[:, s:s + P], T.wsm[:, 3 * P:4 * P], op_.min)
-    for q in sorted(cross, reverse=True):
-        c = 4 * peers.index(q)
-        V("copy", "wnc", "val llc", T.wnc[:].indirect(T.ll[:, c:c + 4]), T.val[:, 64 * q:64 * q + 64])
-    V("tt", "wsm1", "wsm0 wnc", T.wsm[:, P:2 * P], T.wsm[:, 0:P], T.wnc[:, s:s + P], op_.min)
-    V("scan", "wsm2", "wsm1 r16b", T.wsm[:, 2 * P:3 * P], T.r16b[:], T.wsm[:, P:2 * P], 0.0, op_.mult, op_.add)
-    won = T.wsm[:, 2 * P + 15:3 * P:16]
-    V("ts", "wu", "wsm2", T.wu[:], won, float(P - 1), None, op_.min)
-    tot["a_pt"] = 7 * 2 * noff
-    wr_["pwa"] = [("a_pt", tot["a_pt"])]
-    S(Copy, "pps", "pwa pwo wu", T.pps[:], T.pws[:].indirect(T.wu[:]))
-    V("copy", "ppc", "pwa pwo wu", u32(T.ppc[:]), u32(T.pwc[:]).indirect(T.wu[:]))
+    maps(0)
+    send([(T.mo[:, 8 * x:8 * x + 8], [T.rm[:]], [ids_r[x]], e_q[x], "r_mp") for x in range(4)], "mo0")
+    maps(1)
+    send([(T.mo[:, 32 + 8 * y:40 + 8 * y], [T.ml[:, 32 + 8 * at_s[y]:40 + 8 * at_s[y]]], [ids_s[y]], e_s[y], "a_ms") for y in range(3)], "mo1")
+
+    V("ts", "eqv", "nr vv", T.qb[:, 0:32], T.nr[:], 16.0, vv, op_.add, op_.is_equal)
+    S(Ident, "t0a", "t0z mk4 vv", T.t0[:, 0:4], fc[:, 52:56], scale=vv)
+    V("tt", "mlo", "mo1 dfl", T.ml[:, 56:64], T.mo[:, 56:64], T.dfl[:], op_.max)
+    V("tt", "eqc", "eqv ci0 ci1", T.qb[:, 32:64], T.qb[:, 0:32], T.ci[:], op_.mult)
+    V("red", "cix", "eqc", T.qb[:, 64:65], T.qb[:, 32:64], AxisListType.X, op_.max)
+    V("ts", "t0b", "t0z mk4 cix", T.t0[:, 4:8], fc[:, 52:56], T.qb[:, 64:65], None, op_.mult)
     for b in range(4):
-        mm(T["pd%d" % b][:, 0:P], T.ec[:, P * b:P * b + P], T.es[:, P * b:P * b + P], T.ppc[:], T.pps[:], False, True, "ec es ppc pps", "pd%d" % b)
-    V("ts", "wl", "wsm2", T.wl[:], won, float(P), float(P), op_.is_lt, op_.mult)
-    V("tt", "wl", "wl sk", T.wl[:], T.wl[:], T.fc[:, 0:8], op_.add)
-    V("copy", "fl", "wl", T.fl[:], T.wl[:])
+        V("tr", "t1%d" % b, "t0a t0b", T.t1[0:32, 32 * b:32 * b + 32], T.t0[blk[b], :])
+    V("scan", "t2", keys("t1", 4) + " r8", T.t2[0:32, :], T.r8[0:32, :], T.t1[0:32, :], 0.0, op_.mult, op_.add)
+    for d in range(2):
+        V("copy", "t3%d" % d, "t2", T.t3[0:32, 16 * d:16 * d + 16], T.t2[0:32, 7:128:8])
+    S(Relu, "kp1", "t2", T.kpf[0:4, 0:16], T.t2[0:4, 7:128:8], bias=-15.0)
+    S(Ident, "kp2", "kp1", T.kpf[0:4, 16:32], T.kpf[0:4, 0:16], bias=-1.0)
+    dma("s", "dkp", T.kp[:], T.kpf[0:4, 16:32], "kp2", "kp")
+    V("tr", "t4", "t30 t31", T.t4[0:32, :], T.t3[0:32, :])
     for b in range(4):
-        o, i = T.nt[:, b:512:4], T["pd%d" % b][:, 0:P]
-        if b % 2 == 0:
-            V("copy", "nt%d" % b, "pd%d" % b, o, i)
-        else:
-            S(Copy, "nt%d" % b, "pd%d" % b, o, i)
-    V("qz", "fwn fsn", "nt0 nt1 nt2 nt3", T.fwc[:, P:2 * P], T.fws[:, P:2 * P], T.nt[:])
-    S(Copy, "fos", "fso fsn fl", T.fos[:], T.fws[:].indirect(T.fl[:]))
-    V("copy", "foc", "fwo fwn fl", u32(T.foc[:]), u32(T.fwc[:]).indirect(T.fl[:]))
-    dma("s", "doc", T.oc[:], u8(T.foc[:]), "foc", "oc")
+        V("copy", "yl%d" % b, "t4", T.yl[blk[b], 0:8:2], T.t4[0:32, 4:8])
     for k in range(4):
-        dma("a" if k < 3 else "s", "doc", T.osc[4 * k:4 * k + 4, :], T.fos[32 * k:32 * k + 4, :], "fos", "osc")
+        S(Copy, "yb%d" % k, "zb zbz " + keys("yl", 4), T.yb[:, k:64:4], T.zb[:].indirect(T.yl[:, 2 * k:2 * k + 1]))
+    dma("s", "dy", T.y[:], T.yb[:], keys("yb", 4), "y")
+
+    lands("mls", "a_ms", sum(len(e_s[f]) for f in at_s))
+    lands("mlc", "a_mc", 4 * noff)
+    V("tt", "e1", "mls mlo", T.mx[:, 0:16], T.ml[:, 32:48], T.ml[:, 48:64], op_.max)
+    V("tt", "e2", "e1", T.mx[:, 16:24], T.mx[:, 0:8], T.mx[:, 8:16], op_.max)
+    V("tt", "x1", "mlc", T.mt[:, 0:16], T.ml[:, 0:16], T.ml[:, 16:32], op_.max)
+    V("tt", "x2", "x1", T.mt[:, 16:24], T.mt[:, 0:8], T.mt[:, 8:16], op_.max)
+    V("tt", "x3", "x2 e2", T.mx[:, 24:32], T.mt[:, 16:24], T.mx[:, 16:24], op_.max)
+    VX("x4", "x3", T.mt[0:64, 24:32], T.mx[0:64, 24:32], T.mx[64:128, 24:32], op_.max)
+    VX("x5", "x4 mx0", T.mx[0:32, 32:40], T.mt[0:32, 24:32], T.mt[32:64, 24:32], op_.max)
+    V("tr", "x6", "x5", T.mt[0:32, 32:64], T.mx[0:32, 32:64])
+    for d in range(2):
+        V("tt", "x7%d" % d, "x6", T.mt[0:32, 64 + 16 * d:80 + 16 * d], T.mt[0:32, 32:48], T.mt[0:32, 48:64], op_.max)
+    V("tr", "x8", "x70 x71", T.mt[0:32, 96:128], T.mt[0:32, 64:96])
+    for b in range(4):
+        V("ts", "wu%d" % b, "x8", T.wu[blk[b], :], T.mt[0:32, 96:104], -1.0, 255.0, op_.mult, op_.add)
+    for b in range(4):
+        V("tt", "nt%d" % b, "hv%d hp%d ho%d " % (b, b, b) + keys("wu", 4), T.nt[:, b:512:4], H[b][:, P:3 * P].indirect(T.wu[:]), H[b][:, 0:P], op_.add)
+    V("qz", "fo", keys("nt", 4), T.foc[:], T.fos[:], T.nt[:])
+    dma("s", "doc", T.oc[:], u8(T.foc[:]), "fo", "oc")
+    for k in range(4):
+        dma("a" if k < 3 else "s", "doc", T.osc[4 * k:4 * k + 4, :], T.fos[32 * k:32 * k + 4, :], "fo", "osc")
     need("g", [(x, tot[x]) for x in tot])

@@ -17,30 +17,32 @@ for _n, _w, _d in [
     ("cdu", 32, U16), ("fla", 1792, BF), ("flb", 1792, BF), ("mrg", 256, BF), ("nam", 256, BF), ("one", 128, BF),
     ("inc", 256, BF), ("le", 384, BF), ("cs", 384, BF), ("rs", 384, BF), ("sgo", 384, BF), ("sga", 4, F32),
     ("rq", 6, U16), ("rql", 18, U16),
-    ("tw", 2 * P, X4), ("tws", 2 * P, U8), ("idl", 10, U16), ("wc", WCOLS, X4), ("ws", WCOLS, U8),
+    ("tw", 2 * P, X4), ("tws", 2 * P, U8), ("wc", WCOLS, X4), ("ws", WCOLS, U8),
     ("xc", 128, X4), ("xs", 128, U8), ("wqc", 128, X4), ("wqs", 128, U8), ("pwc", 128, X4), ("pws", 128, U8),
-    ("xrc", 256, X4), ("xrs", 256, U8), ("dc", 3 * RUN, X4), ("ds", 3 * RUN, U8), ("rlc", LC, X4), ("rls", P, U8),
-    ("rpc", 16, X4), ("rps", 64, U8), ("kc", 288, X4), ("ks", 288, U8),
+    ("xrc", 3 * RUN, X4), ("xrs", 4 * RUN, U8), ("dc", 3 * RUN, X4), ("ds", 3 * RUN, U8), ("rlc", LC, X4), ("rls", P, U8),
+    ("rdc", RUN, X4), ("rds", 4 * RUN, U8), ("rpc", 16, X4), ("rps", 64, U8), ("kc", 288, X4), ("ks", 288, U8),
     ("foc", 128, X4), ("fos", 128, U8), ("ez", 516, BF), ("ec", 512, X4), ("es", 512, U8),
-    ("ii", 8, I32), ("fc", 64, F32), ("cj", 64, F32), ("idx", 1024, F32), ("c16", 256, F32), ("wm", 256, F32),
-    ("r16", 256, F32), ("r16b", 128, BF), ("r17", 34, F32), ("c8", 128, F32), ("r8", 128, F32), ("m16", 1040, BF),
-    ("zt", 512, F32), ("nrz", 32, F32), ("lgs", 6, U16), ("xl", 16, U16), ("ci", 32, F32), ("dfl", 8, BF),
+    ("ii", 16, I32), ("fc", 80, F32), ("idx", 1024, F32), ("c16", 256, F32), ("wm", 256, F32),
+    ("r16", 256, F32), ("r16b", 128, BF), ("m16", 1040, BF), ("nrz", 32, F32), ("lf", 32, F32), ("ul", 32, U16),
+    ("ci", 32, F32), ("dfl", 8, BF), ("pw", 64, F32),
+    ("t1", 258, F32), ("t2", 852, BF), ("hh", 64, F32), ("ar", 272, BF), ("cr", 272, BF), ("sg", 656, BF), ("r3", 576, BF),
+    ("r5", 80, BF), ("mk", 64, F32),
     ("loc", 264, F32), ("cdk", 16, U16), ("posm", 256, F32), ("posc", 256, F32), ("psa", 32, F32), ("kpl", 16, U16),
     ("cpu", 2, U16), ("nr", 32, F32), ("lw", 32, F32),
-    ("pb", 288, F32), ("pbx", 256, F32), ("gs", 32, F32), ("qa", 128, F32), ("rku", 2, U16), ("ge2", 32, F32),
-    ("bsw", 40, F32), ("pk", 34, F32), ("pku", 2, U16), ("own", 32, F32), ("msw", 40, I32), ("ms", 8, I32), ("nsw", 40, F32),
-    ("ui", 56, I32), ("fv", 8, F32), ("pn", 80, F32),
+    ("pb", 288, F32), ("pbx", 256, F32), ("gs", 32, F32), ("qa", 224, F32), ("rku", 2, U16), ("ge2", 32, F32),
+    ("bsw", 32, F32), ("pk", 32, F32), ("pku", 2, U16), ("own", 64, F32), ("cl", 4, U16), ("o2", 64, F32), ("nsw", 32, F32),
+    ("pn", 64, F32),
     ("off", 4, U16), ("val", 32, BF), ("mp", 1040, BF), ("msc", 1024, BF), ("mo", 64, BF), ("rm", 8, BF), ("ml", 64, BF),
     ("mx", 64, BF), ("mt", 128, BF), ("wu", 8, U16),
-    ("qb", 72, F32), ("t0", 32, F32), ("t1", 128, F32), ("t2", 128, F32), ("t3", 32, F32), ("t4", 32, F32), ("kpf", 32, F32),
-    ("yl", 8, U16), ("zb", 272, F32), ("yb", 64, F32),
-    ("h0", 384, F32), ("h1", 384, F32), ("h2", 384, F32), ("h3", 384, F32), ("nt", 512, BF),
+    ("qb", 72, F32), ("cu", 2, U16), ("kpf", 2, F32), ("yl", 16, U16), ("zb", 272, F32), ("yb", 64, F32),
+    ("h0", 384, F32), ("h1", 384, F32), ("h2", 384, F32), ("h3", 384, F32), ("gh", 256, F32), ("nt", 512, BF),
 ]:
     _sb(_n, _w, _d)
 for _n in ("pg0", "pg1", "pd0", "pd1", "pz", "ph0", "ph1", "ph2"):
     SCRATCH[_n] = ("psum", [128, 512], F32)
-SEMAPHORES = ["cv", "ca", "ct", "cg", "dcd", "dcp", "dtb", "dx", "dw", "dy", "dkp", "doc", "ls",
-              "a_tb", "a_rq", "a_dt", "a_pt", "a_mc", "a_ms", "r_pt", "r_tb", "r_mp"]
+SCRATCH["dl"] = ("dram", [16, 16], U16)
+SEMAPHORES = ["cv", "ca", "ct", "cg", "dcd", "dcp", "dtb", "dx", "dw", "dy", "dkp", "doc", "dl1", "dl2", "ls",
+              "a_tb", "a_rq", "a_dt", "a_pt", "a_mc", "a_ms", "r_pt", "r_tb", "r_dt", "r_mp"]
 
 
 def _bits(es):
@@ -52,7 +54,7 @@ def _bits(es):
 
 def _peers(topo, cores, r):
     cross = [q for q in range(N) if q != r and not topo.may_write(cores[r], cores[q])]
-    same = [q for q in range(N) if q != r and topo.may_write(cores[r], cores[q])]
+    same = [q % N for q in range(r + 1, r + N) if topo.may_write(cores[r], cores[q % N])]
     assert sorted(q // 2 for q in same + [r]) == list(range(N // 2))
     return cross, same
 
@@ -70,10 +72,6 @@ def _dst(topo, d, s):
     return DstId(rid=rid, pnc=pid)
 
 
-def _same_engines(es):
-    return [es[0:4], es[4:6], es[6:8]], [es[0:2], es[2:4], es[4:8]]
-
-
 def _relay_program(g, core, T, topo, cores, r, x):
     cross, same = _peers(topo, cores, r)
     to = cross + same
@@ -86,8 +84,9 @@ def _relay_program(g, core, T, topo, cores, r, x):
         n[0] += len(es)
 
     non = len(topo.engines(cores[r], core))
-    a, o = A * r, P * (r % 2)
+    a, o, w0 = A * r, P * (r % 2), 2 * P + RUN * (r // 2)
     pts = [(T.rpc[:].bitcast(dt.uint8), T.pwc[:, a:a + A].bitcast(dt.uint8)), (T.rps[:, 0:A], T.pws[:, a:a + A])]
+    run = [(T.rds[:, 3 * RUN:4 * RUN], T.ws[:, w0:w0 + RUN]), (T.rdc[:].bitcast(dt.uint8), T.wc[:, w0:w0 + RUN].bitcast(dt.uint8))]
     if x < 2:
         g.wait_ge(T.sem.r_pt, non // 2)
         fwd(pts[x][0], pts[x][1], to[0:1], "a_pt")
@@ -99,6 +98,9 @@ def _relay_program(g, core, T, topo, cores, r, x):
         fwd(T.rls[:, 0:P], T.tws[:, o:o + P], [r ^ 1], "a_tb")
     if x < 2:
         fwd(pts[x][0], pts[x][1], to[1:], "a_pt")
+    else:
+        g.wait_ge(T.sem.r_dt, non // 2)
+        fwd(run[x - 2][0], run[x - 2][1], same[0:1], "a_dt")
     at = _peers(topo, cores, cross[x])[0].index(r)
     g.wait_ge(T.sem.r_mp, non // 4)
     fwd(T.rm[:], T.ml[:, 8 * at:8 * at + 8], [cross[x]], "a_mc")
@@ -218,20 +220,23 @@ def rank_program(g, core, T, topo):
     noff = len(eoff)
     e_h = [eon[0:len(eon) // 2], eon[len(eon) // 2:]]
     e_q = [eon[len(eon) // 4 * k:len(eon) // 4 * (k + 1)] for k in range(4)]
-    e_s, e_s2 = _same_engines(eoff)
+    e_s = [eoff[0:noff // 2], eoff[noff // 2:3 * noff // 4], eoff[3 * noff // 4:]]
+    e_d = [None, eoff[0:noff // 2], eoff[noff // 2:]]
     at_s = [_peers(topo, cores, q)[1].index(r) for q in same]
     o, op = P * (r % 2), P * (1 - r % 2)
 
-    pin, ti, o7 = [T.ii[:, 2 * k:2 * k + 2] for k in range(3)]
+    pin, ti = T.ii[:, 0:2], T.ii[:, 2:4]
     fc = T.fc
     tf = fc[:, 0:1]
     sk = [fc[:, k:k + 1] for k in range(8)]
     pf2, n8, n8b = fc[:, 30:31], fc[:, 32:33], fc[:, 33:34]
     lo, hi = fc[:, 36:37], fc[:, 37:38]
     k7, kq, gb = fc[:, 48:49], fc[:, 50:51], fc[:, 51:52]
-    c17, xlf = T.cj[:, 0:34], T.cj[:, 40:56]
-    eqt, gt, el = [T.qa[:, 32 * k:32 * k + 32] for k in range(3)]
-    psn, geq, vsc, dn = [T.pn[:, 8 * k:8 * k + 8] for k in range(4)]
+    g2 = T.lf[:, 20:21]
+    xl, lg, idl, id0 = T.ul[:, 0:18], [T.ul[:, 18 + 2 * k:20 + 2 * k] for k in range(3)], T.ul[:, 24:32], T.ul[:, 16:17]
+    zero, hg = T.tbx[:, 576:1024], T.hh[:, 32:64]
+    eqt, gt, el, _, ga, gc_, gd = [T.qa[:, 32 * k:32 * k + 32] for k in range(7)]
+    geq, vsc, dn, thr = T.pn[:, 8:16], T.pn[:, 16:24], T.pn[:, 24:32], T.pn[:, 48:56]
     vv = T.pn[:, 23:24]
     H = [T["h%d" % b] for b in range(4)]
 
@@ -247,41 +252,29 @@ def rank_program(g, core, T, topo):
     iota(fc[:, 8:16], "k16", [[16, 8]])
     iota(T.c16[:], "c16", [[0, 16], [1, 16]])
     iota(pf2, "pf2", [[0, 1]], 0, 1)
-    iota(c17, "c17", [[0, 2], [1, 17]])
 
-    V("set", "xtz", "", T.tbx[:, 576:1024], 0.0)
+    V("set", "xtz", "", zero, 0.0)
     V("set", "one", "", T.one[:], 1.0)
     V("ts", "ti", "pin", ti, pin, 15, None, op_.bitwise_and)
     V("set", "fla", "", T.fla[:, 768:1024], -200.0)
     V("copy", "tf", "ti", fc[:, 34:36], ti)
     V("set", "flb", "", T.flb[:, 768:1024], 0.0)
     V("ts", "sk", "k16 tf", fc[:, 0:8], fc[:, 8:16], fc[:, 34:35], None, op_.add)
-    V("ts", "bi", "pin", T.ii[:, 6:8], pin, 5, None, op_.logical_shift_right)
-    V("set", "ez", "", T.ez[:], 0.5)
-    V("copy", "bf", "bi", fc[:, 60:62], T.ii[:, 6:8])
+    V("ts", "tb4", "pin", T.ii[:, 12:13], T.ii[:, 0:1], 5, None, op_.logical_shift_right)
+    for m in range(4):
+        V("ts", "tb%d" % m, "pin", T.ii[:, 8 + m:9 + m], T.ii[:, 0:1], m, 1, op_.logical_shift_right, op_.bitwise_and)
     for k in range(3):
         S(Copy, "rs%d" % k, "one", T.rs[:, P * k:P * k + P], T.one[:])
-    S(Copy, "rs", "rs0 rs1 rs2 xtz", T.rs[:, 0:384:128], T.tbx[:, 576:579])
+    S(Copy, "rs", "rs0 rs1 rs2 xtz", T.rs[:, 0:384:128], zero[:, 0:3])
     S(Ident, "half", "sk", fc[:, 44:47], fc[:, 0:3], bias=0.5)
     S(Copy, "n8", "sk", n8, tf, scale=-0.125)
     S(Copy, "lhc", "sk", fc[:, 39:40], tf, scale=-1.0)
     S(Abs, "wm", "c16 sk", T.wm[:], T.c16[:], bias=tf, scale=-1.0)
     S(Ident, "n8b", "n8", n8b, n8, bias=273.0)
     S(Ident, "lo", "lhc", lo, fc[:, 39:40], bias=7.5)
-    S(Ident, "lg2", "pf2 n8", fc[:, 26:27], pf2, bias=n8, scale=0.125)
+    S(Ident, "lg2", "pf2 n8", g2, pf2, bias=n8, scale=0.125)
     S(Relu, "wm", "wm", T.wm[:], T.wm[:], bias=1.0, scale=-1.0)
     S(Ident, "hi", "sk", hi, tf, bias=-7.5)
-    S(Copy, "bsw", "c16", T.bsw[:, 0:34:17], T.c16[:, 0:2])
-    S(Copy, "fv0", "c16", T.fv[:, 0:1], T.c16[:, 0:1])
-    S(Sign, "lh", "lo hi", fc[:, 36:38], fc[:, 36:38])
-    S(Sign, "r17", "c17", T.r17[:], c17)
-    S(Relu, "lh", "lh", fc[:, 36:38], fc[:, 36:38])
-    S(Copy, "r17", "r17", T.r17[:], T.r17[:], scale=2.0)
-    S(Copy, "lh16", "lh", fc[:, 56:58], fc[:, 36:38], scale=16.0)
-    S(Ident, "lg3", "pf2 n8b", fc[:, 27:28], pf2, bias=n8b, scale=0.125)
-    for h in range(2):
-        S(Ident, "lb%d" % h, "bf", fc[:, 42 + h:43 + h], fc[:, 60:61], bias=float(2 * P + LC * h - 1), scale=float(RUN))
-    S(Sign, "r16", "c16", T.r16[:], T.c16[:])
 
     V("qz", "xc xs", "xt xtz", T.xc[:], T.xs[:], T.tbx[:, 512:1024])
     send([(u8(T.xc[:, 0:16]), [u8(T.rpc[:])], ids_r[0:1], e_h[0], "r_pt"),
@@ -289,6 +282,7 @@ def rank_program(g, core, T, topo):
 
     for b in range(4):
         V("ts", "cdu%d" % b, "cdi", T.cdu[blk[b], 0:32:2], T.cdi[0:32, :], float(768 - 256 * b), None, op_.add)
+    V("copy", "tm", keys("tb", 5), fc[:, 64:69], T.ii[:, 8:13])
     for i in range(A):
         f = "flb" if i % 2 else "fla"
         V("copy", f, keys("cdu", 4) + " one", T[f][:].indirect(T.cdu[:, 2 * i:2 * i + 1]), T.one[:, 0:16])
@@ -298,38 +292,76 @@ def rank_program(g, core, T, topo):
           (T.tws[:, o:o + P], [T.rls[:]], [ids_r[3]], e_h[1], "r_tb")], "two")
     send([(u8(T.tw[:, o + LC * x:o + LC * x + LC]), [u8(T.rlc[:])], [ids_r[x]], e_h[x], "r_tb") for x in range(2)], "two")
     iota(T.idx[:, 0:256], "idx", [[1, 256]])
+    iota(T.lf[:, 0:16], "xlf", [[1, 2], [2, 8]])
+    iota(T.lf[:, 18:20], "lg0", [[128, 2]], 16, 1)
+    iota(T.lf[:, 22:24], "lg4", [[128, 2]], 0, 1)
+
+    def hh(m):
+        S(Ident, "hh", "hh tm", T.hh[:, 2 ** m:2 ** (m + 1)], T.hh[:, 0:2 ** m], bias=fc[:, 63 + m:64 + m])
+
+    def ar(x0, x1):
+        runs = [(0, 0, 64, 2), (1, 0, 64, 8), (1, 1, 64, 8), (1, 3, 64, 8), (2, 0, 8, 1), (2, 9, 16, 2), (2, 18, 19, 1), (2, 20, 24, 1), (2, 29, 32, 2)]
+        for x in range(x0, x1):
+            i, a, e, st = runs[x]
+            S(Copy, "ar%d" % (x + 1), "arz one", T.ar[:, 3 * a + i:3 * e:3 * st], T.one[:, 0:len(range(a, e, st))])
+
+    S(Copy, "hh", "c16", T.hh[:, 0:2], T.c16[:, 0:2])
+    S(Sign, "lh", "lo hi", fc[:, 36:38], fc[:, 36:38])
+    hh(1)
+    S(Relu, "lh", "lh", fc[:, 36:38], fc[:, 36:38])
+    hh(2)
+    S(Ident, "lg3", "pf2 n8b", T.lf[:, 21:22], pf2, bias=n8b, scale=0.125)
+    hh(3)
+    S(Ident, "k7", "lh sk", k7, hi, bias=tf, scale=-8.0)
+    hh(4)
+    for h in range(2):
+        S(Ident, "lb%d" % h, "tm", fc[:, 42 + h:43 + h], fc[:, 68:69], bias=float(2 * P + LC * h - 1), scale=float(RUN))
+    S(Sign, "hg", "hh", hg, T.hh[:, 0:32])
+    S(Relu, "kq0", "k7", fc[:, 49:50], k7, bias=-3.0)
+    S(Ident, "idl", "sk", T.lf[:, 24:32], fc[:, 0:8], bias=float(op))
+    S(Copy, "id0", "sk", T.lf[:, 16:18], fc[:, 0:2])
+    S(Copy, "locz", "xtz", T.loc[:, 0:258:257], zero[:, 0:2])
+    S(Copy, "tn", "tm", fc[:, 70:74], fc[:, 64:68], scale=-4096.0)
+    S(Copy, "arz", "xtz", T.ar[:, 0:192], zero[:, 0:192])
+    S(Copy, "ar0", "one", T.ar[:, 192:272:5], T.one[:, 0:16])
+
+    def cdk(k):
+        V("ts", "cdk%d" % k, keys("cdu", 4), T.cdk[:, 8 * k:8 * k + 8], T.cdu[:, 2 * k:32:4], -767.0, 257.0, op_.add, op_.min)
+
     V("scan", "mrg", "fla flb", T.mrg[:], T.fla[:, 768:1024], T.flb[:, 768:1024], 0.0, op_.add, op_.max)
+    cdk(0)
     V("ts", "nam", "mrg", T.nam[:], T.mrg[:], 0.5, None, op_.is_ge)
+    cdk(1)
     V("scan", "inc", "nam rs", T.inc[:], T.rs[:, 0:256], T.nam[:], 0.0, op_.mult, op_.add)
+    V("copy", "cpu", "cpi", T.cpu[:], T.cpi[:])
     for k in range(3):
         S(Sign, "sg%d" % k, "inc half", T.sgo[:, P * k:P * k + P - 1], T.inc[:, P:2 * P - 1],
           bias=fc[:, 44 + k:45 + k], scale=-1.0, accum_out=T.sga[:, k:k + 1])
     for k in range(3):
         V("ts", "le%d" % k, "inc sk", T.le[:, P * k:P * k + P], T.inc[:, 0:P], sk[k], None, op_.is_le)
+    V("ts", "cpf", "cpi", fc[:, 20:22], T.cpi[:], 0.5, None, op_.add)
     V("scan", "cs", "rs le0 le1 le2", T.cs[:], T.rs[:], T.le[:], 0.0, op_.mult, op_.add)
     V("ts", "rq1", "sg0 sg1 sg2", T.rq[:, 3:6], T.sga[:, 0:3], 0.5, 0.5 * (P - 1) + P, op_.mult, op_.add)
     V("copy", "rq0", "cs", T.rq[:, 0:3], T.cs[:, P - 2:384:P])
     send([(T.rq[:], [T.rql[:, 6 * a:6 * a + 6] for a in at_s], ids_s, eoff, "a_rq")], "rq0 rq1")
-    iota(xlf, "xlf", [[1, 2], [2, 8]])
-    iota(fc[:, 24:26], "lg0", [[128, 2]], 16, 1)
-    iota(fc[:, 28:30], "lg4", [[128, 2]], 0, 1)
-    do("g", lambda q: q.affine_select(T.ez[:], T.ez[:], [[-1, 516]], op_.is_equal, 0.0, 3, 4), ["ez"], ["ez"])
+    for m in range(4):
+        iota(T.ar[:, 193 + m:272:5], "ab%d" % m, [[0, 8 >> m], [1, 2], [0, 1 << m]])
+    iota(T.r5[:], "r5", [[0, 16], [16, 5]])
+    iota(T.pw[:, 32:64], "w2", [[254, 2], [0, 16]], 2)
 
-    for k in range(2):
-        V("ts", "cdk%d" % k, keys("cdu", 4), T.cdk[:, 8 * k:8 * k + 8], T.cdu[:, 2 * k:32:4], -767.0, 257.0, op_.add, op_.min)
-    V("set", "locz", "", T.loc[:, 0:258:257], 0.0)
-    V("qz", "wco", "tbt", T.wc[:, o:o + P], T.ws[:, o:o + P], T.tbx[:, 0:512])
-    V("ts", "idl", "sk", T.idl[:, 0:8], fc[:, 0:8], float(op), None, op_.add)
-    V("copy", "idx8", "sk", T.idl[:, 8:10], fc[:, 0:2])
-    V("qz", "kcx", "xt xtz", T.kc[:, 0:P], T.ks[:, 0:P], T.tbx[:, 512:1024])
-    V("qz", "kcy", "xt tbt", T.kc[:, 160:288], T.ks[:, 160:288], T.tbx[:, 64:576])
-    V("ts", "o7", "pin", o7, pin, 7, None, op_.bitwise_and)
-    V("copy", "cpf", "cpi", fc[:, 20:22], T.cpi[:])
-    V("copy", "cpu", "cpi", T.cpu[:], T.cpi[:])
-    V("copy", "k7", "o7", fc[:, 48:50], o7)
     for h in range(2):
         S(Ident, "loc%d" % h, "inc lb%d" % h, T.loc[:, 1 + P * h:1 + P * h + P], T.inc[:, P * h:P * h + P], bias=fc[:, 42 + h:43 + h])
     S(Copy, "loc", "loc0 loc1 idx", T.loc[blk[B], 1:257], T.idx[blk[B], 0:256])
+    V("copy", "ul", "xlf lg0 lg2 lg3 lg4 idl id0", T.ul[:], T.lf[:])
+    V("qz", "wqc wqs", "wt", T.wqc[:], T.wqs[:], T.wt[:])
+    V("copy", "xrc", "xc ul", u32(T.xrc[:]), u32(T.xc[:]).indirect(xl))
+    V("tt", "posm", "loc locz cdk0 cdk1 wm", T.posm[:], T.loc[:, 0:258].indirect(T.cdk[:]), T.wm[:], op_.mult)
+    V("set", "ez", "", T.ez[:], 0.5)
+    S(Copy, "xrs", "xs ul", T.xrs[:, 0:3 * RUN], T.xs[:].indirect(xl))
+    S(Sign, "r16", "c16", T.r16[:], T.c16[:])
+    S(Ident, "kq", "kq0 k7", kq, fc[:, 49:50], bias=k7, scale=100.0)
+    ar(0, 5)
+    S(Ident, "th", "kq c16", fc[:, 74:78], T.c16[:, 0:4], bias=kq, scale=-1.0)
 
     lands("twp", "a_tb", 4 * noff)
     lands("rqa", "a_rq", 3 * noff)
@@ -337,52 +369,58 @@ def rank_program(g, core, T, topo):
         if b != B:
             V("copy", "rql%d" % b, "rqa", T.rql[blk[b], :], T.rql[blk[B], :])
     wr_["rql%d" % B] = wr_["rqa"]
-    S(Copy, "ds", "two twp " + keys("rql", 4), T.ds[:], T.tws[:].indirect(T.rql[:]))
-    V("copy", "dc", "two twp " + keys("rql", 4), u32(T.dc[:]), u32(T.tw[:]).indirect(T.rql[:]))
+    rd = "two twp " + keys("rql", 4)
+    S(Copy, "ds0", rd, T.xrs[:, 3 * RUN:4 * RUN], T.tws[:].indirect(T.rql[:, 0:6]))
+    V("copy", "dc0", rd, u32(T.dc[:, 0:RUN]), u32(T.tw[:]).indirect(T.rql[:, 0:6]))
+    S(Copy, "ds", rd, T.ds[:, RUN:3 * RUN], T.tws[:].indirect(T.rql[:, 6:18]))
+    V("copy", "dc", rd, u32(T.dc[:, RUN:3 * RUN]), u32(T.tw[:]).indirect(T.rql[:, 6:18]))
     w0 = 2 * P + RUN * B
-    send([(u8(T.dc[:, RUN * y:RUN * y + RUN]), [u8(T.wc[:, w0:w0 + RUN])], [ids_s[y]], e_s[y], "a_dt") for y in range(3)], "dc")
-    send([(T.ds[:, RUN * y:RUN * y + RUN], [T.ws[:, w0:w0 + RUN]], [ids_s[y]], e_s2[y], "a_dt") for y in range(3)], "ds")
-    iota(T.c8[:], "c8", [[0, 16], [1, 8]])
+    send([(u8(T.dc[:, 0:RUN]), [u8(T.rdc[:])], [ids_r[3]], e_h[1], "r_dt"), (T.xrs[:], [T.rds[:]], [ids_r[2]], e_h[0], "r_dt")], "dc0 ds0 xrs")
+    send([(u8(T.dc[:, RUN * y:RUN * y + RUN]), [u8(T.wc[:, w0:w0 + RUN])], [ids_s[y]], e_d[y], "a_dt") for y in (1, 2)], "dc")
+    send([(T.ds[:, RUN * y:RUN * y + RUN], [T.ws[:, w0:w0 + RUN]], [ids_s[y]], e_d[y], "a_dt") for y in (1, 2)], "ds")
+    iota(T.idx[:, 256:1024], "idy", [[1, 768]], 256)
     iota(T.m16[:], "m16", [[0, 65], [1, 16]])
+    iota(T.mp[:], "mp", [[0, 1040]])
+    do("g", lambda q: q.affine_select(T.ez[:], T.ez[:], [[-1, 516]], op_.is_equal, 0.0, 3, 4), ["ez"], ["ez"])
 
-    S(Copy, "wsp", "two twp idl", T.ws[:, op:op + P], T.tws[:].indirect(T.idl[:, 0:8]))
-    for k in range(1, 4):
-        S(Ident, "idx%d" % k, "idx", T.idx[:, 256 * k:256 * k + 256], T.idx[:, 0:256], bias=float(256 * k))
-    V("tt", "posm", "loc locz cdk0 cdk1 wm", T.posm[:], T.loc[:, 0:258].indirect(T.cdk[:]), T.wm[:], op_.mult)
-    V("copy", "xl", "xlf", T.xl[:], xlf)
+    ar(5, 9)
+    S(Copy, "wsp", "two twp ul", T.ws[:, op:op + P], T.tws[:].indirect(idl))
+    S(Relu, "cls", "hh", fc[:, 78:79], T.hh[:, 30:31], bias=3.0, scale=-1.0)
+    S(Copy, "t1z", "xtz", T.t1[:, 0:257:256], zero[:, 0:2])
+    for m in range(1, 5):
+        S(Abs, "t1%d" % m, "hg tn", T.t1[:, 2 ** m:2 ** (m + 1)], hg[:, 0:2 ** m], bias=fc[:, 69 + m:70 + m], scale=4096.0)
+    S(Ident, "t10", "cls", T.t1[:, 1:2], fc[:, 78:79], bias=83.0 + 3 * 192, scale=-192.0)
+    S(Copy, "t15", "hg", T.t1[:, 32:64], hg, scale=3.0)
+    for h in range(2):
+        S(Ident, "t16%d" % h, "hg", T.t1[:, 64 + 32 * h:96 + 32 * h], hg, bias=6.0 * h, scale=12.0)
+    for h in range(4):
+        S(Ident, "t17%d" % h, "hg", T.t1[:, P + 32 * h:P + 32 + 32 * h], hg, bias=24.0 * h, scale=96.0)
     V("scan", "posc", "posm r16", T.posc[:], T.r16[:], T.posm[:], 0.0, op_.mult, op_.add)
-    V("copy", "lgs", "lg0 lg2 lg3 lg4", T.lgs[:], fc[:, 24:30])
+    V("set", "r3a", "", T.r3[:], 1.0)
     VX("psa", "posc", T.psa[0:64, 0:16], T.posc[0:64, 15:256:16], T.posc[64:128, 15:256:16], op_.add)
     VX("psb", "psa", T.psa[0:32, 16:32], T.psa[0:32, 0:16], T.psa[32:64, 0:16], op_.add)
     for b in range(4):
-        V("qz", "ec%d" % b, "ez", T.ec[:, P * b:P * b + P], T.es[:, P * b:P * b + P], T.ez[:, 3 - b:515 - b])
-    for b in range(4):
         V("copy", "kpl%d" % b, "psb", T.kpl[blk[b], :], T.psa[0:32, 16:32])
-    pb_ = ["pg0", "pg1", "pd0", "pd1"]
-    for b in range(4):
-        mm(T[pb_[b]][:, 0:P], T.ec[:, P * b:P * b + P], T.es[:, P * b:P * b + P], T.wc[:, o:o + P], T.ws[:, o:o + P], "ec%d wco" % b, pb_[b])
-    for b in range(4):
-        V("tt", "ho%d" % b, "tbt " + pb_[b], H[b][:, 256:384], T.tbx[:, b:512:4], T[pb_[b]][:, 0:P], op_.subtract)
-    V("copy", "wcp", "two twp idl", u32(T.wc[:, op:op + P]), u32(T.tw[:]).indirect(T.idl[:, 0:8]))
-    V("copy", "nr", "idx idx1 idx2 idx3 cpu", T.nr[:], T.idx[:].indirect(T.cpu[:]))
-    S(Copy, "xrs", "xs xl", T.xrs[:], T.xs[:].indirect(T.xl[:]))
-    V("copy", "xrc", "xc xl", u32(T.xrc[:]), u32(T.xc[:]).indirect(T.xl[:]))
-    for b in range(4):
-        S(Copy, "hv%d" % b, "ho%d " % b + pb_[b], H[b][:, 0:P], T[pb_[b]][:, 0:P])
+    V("set", "r3", "r3a", T.r3[:, 0:576:3], 0.0)
+    V("qz", "wco", "tbt", T.wc[:, o:o + P], T.ws[:, o:o + P], T.tbx[:, 0:512])
+    V("qz", "kcx", "xt xtz", T.kc[:, 0:P], T.ks[:, 0:P], T.tbx[:, 512:1024])
+    V("qz", "kcy", "xt tbt", T.kc[:, 160:288], T.ks[:, 160:288], T.tbx[:, 64:576])
+    V("scan", "cr0", "r3 " + keys("ar", 10, 1), T.cr[:, 0:192], T.r3[:, 0:192], T.ar[:, 0:192], 0.0, op_.mult, op_.add)
+    V("scan", "cr1", "r5 ar0 " + keys("ab", 4), T.cr[:, 192:272], T.r5[:], T.ar[:, 192:272], 0.0, op_.min, op_.add)
+    V("copy", "wcp", "two twp ul", u32(T.wc[:, op:op + P]), u32(T.tw[:]).indirect(idl))
+    for n in range(1, 4):
+        V("ts", "sg%dx" % n, "cr0 th", T.sg[:, 192 * n - 112:192 * n + 80], T.cr[:, 0:192], fc[:, 74 + n:75 + n], None, op_.is_gt)
+    V("ts", "sg0x", "cr1 th", T.sg[:, 0:80], T.cr[:, 192:272], fc[:, 74:75], None, op_.is_gt)
+    V("scan", "pw0", "w2", T.pw[:, 0:16], T.pw[:, 32:48], T.pw[:, 48:64], 0.5, op_.mult, op_.min)
+    V("scan", "t2g", "r3 sg1x sg2x sg3x", T.t2[:, 81:657], T.r3[:], T.sg[:, 80:656], 0.0, op_.mult, op_.add)
+    S(Copy, "nr", "idx idy cpu", T.nr[:], T.idx[:].indirect(T.cpu[:]))
+    S(Copy, "lh16", "lh", fc[:, 56:58], fc[:, 36:38], scale=16.0)
     for j in range(2):
-        V("ts", "lw%d" % j, "nr cpf", T.lw[:, 16 * j:16 * j + 16], T.nr[:, 16 * j:16 * j + 16], fc[:, 20 + j:21 + j], None, op_.is_lt)
-    V("qz", "wqc wqs", "wt", T.wqc[:], T.wqs[:], T.wt[:])
-    V("copy", "pwo", "xc idx8", u32(T.pwc[:, A * r:A * r + A]), u32(T.xc[:]).indirect(T.idl[:, 8:9]))
-    V("ts", "kq0", "k7", kq, k7, 3.5, 100.0, op_.is_ge, op_.mult)
-    V("ts", "mk4", "k7 c16", fc[:, 52:56], T.c16[:, 0:4], k7, None, op_.is_equal)
-    V("ts", "kq", "kq0 k7", kq, kq, k7, 1.0, op_.add, op_.add)
-    V("set", "nsz", "", T.pn[:, 40:41], 0.0)
-    S(Ident, "zt1", "idx lh", T.zt[:, 0:256], T.idx[:, 0:256], scale=lo)
-    S(Ident, "zt2", "idx lh", T.zt[:, 256:512], T.idx[:, 0:256], scale=hi)
-    S(Copy, "pso", "xs idx8", T.pws[:, A * r:A * r + A], T.xs[:].indirect(T.idl[:, 8:9]))
-    V("set", "mp", "", T.mp[:], 0.0)
+        S(Sign, "lw%d" % j, "nr cpf", T.lw[:, 16 * j:16 * j + 16], T.nr[:, 16 * j:16 * j + 16], bias=fc[:, 20 + j:21 + j], scale=-1.0)
+    S(Copy, "pw1", "pw0", T.pw[:, 16:32], T.pw[:, 0:16])
+    S(Relu, "lw", "lw0 lw1", T.lw[:], T.lw[:])
 
-    lands("wca", "a_dt", sum(len(e_s[f]) + len(e_s2[f]) for f in at_s))
+    lands("wca", "a_dt", sum(noff * (1 if f else 2) for f in at_s))
     for j in range(2):
         a = 16 + P * j
         rd = "wco wcp wsp wca kcx kcy " + keys("kpl", 4)
@@ -394,96 +432,71 @@ def rank_program(g, core, T, topo):
         mm(T["pd%d" % j][:, 0:P], T.xrc[:, P * j:P * j + P], T.xrs[:, P * j:P * j + P], T.kc[:, a:a + P], T.ks[:, a:a + P],
            "kc%d ks%d xrc xrs" % (j, j), "pd%d" % j)
     mm(T.pz[:, 0:256], T.wqc[:], T.wqs[:], T.kc[:, 16:272], T.ks[:, 16:272], "wqc wqs kc0 ks0 kc1 ks1", "pz")
-    lands("pwa", "a_pt", 7 * 2 * noff)
-    ph_ = ["ph0", "ph1", "ph2", "pd0"]
-    for b in range(3):
-        mm(T[ph_[b]][:, 0:P], T.ec[:, P * b:P * b + P], T.es[:, P * b:P * b + P], T.pwc[:], T.pws[:], "ec%d pwa pwo pso" % b, ph_[b])
-    V("set", "mx0", "", T.mx[0:32, 32:64], 0.0)
-    V("set", "t0z", "", T.t0[:], 0.0)
+    V("scan", "t2f", "r5 sg0x", T.t2[:, 1:81], T.r5[:], T.sg[:, 0:80], 0.0, op_.min, op_.add)
     V("copy", "pb0", "pg0", T.pb[:, 0:144], T.pg0[:, 0:144])
+    S(Copy, "nsz", "xtz", T.pn[:, 40:41], zero[:, 0:1])
     S(Copy, "pb1", "pg1", T.pb[:, 144:288], T.pg1[:, 0:144])
     V("copy", "pbx0", "pd0", T.pbx[:, 0:P], T.pd0[:, 0:P])
     S(Copy, "pbx1", "pd1", T.pbx[:, P:2 * P], T.pd1[:, 0:P])
-    mm(T.pd0[:, 0:P], T.ec[:, 3 * P:4 * P], T.es[:, 3 * P:4 * P], T.pwc[:], T.pws[:], "ec3 pwa pwo pso", "pd0")
+    V("ts", "t2c", "xtz th", T.t2[:, 657:852], zero[:, 0:195], fc[:, 77:78], 3.0, op_.is_ge, op_.mult)
     for j in range(2):
         S(Ident, "nrz%d" % j, "nr lh lh16", T.nrz[:, 16 * j:16 * j + 16], T.nr[:, 16 * j:16 * j + 16], bias=fc[:, 56 + j:57 + j], scale=[lo, hi][j])
-    S(Ident, "cd0", "lg2", fc[:, 58:59], fc[:, 26:27], bias=float(255 - A * r), scale=-1.0)
-    S(Ident, "cd1", "lg2", fc[:, 59:60], fc[:, 26:27], bias=float(254 - A * r), scale=-1.0)
+    S(Ident, "fcl", "sk", fc[:, 79:80], tf, bias=5.0, scale=5.0)
+    for j in range(2):
+        S(Ident, "mk%d" % j, "one lh", T.mk[:, 32 * j:32 * j + 32], T.one[:, 0:32], scale=[lo, hi][j])
+    S(Copy, "t2z", "xtz", T.t2[:, 0:1], zero[:, 0:1])
+    S(Ident, "thr", "c16", thr, T.c16[:, 0:8], bias=7.0, scale=-1.0)
+    S(Ident, "cd0", "lg2", fc[:, 58:59], g2, bias=float(255 - A * r), scale=-1.0)
+    S(Ident, "cd1", "lg2", fc[:, 59:60], g2, bias=float(254 - A * r), scale=-1.0)
+    S(Ident, "gb", "lg2", gb, g2, bias=16.0, scale=8.0)
     S(Sign, "r16b", "c16", T.r16b[:], T.c16[:, 0:P])
-    S(Copy, "zb", "pz", T.zb[:, 16:272], T.pz[:, 0:256])
-    S(Copy, "zbz", "xtz", T.zb[:, 0:16], T.tbx[:, 576:592])
-    S(Ident, "dfl", "sk", T.dfl[:], fc[:, 0:8], bias=float(P - 1), scale=-1.0)
-    S(Ident, "gb", "lg2", gb, fc[:, 26:27], bias=16.0, scale=8.0)
-    S(Sign, "r8", "c8", T.r8[:], T.c8[:])
     S(Ident, "ci0", "gb c16", T.ci[:, 0:16], T.c16[:, 0:16], bias=gb)
+    S(Ident, "dfl", "sk", T.dfl[:], fc[:, 0:8], bias=float(P - 1), scale=-1.0)
     S(Ident, "ci1", "ci0", T.ci[:, 16:32], T.ci[:, 0:16], bias=float(P))
-    for b in range(4):
-        S(Copy, "hp%d" % b, ph_[b], H[b][:, P:2 * P], T[ph_[b]][:, 0:P])
-    V("copy", "gs", "pb0 pb1 lgs", T.gs[:], T.pb[:].indirect(T.lgs[:, 2:4]))
-    V("tt", "eqt", "pbx0 pbx1 lgs gs", eqt, T.pbx[:].indirect(T.lgs[:, 4:6]), T.gs[:], op_.is_equal)
-    V("tt", "gt", "pbx0 pbx1 lgs gs", gt, T.pbx[:].indirect(T.lgs[:, 4:6]), T.gs[:], op_.is_gt)
-    V("tt", "ge2", "pb0 pb1 lgs gs", T.ge2[:], T.pb[:].indirect(T.lgs[:, 0:2]), T.gs[:], op_.is_ge)
-    V("tt", "el", "eqt lw0 lw1", el, eqt, T.lw[:], op_.mult)
+    S(Copy, "pso", "xs ul", T.pws[:, A * r:A * r + A], T.xs[:].indirect(id0))
+    S(Copy, "mx0", "xtz", T.mx[0:32, 32:64], T.tbx[0:32, 576:608])
+    S(Copy, "zbz", "xtz", T.zb[:, 0:16], zero[:, 0:16])
+    S(Copy, "zb", "pz", T.zb[:, 16:272], T.pz[:, 0:256])
+    V("copy", "gs", "pb0 pb1 ul", T.gs[:], T.pb[:].indirect(lg[1]))
+    V("copy", "pwo", "xc ul", u32(T.pwc[:, A * r:A * r + A]), u32(T.xc[:]).indirect(id0))
+    V("tt", "eqt", "pbx0 pbx1 ul gs", eqt, T.pbx[:].indirect(lg[2]), T.gs[:], op_.is_equal)
+    V("tt", "gt", "pbx0 pbx1 ul gs", gt, T.pbx[:].indirect(lg[2]), T.gs[:], op_.is_gt)
+    V("tt", "ge2", "pb0 pb1 ul gs", T.ge2[:], T.pb[:].indirect(lg[0]), T.gs[:], op_.is_ge)
+    V("tt", "el", "eqt lw", el, eqt, T.lw[:], op_.mult)
+    V("tt", "ga", "ge2 wm", ga, T.ge2[:], T.wm[:, 0:32], op_.max)
     for j in range(2):
         a = 16 * j
-        V("scan", "sc%d" % j, "gt el", T.qa[:, 96 + a:112 + a], T.qa[:, 32 + a:48 + a], T.qa[:, 64 + a:80 + a], float(1 + 17 * j), op_.add, op_.add)
+        V("scan", "sc%d" % j, "gt el", T.qa[:, 96 + a:112 + a], T.qa[:, 32 + a:48 + a], T.qa[:, 64 + a:80 + a], float(a - 1), op_.add, op_.add)
+    V("tt", "gc", "gt el", gc_, gt, el, op_.add)
     V("copy", "rku", "sc0 sc1", T.rku[:], T.qa[:, 111:128:16])
-    V("copy", "bsw", "ge2 rku", T.bsw[:].indirect(T.rku[:]), T.ge2[:])
+    V("tt", "gd", "gc ga", gd, gc_, ga, op_.min)
     V("copy", "nsw", "nrz0 nrz1 rku", T.nsw[:].indirect(T.rku[:]), T.nrz[:])
-    V("scan", "pk", "bsw r17", T.pk[:], T.r17[:], T.bsw[:, 0:34], 0.0, op_.mult, op_.add)
-    V("tt", "ns", "nsw", T.pn[:, 32:40], T.nsw[:, 1:9], T.nsw[:, 18:26], op_.add)
-    V("copy", "pku", "pk", T.pku[:], T.pk[:, 8:26:17])
+    V("tt", "bsw", "gd rku pw0 pw1", T.bsw[:], T.pw[:, 0:32].indirect(T.rku[:]), gd, op_.mult)
+    V("tt", "ns", "nsw", T.pn[:, 32:40], T.nsw[:, 0:8], T.nsw[:, 16:24], op_.add)
+    V("scan", "pk", "bsw r16", T.pk[:], T.r16[:, 0:32], T.bsw[:], 0.0, op_.mult, op_.add)
     V("tt", "dn", "ns nsz", dn, T.pn[:, 32:40], T.pn[:, 33:41], op_.subtract)
-    V("copy", "own", "zt1 zt2 pku", T.own[:], T.zt[:].indirect(T.pku[:]))
-    V("copy", "msw", "own rku", T.msw[:].indirect(T.rku[:]), T.own[:])
-    V("tt", "ms", "msw", T.ms[:], T.msw[:, 1:9], T.msw[:, 18:26], op_.add)
-
-    def plane(m):
-        V("ts", "ui%d" % m, "ms", T.ui[:, 8 * m:8 * m + 8], T.ms[:], 7 - m, 1, op_.logical_shift_right, op_.bitwise_and)
-
-    def pair(m, j):
-        V("ts", "fv%d" % j, "ui%d fv%d fv%d" % (m, m, j), T.fv[:, j:j + 1], T.ui[:, 8 * m + j:8 * m + j + 1], T.fv[:, m:m + 1],
-          T.fv[:, j:j + 1], op_.subtract, op_.max)
-
-    def far(m, a):
-        V("ts", "tmp%d" % m, "ui%d fv%d" % (m, m), T.pn[:, 40 + 8 * m + a:48 + 8 * m], T.ui[:, 8 * m + a:8 * m + 8], T.fv[:, m:m + 1], None, op_.subtract)
-
-    def far2(m, a):
-        k = keys("fv", 8, a)
-        V("tt", k, "tmp%d " % m + k, T.fv[:, a:8], T.fv[:, a:8], T.pn[:, 40 + 8 * m + a:48 + 8 * m], op_.max)
-
-    V("ts", keys("fv", 8, 1), "ms", T.fv[:, 1:8], T.ms[:, 1:8], 128.0, None, op_.is_ge)
-    plane(1)
-    plane(2)
-    pair(1, 2)
-    far(1, 3)
-    plane(3)
-    far(2, 4)
-    far2(1, 3)
-    plane(4)
-    pair(2, 3)
-    far2(2, 4)
-    far(3, 5)
-    pair(3, 4)
-    far2(3, 5)
-    plane(5)
-    pair(4, 5)
-    pair(4, 6)
-    plane(6)
-    pair(4, 7)
-    pair(5, 6)
-    pair(5, 7)
-    pair(6, 7)
-    V("scan", "psn", keys("fv", 8) + " one", psn, T.one[:, 0:8], T.fv[:], 0.0, op_.add, op_.subtract)
-    V("ts", "geq", "psn kq", geq, psn, kq, None, op_.is_ge)
+    V("ts", "pku", "pk", T.pku[:], T.pk[:, 15:32:16], 256.0, None, op_.min)
+    V("copy", "own", "t1z t10 t11 t12 t13 t14 t15 t160 t161 " + keys("t17", 4) + " pku", T.own[:, 0:32], T.t1[:, 0:257].indirect(T.pku[:]))
+    V("scan", "sm", "own r16", T.own[:, 32:64], T.r16[:, 0:32], T.own[:, 0:32], 0.0, op_.mult, op_.add)
+    V("ts", "cl0", "sm", T.cl[:, 0:4:2], T.own[:, 47:64:16], -16384.0, None, op_.add)
+    V("ts", "cl1", "sm fcl", T.cl[:, 1:4:2], T.own[:, 47:64:16], 16384.0, fc[:, 79:80], op_.is_ge, op_.mult)
+    V("tt", "o2", "t2g t2f t2c t2z cl0 cl1 mk0 mk1", T.o2[:], T.t2[:].indirect(T.cl[:]), T.mk[:], op_.mult)
+    V("red", "mm", "o2", T.pn[:, 56:57], T.o2[:], AxisListType.X, op_.add)
+    V("ts", "geq", "mm thr", geq, thr, T.pn[:, 56:57], None, op_.is_lt)
     V("scan", "vv", "dn geq", vsc, dn, geq, 0.0, op_.add, op_.mult)
 
     V("ts", "off", "vv lh sk", T.off[:, 0:4:2], fc[:, 36:38], vv, tf, op_.mult, op_.max)
+    V("ts", "eqv", "nr vv", T.qb[:, 0:32], T.nr[:], 16.0, vv, op_.add, op_.is_equal)
     for j in (1, 0):
         V("ts", "val%d" % j, "off m16 sk cd%d" % j, T.val[:, 16 * j:16 * j + 16], T.m16[:].indirect(T.off[:, 2 * j:2 * j + 1]), tf,
           fc[:, 58 + j:59 + j], op_.is_equal, op_.mult)
+    V("tt", "eqc", "eqv ci0 ci1", T.qb[:, 32:64], T.qb[:, 0:32], T.ci[:], op_.mult)
     for j in (1, 0):
         V("copy", "mp", "off val%d" % j, T.mp[:].indirect(T.off[:, 2 * j:2 * j + 1]), T.val[:, 16 * j:16 * j + 16])
+        if j:
+            V("red", "cix", "eqc", T.qb[:, 64:65], T.qb[:, 32:64], AxisListType.X, op_.max)
+    V("ts", "cu", "cix one", T.cu[:], T.one[:, 0:2], T.qb[:, 64:65], None, op_.mult)
+    dma("s", "dl1", T.dl[:], T.cu[:], "cu", "dl")
     order = cross + same + [r]
 
     def maps(h):
@@ -497,25 +510,27 @@ def rank_program(g, core, T, topo):
     maps(1)
     send([(T.mo[:, 32 + 8 * y:40 + 8 * y], [T.ml[:, 32 + 8 * at_s[y]:40 + 8 * at_s[y]]], [ids_s[y]], e_s[y], "a_ms") for y in range(3)], "mo1")
 
-    V("ts", "eqv", "nr vv", T.qb[:, 0:32], T.nr[:], 16.0, vv, op_.add, op_.is_equal)
-    S(Ident, "t0a", "t0z mk4 vv", T.t0[:, 0:4], fc[:, 52:56], scale=vv)
+    lands("pwa", "a_pt", 7 * 2 * noff)
+    pv, ph_ = ["pd0", "pd1", "ph0", "ph1"], ["ph2", "pg0", "pg1", "pz"]
+    for b in range(4):
+        V("qz", "ec%d" % b, "ez", T.ec[:, P * b:P * b + P], T.es[:, P * b:P * b + P], T.ez[:, 3 - b:515 - b])
+        mm(T[pv[b]][:, 0:P], T.ec[:, P * b:P * b + P], T.es[:, P * b:P * b + P], T.tw[:, o:o + P], T.tws[:, o:o + P], "ec%d two" % b, pv[b])
+        mm(T[ph_[b]][:, 0:P], T.ec[:, P * b:P * b + P], T.es[:, P * b:P * b + P], T.pwc[:], T.pws[:], "ec%d pwa pwo pso" % b, ph_[b])
     V("tt", "mlo", "mo1 dfl", T.ml[:, 56:64], T.mo[:, 56:64], T.dfl[:], op_.max)
-    V("tt", "eqc", "eqv ci0 ci1", T.qb[:, 32:64], T.qb[:, 0:32], T.ci[:], op_.mult)
-    V("red", "cix", "eqc", T.qb[:, 64:65], T.qb[:, 32:64], AxisListType.X, op_.max)
-    V("ts", "t0b", "t0z mk4 cix", T.t0[:, 4:8], fc[:, 52:56], T.qb[:, 64:65], None, op_.mult)
     for b in range(4):
-        V("tr", "t1%d" % b, "t0a t0b", T.t1[0:32, 32 * b:32 * b + 32], T.t0[blk[b], :])
-    V("scan", "t2", keys("t1", 4) + " r8", T.t2[0:32, :], T.r8[0:32, :], T.t1[0:32, :], 0.0, op_.mult, op_.add)
-    for d in range(2):
-        V("copy", "t3%d" % d, "t2", T.t3[0:32, 16 * d:16 * d + 16], T.t2[0:32, 7:128:8])
-    S(Relu, "kp1", "t2", T.kpf[0:4, 0:16], T.t2[0:4, 7:128:8], bias=-15.0)
-    S(Ident, "kp2", "kp1", T.kpf[0:4, 16:32], T.kpf[0:4, 0:16], bias=-1.0)
-    dma("s", "dkp", T.kp[:], T.kpf[0:4, 16:32], "kp2", "kp")
-    V("tr", "t4", "t30 t31", T.t4[0:32, :], T.t3[0:32, :])
-    for b in range(4):
-        V("copy", "yl%d" % b, "t4", T.yl[blk[b], 0:8:2], T.t4[0:32, 4:8])
+        V("tt", "ho%d" % b, "tbt " + pv[b], H[b][:, 256:384], T.tbx[:, b:512:4], T[pv[b]][:, 0:P], op_.subtract)
+    S(Relu, "kp1", "vv", T.kpf[:, 0:1], vv, bias=-15.0)
+    S(Ident, "kp2", "kp1", T.kpf[:, 1:2], T.kpf[:, 0:1], bias=-1.0)
     for k in range(4):
-        S(Copy, "yb%d" % k, "zb zbz " + keys("yl", 4), T.yb[:, k:64:4], T.zb[:].indirect(T.yl[:, 2 * k:2 * k + 1]))
+        dma("s", "dkp", T.kp[k:k + 1, :], T.kpf[k:128:8, 1:2], "kp2", "kp")
+    for b in range(4):
+        S(Copy, "hp%d" % b, ph_[b], H[b][:, P:2 * P], T[ph_[b]][:, 0:P])
+    for b in range(2):
+        S(Copy, "hv%d" % b, "ho%d " % b + pv[b], H[b][:, 0:P], T[pv[b]][:, 0:P])
+    for k in range(8):
+        dma("s", "dl2", T.yl[16 * k:16 * k + 16, :], T.dl[:], "dl", "yl")
+    for k in range(4):
+        S(Copy, "yb%d" % k, "zb zbz yl", T.yb[:, k:64:4], T.zb[:].indirect(T.yl[:, 2 * k:2 * k + 1]))
     dma("s", "dy", T.y[:], T.yb[:], keys("yb", 4), "y")
 
     lands("mls", "a_ms", sum(len(e_s[f]) for f in at_s))
@@ -533,8 +548,11 @@ def rank_program(g, core, T, topo):
     V("tr", "x8", "x70 x71", T.mt[0:32, 96:128], T.mt[0:32, 64:96])
     for b in range(4):
         V("ts", "wu%d" % b, "x8", T.wu[blk[b], :], T.mt[0:32, 96:104], -1.0, 255.0, op_.mult, op_.add)
-    for b in range(4):
+    for b in range(2):
+        S(Copy, "gh%d" % b, "hp%d ho%d " % (b + 2, b + 2) + keys("wu", 4), T.gh[:, P * b:P * b + P], H[b + 2][:, P:3 * P].indirect(T.wu[:]))
         V("tt", "nt%d" % b, "hv%d hp%d ho%d " % (b, b, b) + keys("wu", 4), T.nt[:, b:512:4], H[b][:, P:3 * P].indirect(T.wu[:]), H[b][:, 0:P], op_.add)
+    for b in range(2):
+        V("tt", "nt%d" % (b + 2), "gh%d ph%d" % (b, b), T.nt[:, b + 2:512:4], T.gh[:, P * b:P * b + P], T["ph%d" % b][:, 0:P], op_.add)
     V("qz", "fo", keys("nt", 4), T.foc[:], T.fos[:], T.nt[:])
     dma("s", "doc", T.oc[:], u8(T.foc[:]), "fo", "oc")
     for k in range(4):

from concourse.bass import DstId, RemoteDMATransfer
from concourse.mybir import dt, AluOpType, ActivationFunctionType, AxisListType

N, P, A, LC = 8, 128, 16, 48
F32, BF, I32, U16, U8, X4 = "float32", "bfloat16", "int32", "uint16", "uint8", "float8_e4m3fn_x4"
RUN = 2 * LC
WCOLS = 2 * P + 4 * RUN
SCRATCH = {}


def _sb(name, n, d):
    SCRATCH[name] = ("sbuf", [128, n], d)


for _n, _w, _d in [
    ("cdi", 16, I32), ("cpi", 2, I32), ("tbx", 1024, BF), ("wt", 512, BF),
    ("cdu", 32, U16), ("fla", 1792, BF), ("flb", 1792, BF), ("mrg", 256, BF), ("nam", 256, BF), ("one", 128, BF),
    ("inc", 256, BF), ("le", 384, BF), ("cs", 384, BF), ("rs", 384, BF), ("sgo", 384, BF), ("sga", 4, F32),
    ("rq", 6, U16), ("rql", 18, U16),
    ("tw", 2 * P, X4), ("tws", 2 * P, U8), ("wc", WCOLS, X4), ("ws", WCOLS, U8),
    ("xc", 128, X4), ("xs", 128, U8), ("wqc", 128, X4), ("wqs", 128, U8), ("pwc", 128, X4), ("pws", 128, U8),
    ("xrc", 3 * RUN, X4), ("xrs", 4 * RUN, U8), ("dc", 3 * RUN, X4), ("ds", 3 * RUN, U8), ("rlc", LC, X4), ("rls", P, U8),
    ("rdc", RUN, X4), ("rds", 4 * RUN, U8), ("rpc", 16, X4), ("rps", 64, U8), ("kc", 288, X4), ("ks", 288, U8),
    ("foc", 128, X4), ("fos", 128, U8), ("ez", 516, BF), ("ec", 512, X4), ("es", 512, U8),
    ("ii", 16, I32), ("fc", 80, F32), ("idx", 1024, F32), ("c16", 256, F32), ("wm", 256, F32),
    ("r16", 256, F32), ("r16b", 128, BF), ("m16", 1040, BF), ("nrz", 32, F32), ("lf", 32, F32), ("ul", 32, U16),
    ("ci", 32, F32), ("dfl", 8, BF), ("pw", 64, F32),
    ("t1", 258, F32), ("t2", 852, BF), ("hh", 64, F32), ("ar", 272, BF), ("cr", 272, BF), ("sg", 656, BF), ("r3", 576, BF),
    ("r5", 80, BF), ("mk", 64, F32),
    ("loc", 264, F32), ("cdk", 16, U16), ("posm", 256, F32), ("posc", 256, F32), ("psa", 32, F32), ("kpl", 16, U16),
    ("cpu", 2, U16), ("nr", 32, F32), ("lw", 32, F32),
    ("pb", 288, F32), ("pbx", 256, F32), ("gs", 32, F32), ("qa", 224, F32), ("rku", 2, U16), ("ge2", 32, F32),
    ("bsw", 32, F32), ("pk", 32, F32), ("pku", 2, U16), ("own", 64, F32), ("cl", 4, U16), ("o2", 64, F32), ("nsw", 32, F32),
    ("pn", 64, F32),
    ("off", 4, U16), ("val", 32, BF), ("mp", 1040, BF), ("msc", 1024, BF), ("mo", 64, BF), ("rm", 8, BF), ("ml", 64, BF),
    ("mx", 64, BF), ("mt", 128, BF), ("wu", 8, U16),
    ("qb", 72, F32), ("cu", 2, U16), ("kpf", 2, F32), ("yl", 16, U16), ("zb", 272, F32), ("yb", 64, F32),
    ("h0", 384, F32), ("h1", 384, F32), ("h2", 384, F32), ("h3", 384, F32), ("gh", 256, F32), ("nt", 512, BF),
]:
    _sb(_n, _w, _d)
for _n in ("pg0", "pg1", "pd0", "pd1", "pz", "ph0", "ph1", "ph2"):
    SCRATCH[_n] = ("psum", [128, 512], F32)
SCRATCH["dl"] = ("dram", [16, 16], U16)
SEMAPHORES = ["cv", "ca", "ct", "cg", "dcd", "dcp", "dtb", "dx", "dw", "dy", "dkp", "doc", "dl1", "dl2", "ls",
              "a_tb", "a_rq", "a_dt", "a_pt", "a_mc", "a_ms", "r_pt", "r_tb", "r_dt", "r_mp"]


def _bits(es):
    m = 0
    for e in es:
        m |= 1 << e
    return m


def _peers(topo, cores, r):
    cross = [q for q in range(N) if q != r and not topo.may_write(cores[r], cores[q])]
    same = [q % N for q in range(r + 1, r + N) if topo.may_write(cores[r], cores[q % N])]
    assert sorted(q // 2 for q in same + [r]) == list(range(N // 2))
    return cross, same


def _relays(topo, cores, r):
    cross, _ = _peers(topo, cores, r)
    ok = [c for c in topo.cores_of(cores[r]) if c != cores[r] and topo.may_write(c, cores[cross[0]])]
    d0 = [c for c in ok if topo.die(c) == topo.die(cores[r])]
    d1 = [c for c in ok if topo.die(c) != topo.die(cores[r])]
    return [d0[0], d1[0], d0[1], d1[1]]


def _dst(topo, d, s):
    rid, pid = topo.addr(d, s)
    return DstId(rid=rid, pnc=pid)


def _relay_program(g, core, T, topo, cores, r, x):
    cross, same = _peers(topo, cores, r)
    to = cross + same
    es = topo.engines(core, cores[cross[x]])
    n = [0]

    def fwd(src, dst, qs, sem):
        g.remote_dma_fused([RemoteDMATransfer(dst_ids=[_dst(topo, cores[q], core) for q in qs], dma_engine_mask=_bits(es),
                                              remote_sem=T.sem[sem], srcs=[src], dsts=[dst] * len(qs))], local_sem=T.sem.ls)
        n[0] += len(es)

    non = len(topo.engines(cores[r], core))
    a, o, w0 = A * r, P * (r % 2), 2 * P + RUN * (r // 2)
    pts = [(T.rpc[:].bitcast(dt.uint8), T.pwc[:, a:a + A].bitcast(dt.uint8)), (T.rps[:, 0:A], T.pws[:, a:a + A])]
    run = [(T.rds[:, 3 * RUN:4 * RUN], T.ws[:, w0:w0 + RUN]), (T.rdc[:].bitcast(dt.uint8), T.wc[:, w0:w0 + RUN].bitcast(dt.uint8))]
    if x < 2:
        g.wait_ge(T.sem.r_pt, non // 2)
        fwd(pts[x][0], pts[x][1], to[0:1], "a_pt")
    g.wait_ge(T.sem.r_tb, non // 2)
    if x < 3:
        w = min(LC, P - LC * x)
        fwd(T.rlc[:, 0:w].bitcast(dt.uint8), T.tw[:, o + LC * x:o + LC * x + w].bitcast(dt.uint8), [r ^ 1], "a_tb")
    else:
        fwd(T.rls[:, 0:P], T.tws[:, o:o + P], [r ^ 1], "a_tb")
    if x < 2:
        fwd(pts[x][0], pts[x][1], to[1:], "a_pt")
    else:
        g.wait_ge(T.sem.r_dt, non // 2)
        fwd(run[x - 2][0], run[x - 2][1], same[0:1], "a_dt")
    at = _peers(topo, cores, cross[x])[0].index(r)
    g.wait_ge(T.sem.r_mp, non // 4)
    fwd(T.rm[:], T.ml[:, 8 * at:8 * at + 8], [cross[x]], "a_mc")
    g.wait_ge(T.sem.ls, n[0])


def rank_program(g, core, T, topo):
    cores = T.cores
    r = T.rank_of(core)
    if r is None:
        for k in range(N):
            if cores[k] in topo.cores_of(core):
                rel = _relays(topo, cores, k)
                if core in rel:
                    _relay_program(g, core, T, topo, cores, k, rel.index(core))
        return

    op_ = AluOpType
    AF = ActivationFunctionType
    Copy, Sign, Ident, Abs, Relu = AF.Copy, AF.Sign, AF.Identity, AF.Abs, AF.Relu
    rel = _relays(topo, cores, r)
    cross, same = _peers(topo, cores, r)
    B = r // 2
    blk = [slice(32 * b, 32 * b + 32) for b in range(4)]

    eng = {"v": g.vector, "a": g.scalar, "t": g.tensor, "g": g, "s": g.sync}
    csem = {"v": "cv", "a": "ca", "t": "ct", "g": "cg"}
    tot, seen, wr_, rd_ = {}, {e: {} for e in eng}, {}, {}

    def need(e, toks):
        want = {}
        for s, c in toks:
            c = tot[s] if c is None else c
            want[s] = max(want.get(s, 0), c)
        for s in want:
            if seen[e].get(s, 0) < want[s]:
                eng[e].wait_ge(T.sem[s], want[s])
                seen[e][s] = want[s]

    def do(e, fn, rd, wr):
        mine = csem[e]
        toks = []
        for k in rd:
            toks += wr_[k]
        for k in wr:
            toks += wr_.get(k, []) + rd_.get(k, [])
        need(e, toks)
        fn(eng[e]).then_inc(T.sem[mine], 1)
        tot[mine] = tot.get(mine, 0) + 1
        tok = (mine, tot[mine])
        for k in wr:
            wr_[k] = [tok]
            rd_[k] = []
        for k in rd:
            rd_[k] = [t for t in rd_.get(k, []) if t[0] != mine] + [tok]

    def V(name, wr, rd, *args):
        def fn(q):
            f = {"copy": q.tensor_copy, "tt": q.tensor_tensor, "ts": q.tensor_scalar, "set": q.memset, "tr": q.transpose,
                 "scan": q.tensor_tensor_scan, "qz": q.quantize_mx, "red": q.tensor_reduce}[name]
            return f(*args)
        do("v", fn, rd.split(), wr.split())

    def VX(wr, rd, *args):
        V("tt", wr, rd, *args)
        need("v", wr_[wr])

    def S(f, wr, rd, out, in_, **k):
        do("a", lambda q: q.activation(out, in_, f, **k), rd.split(), wr.split())

    def iota(out, wr, pattern, base=0, cm=0):
        do("g", lambda q: q.iota(out, pattern, base, cm, allow_small_or_imprecise_dtypes=True), [], [wr])

    def dma(e, sem, out, in_, rd, wr):
        toks = []
        for k in rd.split():
            toks += wr_[k]
        for k in wr.split():
            toks += [t for t in wr_.get(k, []) + rd_.get(k, []) if t[0] != sem]
        need(e, toks)
        eng[e].dma_start(out, in_).then_inc(T.sem[sem], 16)
        tot[sem] = tot.get(sem, 0) + 16
        for k in wr.split():
            wr_[k] = [(sem, None)]
        for k in rd.split():
            rd_[k] = rd_.get(k, []) + [(sem, None)]

    def mm(out, l, ls, m, ms, rd, wr):
        do("t", lambda q: q.matmul_mx(out, l, ls, m, ms, True, True), rd.split(), wr.split())

    def u8(v):
        return v.bitcast(dt.uint8)

    def u32(v):
        return v.bitcast(dt.uint32)

    def send(transfers, rd):
        for k in rd.split():
            need("g", wr_[k])
        ts = []
        for src, dsts, ids, es, sem in transfers:
            ts.append(RemoteDMATransfer(dst_ids=ids, dma_engine_mask=_bits(es), remote_sem=T.sem[sem], srcs=[src], dsts=dsts))
            tot["ls"] = tot.get("ls", 0) + len(es)
        g.remote_dma_fused(ts, local_sem=T.sem.ls)

    def lands(key, sem, n):
        tot[sem] = n
        wr_[key] = [(sem, n)]

    def keys(k, n, a=0):
        return " ".join(k + str(i) for i in range(a, n))

    ids_r = [_dst(topo, c, core) for c in rel]
    ids_s = [_dst(topo, cores[q], core) for q in same]
    eon = topo.engines(core, rel[0])
    eoff = topo.engines(core, cores[same[0]])
    noff = len(eoff)
    e_h = [eon[0:len(eon) // 2], eon[len(eon) // 2:]]
    e_q = [eon[len(eon) // 4 * k:len(eon) // 4 * (k + 1)] for k in range(4)]
    e_s = [eoff[0:noff // 2], eoff[noff // 2:3 * noff // 4], eoff[3 * noff // 4:]]
    e_d = [None, eoff[0:noff // 2], eoff[noff // 2:]]
    at_s = [_peers(topo, cores, q)[1].index(r) for q in same]
    o, op = P * (r % 2), P * (1 - r % 2)

    pin, ti = T.ii[:, 0:2], T.ii[:, 2:4]
    fc = T.fc
    tf = fc[:, 0:1]
    sk = [fc[:, k:k + 1] for k in range(8)]
    pf2, n8, n8b = fc[:, 30:31], fc[:, 32:33], fc[:, 33:34]
    lo, hi = fc[:, 36:37], fc[:, 37:38]
    k7, kq, gb = fc[:, 48:49], fc[:, 50:51], fc[:, 51:52]
    g2 = T.lf[:, 20:21]
    xl, lg, idl, id0 = T.ul[:, 0:18], [T.ul[:, 18 + 2 * k:20 + 2 * k] for k in range(3)], T.ul[:, 24:32], T.ul[:, 16:17]
    zero, hg = T.tbx[:, 576:1024], T.hh[:, 32:64]
    eqt, gt, el, _, ga, gc_, gd = [T.qa[:, 32 * k:32 * k + 32] for k in range(7)]
    geq, vsc, dn, thr = T.pn[:, 8:16], T.pn[:, 16:24], T.pn[:, 24:32], T.pn[:, 48:56]
    vv = T.pn[:, 23:24]
    H = [T["h%d" % b] for b in range(4)]

    dma("s", "dcd", T.cdi[0:16, :], T.cd[:], "", "cdi")
    dma("a", "dx", T.tbx[:, 512:576], T.x[:], "", "xt")
    dma("s", "dcd", T.cdi[16:32, :], T.cd[:], "", "cdi")
    dma("s", "dtb", T.tbx[:, 0:512], T.tb[:], "", "tbt")
    dma("s", "dw", T.wt[:], T.w[:], "", "wt")
    for k in range(8):
        dma("s", "dcp", T.cpi[16 * k:16 * k + 16, :], T.cd[:, 2 * k:2 * k + 2], "", "cpi")

    do("g", lambda q: q.iota(pin, [[0, 2]], 0, 1), [], ["pin"])
    iota(fc[:, 8:16], "k16", [[16, 8]])
    iota(T.c16[:], "c16", [[0, 16], [1, 16]])
    iota(pf2, "pf2", [[0, 1]], 0, 1)

    V("set", "xtz", "", zero, 0.0)
    V("set", "one", "", T.one[:], 1.0)
    V("ts", "ti", "pin", ti, pin, 15, None, op_.bitwise_and)
    V("set", "fla", "", T.fla[:, 768:1024], -200.0)
    V("copy", "tf", "ti", fc[:, 34:36], ti)
    V("set", "flb", "", T.flb[:, 768:1024], 0.0)
    V("ts", "sk", "k16 tf", fc[:, 0:8], fc[:, 8:16], fc[:, 34:35], None, op_.add)
    V("ts", "tb4", "pin", T.ii[:, 12:13], T.ii[:, 0:1], 5, None, op_.logical_shift_right)
    for m in range(4):
        V("ts", "tb%d" % m, "pin", T.ii[:, 8 + m:9 + m], T.ii[:, 0:1], m, 1, op_.logical_shift_right, op_.bitwise_and)
    for k in range(3):
        S(Copy, "rs%d" % k, "one", T.rs[:, P * k:P * k + P], T.one[:])
    S(Copy, "rs", "rs0 rs1 rs2 xtz", T.rs[:, 0:384:128], zero[:, 0:3])
    S(Ident, "half", "sk", fc[:, 44:47], fc[:, 0:3], bias=0.5)
    S(Copy, "n8", "sk", n8, tf, scale=-0.125)
    S(Copy, "lhc", "sk", fc[:, 39:40], tf, scale=-1.0)
    S(Abs, "wm", "c16 sk", T.wm[:], T.c16[:], bias=tf, scale=-1.0)
    S(Ident, "n8b", "n8", n8b, n8, bias=273.0)
    S(Ident, "lo", "lhc", lo, fc[:, 39:40], bias=7.5)
    S(Ident, "lg2", "pf2 n8", g2, pf2, bias=n8, scale=0.125)
    S(Relu, "wm", "wm", T.wm[:], T.wm[:], bias=1.0, scale=-1.0)
    S(Ident, "hi", "sk", hi, tf, bias=-7.5)

    V("qz", "xc xs", "xt xtz", T.xc[:], T.xs[:], T.tbx[:, 512:1024])
    send([(u8(T.xc[:, 0:16]), [u8(T.rpc[:])], ids_r[0:1], e_h[0], "r_pt"),
          (T.xs[:, 0:64], [T.rps[:]], ids_r[1:2], e_h[1], "r_pt")], "xc")

    for b in range(4):
        V("ts", "cdu%d" % b, "cdi", T.cdu[blk[b], 0:32:2], T.cdi[0:32, :], float(768 - 256 * b), None, op_.add)
    V("copy", "tm", keys("tb", 5), fc[:, 64:69], T.ii[:, 8:13])
    for i in range(A):
        f = "flb" if i % 2 else "fla"
        V("copy", f, keys("cdu", 4) + " one", T[f][:].indirect(T.cdu[:, 2 * i:2 * i + 1]), T.one[:, 0:16])
        if i == 3:
            V("qz", "two", "tbt", T.tw[:, o:o + P], T.tws[:, o:o + P], T.tbx[:, 0:512])
    send([(u8(T.tw[:, o + 2 * LC:o + P]), [u8(T.rlc[:, 0:P - 2 * LC])], [ids_r[2]], e_h[0], "r_tb"),
          (T.tws[:, o:o + P], [T.rls[:]], [ids_r[3]], e_h[1], "r_tb")], "two")
    send([(u8(T.tw[:, o + LC * x:o + LC * x + LC]), [u8(T.rlc[:])], [ids_r[x]], e_h[x], "r_tb") for x in range(2)], "two")
    iota(T.idx[:, 0:256], "idx", [[1, 256]])
    iota(T.lf[:, 0:16], "xlf", [[1, 2], [2, 8]])
    iota(T.lf[:, 18:20], "lg0", [[128, 2]], 16, 1)
    iota(T.lf[:, 22:24], "lg4", [[128, 2]], 0, 1)

    def hh(m):
        S(Ident, "hh", "hh tm", T.hh[:, 2 ** m:2 ** (m + 1)], T.hh[:, 0:2 ** m], bias=fc[:, 63 + m:64 + m])

    def ar(x0, x1):
        runs = [(0, 0, 64, 2), (1, 0, 64, 8), (1, 1, 64, 8), (1, 3, 64, 8), (2, 0, 8, 1), (2, 9, 16, 2), (2, 18, 19, 1), (2, 20, 24, 1), (2, 29, 32, 2)]
        for x in range(x0, x1):
            i, a, e, st = runs[x]
            S(Copy, "ar%d" % (x + 1), "arz one", T.ar[:, 3 * a + i:3 * e:3 * st], T.one[:, 0:len(range(a, e, st))])

    S(Copy, "hh", "c16", T.hh[:, 0:2], T.c16[:, 0:2])
    S(Sign, "lh", "lo hi", fc[:, 36:38], fc[:, 36:38])
    hh(1)
    S(Relu, "lh", "lh", fc[:, 36:38], fc[:, 36:38])
    hh(2)
    S(Ident, "lg3", "pf2 n8b", T.lf[:, 21:22], pf2, bias=n8b, scale=0.125)
    hh(3)
    S(Ident, "k7", "lh sk", k7, hi, bias=tf, scale=-8.0)
    hh(4)
    for h in range(2):
        S(Ident, "lb%d" % h, "tm", fc[:, 42 + h:43 + h], fc[:, 68:69], bias=float(2 * P + LC * h - 1), scale=float(RUN))
    S(Sign, "hg", "hh", hg, T.hh[:, 0:32])
    S(Relu, "kq0", "k7", fc[:, 49:50], k7, bias=-3.0)
    S(Ident, "idl", "sk", T.lf[:, 24:32], fc[:, 0:8], bias=float(op))
    S(Copy, "id0", "sk", T.lf[:, 16:18], fc[:, 0:2])
    S(Copy, "locz", "xtz", T.loc[:, 0:258:257], zero[:, 0:2])
    S(Copy, "tn", "tm", fc[:, 70:74], fc[:, 64:68], scale=-4096.0)
    S(Copy, "arz", "xtz", T.ar[:, 0:192], zero[:, 0:192])
    S(Copy, "ar0", "one", T.ar[:, 192:272:5], T.one[:, 0:16])

    def cdk(k):
        V("ts", "cdk%d" % k, keys("cdu", 4), T.cdk[:, 8 * k:8 * k + 8], T.cdu[:, 2 * k:32:4], -767.0, 257.0, op_.add, op_.min)

    V("scan", "mrg", "fla flb", T.mrg[:], T.fla[:, 768:1024], T.flb[:, 768:1024], 0.0, op_.add, op_.max)
    cdk(0)
    V("ts", "nam", "mrg", T.nam[:], T.mrg[:], 0.5, None, op_.is_ge)
    cdk(1)
    V("scan", "inc", "nam rs", T.inc[:], T.rs[:, 0:256], T.nam[:], 0.0, op_.mult, op_.add)
    V("copy", "cpu", "cpi", T.cpu[:], T.cpi[:])
    for k in range(3):
        S(Sign, "sg%d" % k, "inc half", T.sgo[:, P * k:P * k + P - 1], T.inc[:, P:2 * P - 1],
          bias=fc[:, 44 + k:45 + k], scale=-1.0, accum_out=T.sga[:, k:k + 1])
    for k in range(3):
        V("ts", "le%d" % k, "inc sk", T.le[:, P * k:P * k + P], T.inc[:, 0:P], sk[k], None, op_.is_le)
    V("ts", "cpf", "cpi", fc[:, 20:22], T.cpi[:], 0.5, None, op_.add)
    V("scan", "cs", "rs le0 le1 le2", T.cs[:], T.rs[:], T.le[:], 0.0, op_.mult, op_.add)
    V("ts", "rq1", "sg0 sg1 sg2", T.rq[:, 3:6], T.sga[:, 0:3], 0.5, 0.5 * (P - 1) + P, op_.mult, op_.add)
    V("copy", "rq0", "cs", T.rq[:, 0:3], T.cs[:, P - 2:384:P])
    send([(T.rq[:], [T.rql[:, 6 * a:6 * a + 6] for a in at_s], ids_s, eoff, "a_rq")], "rq0 rq1")
    for m in range(4):
        iota(T.ar[:, 193 + m:272:5], "ab%d" % m, [[0, 8 >> m], [1, 2], [0, 1 << m]])
    iota(T.r5[:], "r5", [[0, 16], [16, 5]])
    iota(T.pw[:, 32:64], "w2", [[254, 2], [0, 16]], 2)

    for h in range(2):
        S(Ident, "loc%d" % h, "inc lb%d" % h, T.loc[:, 1 + P * h:1 + P * h + P], T.inc[:, P * h:P * h + P], bias=fc[:, 42 + h:43 + h])
    S(Copy, "loc", "loc0 loc1 idx", T.loc[blk[B], 1:257], T.idx[blk[B], 0:256])
    V("copy", "ul", "xlf lg0 lg2 lg3 lg4 idl id0", T.ul[:], T.lf[:])
    V("qz", "wqc wqs", "wt", T.wqc[:], T.wqs[:], T.wt[:])
    V("copy", "xrc", "xc ul", u32(T.xrc[:]), u32(T.xc[:]).indirect(xl))
    V("tt", "posm", "loc locz cdk0 cdk1 wm", T.posm[:], T.loc[:, 0:258].indirect(T.cdk[:]), T.wm[:], op_.mult)
    V("set", "ez", "", T.ez[:], 0.5)
    S(Copy, "xrs", "xs ul", T.xrs[:, 0:3 * RUN], T.xs[:].indirect(xl))
    S(Sign, "r16", "c16", T.r16[:], T.c16[:])
    S(Ident, "kq", "kq0 k7", kq, fc[:, 49:50], bias=k7, scale=100.0)
    ar(0, 5)
    S(Ident, "th", "kq c16", fc[:, 74:78], T.c16[:, 0:4], bias=kq, scale=-1.0)

    lands("twp", "a_tb", 4 * noff)
    lands("rqa", "a_rq", 3 * noff)
    for b in range(4):
        if b != B:
            V("copy", "rql%d" % b, "rqa", T.rql[blk[b], :], T.rql[blk[B], :])
    wr_["rql%d" % B] = wr_["rqa"]
    rd = "two twp " + keys("rql", 4)
    S(Copy, "ds0", rd, T.xrs[:, 3 * RUN:4 * RUN], T.tws[:].indirect(T.rql[:, 0:6]))
    V("copy", "dc0", rd, u32(T.dc[:, 0:RUN]), u32(T.tw[:]).indirect(T.rql[:, 0:6]))
    S(Copy, "ds", rd, T.ds[:, RUN:3 * RUN], T.tws[:].indirect(T.rql[:, 6:18]))
    V("copy", "dc", rd, u32(T.dc[:, RUN:3 * RUN]), u32(T.tw[:]).indirect(T.rql[:, 6:18]))
    w0 = 2 * P + RUN * B
    send([(u8(T.dc[:, 0:RUN]), [u8(T.rdc[:])], [ids_r[3]], e_h[1], "r_dt"), (T.xrs[:], [T.rds[:]], [ids_r[2]], e_h[0], "r_dt")], "dc0 ds0 xrs")
    send([(u8(T.dc[:, RUN * y:RUN * y + RUN]), [u8(T.wc[:, w0:w0 + RUN])], [ids_s[y]], e_d[y], "a_dt") for y in (1, 2)], "dc")
    send([(T.ds[:, RUN * y:RUN * y + RUN], [T.ws[:, w0:w0 + RUN]], [ids_s[y]], e_d[y], "a_dt") for y in (1, 2)], "ds")
    iota(T.idx[:, 256:1024], "idy", [[1, 768]], 256)
    iota(T.m16[:], "m16", [[0, 65], [1, 16]])
    iota(T.mp[:], "mp", [[0, 1040]])
    do("g", lambda q: q.affine_select(T.ez[:], T.ez[:], [[-1, 516]], op_.is_equal, 0.0, 3, 4), ["ez"], ["ez"])

    ar(5, 9)
    S(Copy, "wsp", "two twp ul", T.ws[:, op:op + P], T.tws[:].indirect(idl))
    S(Relu, "cls", "hh", fc[:, 78:79], T.hh[:, 30:31], bias=3.0, scale=-1.0)
    S(Copy, "t1z", "xtz", T.t1[:, 0:257:256], zero[:, 0:2])
    for m in range(1, 5):
        S(Abs, "t1%d" % m, "hg tn", T.t1[:, 2 ** m:2 ** (m + 1)], hg[:, 0:2 ** m], bias=fc[:, 69 + m:70 + m], scale=4096.0)
    S(Ident, "t10", "cls", T.t1[:, 1:2], fc[:, 78:79], bias=83.0 + 3 * 192, scale=-192.0)
    S(Copy, "t15", "hg", T.t1[:, 32:64], hg, scale=3.0)
    for h in range(2):
        S(Ident, "t16%d" % h, "hg", T.t1[:, 64 + 32 * h:96 + 32 * h], hg, bias=6.0 * h, scale=12.0)
    for h in range(4):
        S(Ident, "t17%d" % h, "hg", T.t1[:, P + 32 * h:P + 32 + 32 * h], hg, bias=24.0 * h, scale=96.0)
    V("scan", "posc", "posm r16", T.posc[:], T.r16[:], T.posm[:], 0.0, op_.mult, op_.add)
    V("set", "r3a", "", T.r3[:], 1.0)
    VX("psa", "posc", T.psa[0:64, 0:16], T.posc[0:64, 15:256:16], T.posc[64:128, 15:256:16], op_.add)
    VX("psb", "psa", T.psa[0:32, 16:32], T.psa[0:32, 0:16], T.psa[32:64, 0:16], op_.add)
    for b in range(4):
        V("copy", "kpl%d" % b, "psb", T.kpl[blk[b], :], T.psa[0:32, 16:32])
    V("set", "r3", "r3a", T.r3[:, 0:576:3], 0.0)
    V("qz", "wco", "tbt", T.wc[:, o:o + P], T.ws[:, o:o + P], T.tbx[:, 0:512])
    V("qz", "kcx", "xt xtz", T.kc[:, 0:P], T.ks[:, 0:P], T.tbx[:, 512:1024])
    V("qz", "kcy", "xt tbt", T.kc[:, 160:288], T.ks[:, 160:288], T.tbx[:, 64:576])
    V("scan", "cr0", "r3 " + keys("ar", 10, 1), T.cr[:, 0:192], T.r3[:, 0:192], T.ar[:, 0:192], 0.0, op_.mult, op_.add)
    V("scan", "cr1", "r5 ar0 " + keys("ab", 4), T.cr[:, 192:272], T.r5[:], T.ar[:, 192:272], 0.0, op_.min, op_.add)
    V("copy", "wcp", "two twp ul", u32(T.wc[:, op:op + P]), u32(T.tw[:]).indirect(idl))
    for n in range(1, 4):
        V("ts", "sg%dx" % n, "cr0 th", T.sg[:, 192 * n - 112:192 * n + 80], T.cr[:, 0:192], fc[:, 74 + n:75 + n], None, op_.is_gt)
    V("ts", "sg0x", "cr1 th", T.sg[:, 0:80], T.cr[:, 192:272], fc[:, 74:75], None, op_.is_gt)
    V("scan", "pw0", "w2", T.pw[:, 0:16], T.pw[:, 32:48], T.pw[:, 48:64], 0.5, op_.mult, op_.min)
    V("scan", "t2g", "r3 sg1x sg2x sg3x", T.t2[:, 81:657], T.r3[:], T.sg[:, 80:656], 0.0, op_.mult, op_.add)
    S(Copy, "nr", "idx idy cpu", T.nr[:], T.idx[:].indirect(T.cpu[:]))
    S(Copy, "lh16", "lh", fc[:, 56:58], fc[:, 36:38], scale=16.0)
    for j in range(2):
        S(Sign, "lw%d" % j, "nr cpf", T.lw[:, 16 * j:16 * j + 16], T.nr[:, 16 * j:16 * j + 16], bias=fc[:, 20 + j:21 + j], scale=-1.0)
    S(Copy, "pw1", "pw0", T.pw[:, 16:32], T.pw[:, 0:16])
    S(Relu, "lw", "lw0 lw1", T.lw[:], T.lw[:])

    lands("wca", "a_dt", sum(noff * (1 if f else 2) for f in at_s))
    for j in range(2):
        a = 16 + P * j
        rd = "wco wcp wsp wca kcx kcy " + keys("kpl", 4)
        S(Copy, "ks%d" % j, rd, T.ks[:, a:a + P], T.ws[:].indirect(T.kpl[:, 8 * j:8 * j + 8]))
        V("copy", "kc%d" % j, rd, u32(T.kc[:, a:a + P]), u32(T.wc[:]).indirect(T.kpl[:, 8 * j:8 * j + 8]))
    for j in range(2):
        a, c = 16 + P * j, 144 * j
        mm(T["pg%d" % j][:, 0:144], T.kc[:, a:a + P], T.ks[:, a:a + P], T.kc[:, c:c + 144], T.ks[:, c:c + 144], "kc%d ks%d" % (j, j), "pg%d" % j)
        mm(T["pd%d" % j][:, 0:P], T.xrc[:, P * j:P * j + P], T.xrs[:, P * j:P * j + P], T.kc[:, a:a + P], T.ks[:, a:a + P],
           "kc%d ks%d xrc xrs" % (j, j), "pd%d" % j)
    mm(T.pz[:, 0:256], T.wqc[:], T.wqs[:], T.kc[:, 16:272], T.ks[:, 16:272], "wqc wqs kc0 ks0 kc1 ks1", "pz")
    V("scan", "t2f", "r5 sg0x", T.t2[:, 1:81], T.r5[:], T.sg[:, 0:80], 0.0, op_.min, op_.add)
    V("copy", "pb0", "pg0", T.pb[:, 0:144], T.pg0[:, 0:144])
    S(Copy, "nsz", "xtz", T.pn[:, 40:41], zero[:, 0:1])
    S(Copy, "pb1", "pg1", T.pb[:, 144:288], T.pg1[:, 0:144])
    V("copy", "pbx0", "pd0", T.pbx[:, 0:P], T.pd0[:, 0:P])
    S(Copy, "pbx1", "pd1", T.pbx[:, P:2 * P], T.pd1[:, 0:P])
    V("ts", "t2c", "xtz th", T.t2[:, 657:852], zero[:, 0:195], fc[:, 77:78], 3.0, op_.is_ge, op_.mult)
    for j in range(2):
        S(Ident, "nrz%d" % j, "nr lh lh16", T.nrz[:, 16 * j:16 * j + 16], T.nr[:, 16 * j:16 * j + 16], bias=fc[:, 56 + j:57 + j], scale=[lo, hi][j])
    S(Ident, "fcl", "sk", fc[:, 79:80], tf, bias=5.0, scale=5.0)
    for j in range(2):
        S(Ident, "mk%d" % j, "one lh", T.mk[:, 32 * j:32 * j + 32], T.one[:, 0:32], scale=[lo, hi][j])
    S(Copy, "t2z", "xtz", T.t2[:, 0:1], zero[:, 0:1])
    S(Ident, "thr", "c16", thr, T.c16[:, 0:8], bias=7.0, scale=-1.0)
    S(Ident, "cd0", "lg2", fc[:, 58:59], g2, bias=float(255 - A * r), scale=-1.0)
    S(Ident, "cd1", "lg2", fc[:, 59:60], g2, bias=float(254 - A * r), scale=-1.0)
    S(Ident, "gb", "lg2", gb, g2, bias=16.0, scale=8.0)
    S(Sign, "r16b", "c16", T.r16b[:], T.c16[:, 0:P])
    S(Ident, "ci0", "gb c16", T.ci[:, 0:16], T.c16[:, 0:16], bias=gb)
    S(Ident, "dfl", "sk", T.dfl[:], fc[:, 0:8], bias=float(P - 1), scale=-1.0)
    S(Ident, "ci1", "ci0", T.ci[:, 16:32], T.ci[:, 0:16], bias=float(P))
    S(Copy, "pso", "xs ul", T.pws[:, A * r:A * r + A], T.xs[:].indirect(id0))
    S(Copy, "mx0", "xtz", T.mx[0:32, 32:64], T.tbx[0:32, 576:608])
    S(Copy, "zbz", "xtz", T.zb[:, 0:16], zero[:, 0:16])
    S(Copy, "zb", "pz", T.zb[:, 16:272], T.pz[:, 0:256])
    V("copy", "gs", "pb0 pb1 ul", T.gs[:], T.pb[:].indirect(lg[1]))
    V("copy", "pwo", "xc ul", u32(T.pwc[:, A * r:A * r + A]), u32(T.xc[:]).indirect(id0))
    V("tt", "eqt", "pbx0 pbx1 ul gs", eqt, T.pbx[:].indirect(lg[2]), T.gs[:], op_.is_equal)
    V("tt", "gt", "pbx0 pbx1 ul gs", gt, T.pbx[:].indirect(lg[2]), T.gs[:], op_.is_gt)
    V("tt", "ge2", "pb0 pb1 ul gs", T.ge2[:], T.pb[:].indirect(lg[0]), T.gs[:], op_.is_ge)
    V("tt", "el", "eqt lw", el, eqt, T.lw[:], op_.mult)
    V("tt", "ga", "ge2 wm", ga, T.ge2[:], T.wm[:, 0:32], op_.max)
    for j in range(2):
        a = 16 * j
        V("scan", "sc%d" % j, "gt el", T.qa[:, 96 + a:112 + a], T.qa[:, 32 + a:48 + a], T.qa[:, 64 + a:80 + a], float(a - 1), op_.add, op_.add)
    V("tt", "gc", "gt el", gc_, gt, el, op_.add)
    V("copy", "rku", "sc0 sc1", T.rku[:], T.qa[:, 111:128:16])
    V("tt", "gd", "gc ga", gd, gc_, ga, op_.min)
    V("copy", "nsw", "nrz0 nrz1 rku", T.nsw[:].indirect(T.rku[:]), T.nrz[:])
    V("tt", "bsw", "gd rku pw0 pw1", T.bsw[:], T.pw[:, 0:32].indirect(T.rku[:]), gd, op_.mult)
    V("tt", "ns", "nsw", T.pn[:, 32:40], T.nsw[:, 0:8], T.nsw[:, 16:24], op_.add)
    V("scan", "pk", "bsw r16", T.pk[:], T.r16[:, 0:32], T.bsw[:], 0.0, op_.mult, op_.add)
    V("tt", "dn", "ns nsz", dn, T.pn[:, 32:40], T.pn[:, 33:41], op_.subtract)
    V("ts", "pku", "pk", T.pku[:], T.pk[:, 15:32:16], 256.0, None, op_.min)
    V("copy", "own", "t1z t10 t11 t12 t13 t14 t15 t160 t161 " + keys("t17", 4) + " pku", T.own[:, 0:32], T.t1[:, 0:257].indirect(T.pku[:]))
    V("scan", "sm", "own r16", T.own[:, 32:64], T.r16[:, 0:32], T.own[:, 0:32], 0.0, op_.mult, op_.add)
    V("ts", "cl0", "sm", T.cl[:, 0:4:2], T.own[:, 47:64:16], -16384.0, None, op_.add)
    V("ts", "cl1", "sm fcl", T.cl[:, 1:4:2], T.own[:, 47:64:16], 16384.0, fc[:, 79:80], op_.is_ge, op_.mult)
    V("tt", "o2", "t2g t2f t2c t2z cl0 cl1 mk0 mk1", T.o2[:], T.t2[:].indirect(T.cl[:]), T.mk[:], op_.mult)
    V("red", "mm", "o2", T.pn[:, 56:57], T.o2[:], AxisListType.X, op_.add)
    V("ts", "geq", "mm thr", geq, thr, T.pn[:, 56:57], None, op_.is_lt)
    V("scan", "vv", "dn geq", vsc, dn, geq, 0.0, op_.add, op_.mult)

    V("ts", "off", "vv lh sk", T.off[:, 0:4:2], fc[:, 36:38], vv, tf, op_.mult, op_.max)
    V("ts", "eqv", "nr vv", T.qb[:, 0:32], T.nr[:], 16.0, vv, op_.add, op_.is_equal)
    for j in (1, 0):
        V("ts", "val%d" % j, "off m16 sk cd%d" % j, T.val[:, 16 * j:16 * j + 16], T.m16[:].indirect(T.off[:, 2 * j:2 * j + 1]), tf,
          fc[:, 58 + j:59 + j], op_.is_equal, op_.mult)
    V("tt", "eqc", "eqv ci0 ci1", T.qb[:, 32:64], T.qb[:, 0:32], T.ci[:], op_.mult)
    for j in (1, 0):
        V("copy", "mp", "off val%d" % j, T.mp[:].indirect(T.off[:, 2 * j:2 * j + 1]), T.val[:, 16 * j:16 * j + 16])
        if j:
            V("red", "cix", "eqc", T.qb[:, 64:65], T.qb[:, 32:64], AxisListType.X, op_.max)
    V("ts", "cu", "cix one", T.cu[:], T.one[:, 0:2], T.qb[:, 64:65], None, op_.mult)
    dma("s", "dl1", T.dl[:], T.cu[:], "cu", "dl")
    order = cross + same + [r]

    def maps(h):
        for x in range(4 * h, 4 * h + 4):
            a = 16 + P * order[x]
            V("scan", "msc%d" % x, "mp r16b", T.msc[:, P * x:P * x + P], T.r16b[:], T.mp[:, a:a + P], 0.0, op_.mult, op_.max)
        V("copy", "mo%d" % h, keys("msc", 4 * h + 4, 4 * h), T.mo[:, 32 * h:32 * h + 32], T.msc[:, 512 * h + 15:512 * h + 512:16])

    maps(0)
    send([(T.mo[:, 8 * x:8 * x + 8], [T.rm[:]], [ids_r[x]], e_q[x], "r_mp") for x in range(4)], "mo0")
    maps(1)
    send([(T.mo[:, 32 + 8 * y:40 + 8 * y], [T.ml[:, 32 + 8 * at_s[y]:40 + 8 * at_s[y]]], [ids_s[y]], e_s[y], "a_ms") for y in range(3)], "mo1")

    lands("pwa", "a_pt", 7 * 2 * noff)
    pv, ph_ = ["pd0", "pd1", "ph0", "ph1"], ["ph2", "pg0", "pg1", "pz"]
    for b in range(4):
        V("qz", "ec%d" % b, "ez", T.ec[:, P * b:P * b + P], T.es[:, P * b:P * b + P], T.ez[:, 3 - b:515 - b])
        mm(T[pv[b]][:, 0:P], T.ec[:, P * b:P * b + P], T.es[:, P * b:P * b + P], T.tw[:, o:o + P], T.tws[:, o:o + P], "ec%d two" % b, pv[b])
        mm(T[ph_[b]][:, 0:P], T.ec[:, P * b:P * b + P], T.es[:, P * b:P * b + P], T.pwc[:], T.pws[:], "ec%d pwa pwo pso" % b, ph_[b])
    V("tt", "mlo", "mo1 dfl", T.ml[:, 56:64], T.mo[:, 56:64], T.dfl[:], op_.max)
    for b in range(4):
        V("tt", "ho%d" % b, "tbt " + pv[b], H[b][:, 256:384], T.tbx[:, b:512:4], T[pv[b]][:, 0:P], op_.subtract)
    S(Relu, "kp1", "vv", T.kpf[:, 0:1], vv, bias=-15.0)
    S(Ident, "kp2", "kp1", T.kpf[:, 1:2], T.kpf[:, 0:1], bias=-1.0)
    for k in range(4):
        dma("s", "dkp", T.kp[k:k + 1, :], T.kpf[k:128:8, 1:2], "kp2", "kp")
    for b in range(4):
        S(Copy, "hp%d" % b, ph_[b], H[b][:, P:2 * P], T[ph_[b]][:, 0:P])
    for b in range(2):
        S(Copy, "hv%d" % b, "ho%d " % b + pv[b], H[b][:, 0:P], T[pv[b]][:, 0:P])
    for k in range(8):
        dma("s", "dl2", T.yl[16 * k:16 * k + 16, :], T.dl[:], "dl", "yl")
    for k in range(4):
        S(Copy, "yb%d" % k, "zb zbz yl", T.yb[:, k:64:4], T.zb[:].indirect(T.yl[:, 2 * k:2 * k + 1]))
    dma("s", "dy", T.y[:], T.yb[:], keys("yb", 4), "y")

    lands("mls", "a_ms", sum(len(e_s[f]) for f in at_s))
    lands("mlc", "a_mc", 4 * noff)
    V("tt", "e1", "mls mlo", T.mx[:, 0:16], T.ml[:, 32:48], T.ml[:, 48:64], op_.max)
    V("tt", "e2", "e1", T.mx[:, 16:24], T.mx[:, 0:8], T.mx[:, 8:16], op_.max)
    V("tt", "x1", "mlc", T.mt[:, 0:16], T.ml[:, 0:16], T.ml[:, 16:32], op_.max)
    V("tt", "x2", "x1", T.mt[:, 16:24], T.mt[:, 0:8], T.mt[:, 8:16], op_.max)
    V("tt", "x3", "x2 e2", T.mx[:, 24:32], T.mt[:, 16:24], T.mx[:, 16:24], op_.max)
    VX("x4", "x3", T.mt[0:64, 24:32], T.mx[0:64, 24:32], T.mx[64:128, 24:32], op_.max)
    VX("x5", "x4 mx0", T.mx[0:32, 32:40], T.mt[0:32, 24:32], T.mt[32:64, 24:32], op_.max)
    V("tr", "x6", "x5", T.mt[0:32, 32:64], T.mx[0:32, 32:64])
    for d in range(2):
        V("tt", "x7%d" % d, "x6", T.mt[0:32, 64 + 16 * d:80 + 16 * d], T.mt[0:32, 32:48], T.mt[0:32, 48:64], op_.max)
    V("tr", "x8", "x70 x71", T.mt[0:32, 96:128], T.mt[0:32, 64:96])
    for b in range(4):
        V("ts", "wu%d" % b, "x8", T.wu[blk[b], :], T.mt[0:32, 96:104], -1.0, 255.0, op_.mult, op_.add)
    for b in range(2):
        S(Copy, "gh%d" % b, "hp%d ho%d " % (b + 2, b + 2) + keys("wu", 4), T.gh[:, P * b:P * b + P], H[b + 2][:, P:3 * P].indirect(T.wu[:]))
        V("tt", "nt%d" % b, "hv%d hp%d ho%d " % (b, b, b) + keys("wu", 4), T.nt[:, b:512:4], H[b][:, P:3 * P].indirect(T.wu[:]), H[b][:, 0:P], op_.add)
    for b in range(2):
        V("tt", "nt%d" % (b + 2), "gh%d ph%d" % (b, b), T.nt[:, b + 2:512:4], T.gh[:, P * b:P * b + P], T["ph%d" % b][:, 0:P], op_.add)
    V("qz", "fo", keys("nt", 4), T.foc[:], T.fos[:], T.nt[:])
    dma("s", "doc", T.oc[:], u8(T.foc[:]), "fo", "oc")
    for k in range(4):
        dma("a" if k < 3 else "s", "doc", T.osc[4 * k:4 * k + 4, :], T.fos[32 * k:32 * k + 4, :], "fo", "osc")
    need("g", [(x, tot[x]) for x in tot])
